import numpy as np, ml_dtypes
CORES = [36,164,52,180,100,228,116,244]
N = 8
BF = ml_dtypes.bfloat16
W, A, S, RO, H = 4096, 256, 2, 4, 3
def parts(rng):
    z = rng.integers(0, 256, (N, 8, 16, W)); w = rng.integers(0, 256, (N, 8, 16, 3)); w[..., 2] = rng.integers(0, 2048, (N, 8, 16))
    return z, w, rng.choice(np.array([750, 850, 950, 1200]), (N, 8, 1, 1))
def loose(rng):
    share = rng.choice(np.array([0.06, 0.15, 0.4, 0.9]), (N, 8, 1, A))
    return np.where(rng.random((N, 8, 16, A)) < share, rng.integers(0, W, (N, 8, 16, A)), -1)
def objects(rng, z, n):
    ix = np.argsort(rng.random((N, 8, W)), axis=-1)[..., :S * 2 * n]
    base = rng.integers(40, 216, (8, 16, 1, 1, n)); dev = rng.integers(-16, 17, (8, 16, 16, 2, n))
    order = np.argsort(rng.random((8, 16, n)), axis=1); rows = np.arange(16)[None, :, None]
    up = rows == order[:, :1]; down = rows == order[:, 1:2]
    v = base + np.where(up[:, None, :, None, :], 16, np.where(down[:, None, :, None, :], -16, dev))
    for q in range(N):
        np.put_along_axis(z[q], np.broadcast_to(ix[q][:, None, :], (8, 16, S * 2 * n)), v[:, :, S * q:S * q + S].reshape(8, 16, S * 2 * n), 2)
    return np.ascontiguousarray(ix.reshape(N, 8, S, 2, n).transpose(1, 0, 2, 3, 4)).reshape(8, 16, 2, n), up | down
def follow(rng, obj, am):
    out = []
    for r in range(N):
        c = rng.integers(0, obj.shape[-1], (8, 1, A))
        one = np.take_along_axis(obj[:, :, 0], c, 2); two = np.take_along_axis(obj[:, :, 1], c, 2); anchor = np.take_along_axis(am, c, 2)
        v = (rng.random((8, 16, A)) < rng.choice(np.array([0, 0, 0.1, 0.5]), (8, 1, A))) & ~anchor
        keep = anchor | (rng.random((8, 16, A)) < rng.random((8, 1, A)))
        out.append(np.where(keep, np.where(v, two, one), -1))
    return np.stack(out)
def pack(z, w, t, p, s):
    return {"tz": np.ascontiguousarray(z.reshape(N, 128, W)).astype(np.float32).astype(BF), "tp": np.ascontiguousarray(p.reshape(N, 128, A)).astype(np.int32),
            "sd": np.ascontiguousarray(s.reshape(N, 128, A)).astype(np.int32), "hw": np.ascontiguousarray(w.reshape(N, 128, 3)).astype(np.int32),
            "th": np.repeat(t.reshape(N, 8, 1), 16, axis=1).astype(np.int32)}
def setup_inputs(rng):
    z, w, t = parts(rng); obj, am = objects(rng, z, A // 4)
    p = np.where(rng.random((N, 8, 1, A)) < 0.5, follow(rng, obj, am), loose(rng))
    s = np.where(rng.random((N, 8, 1, A)) < 0.5, follow(rng, obj, am), loose(rng))
    return pack(z, w, t, p, s)
def setup_inputs_twins(rng):
    z, w, t = parts(rng); obj, am = objects(rng, z, 4); t[:] = 4096
    p = follow(rng, obj, am); p[:, 6:] = loose(rng)[:, 6:]; p[..., A // 2:] = p[..., :A // 2].copy()
    return pack(z, w, t, p, follow(rng, obj, am))
def setup_inputs_ties(rng):
    z, w, t = parts(rng)
    z = np.take_along_axis(rng.integers(0, 256, (N, 8, 16, 6)), rng.integers(0, 6, (N, 8, 1, W)), 3)
    t = rng.choice(np.array([1000, 4096]), (N, 8, 1, 1)); p = loose(rng); s = loose(rng)
    w[:, 0, :, :2] = 0; w[:, 1, :, 2] = 0; w[:, 4, :, 2] = rng.choice(np.array([5, 1031]), (N, 16)); t[:, :2] = 4096
    z[:, 2:4] = 100; t[::2, 2] = 0; t[1::2, 2] = 1; t[:, 3] = 432; p[:, 2:4, :, ::4] = -1
    return pack(z, w, t, p, s)
def setup_inputs_ends(rng):
    z = 255 * rng.integers(0, 2, (N, 8, 16, W)); ends = np.array([-1, 0, 1, W - 2, W - 1])
    p = rng.choice(ends, (N, 8, 16, A)); s = rng.choice(ends, (N, 8, 16, A)); t = rng.choice(np.array([0, 1, 2040, 4080, 4096]), (N, 8, 1, 1))
    w = rng.choice(np.array([0, 1, 254, 255]), (N, 8, 16, 3)); w[..., 2] = rng.choice(np.array([0, 1, 1025, 2046, 2047]), (N, 8, 16))
    p[:, 4] = rng.integers(0, W, (N, 16, A)); t[:, 4] = 4096
    z[:, 5] = 255; w[:, 5, :, :2] = 0; w[:, 5, 0, :2] = 255; w[:, 5, 1, :2] = 2; w[:, 5, :, 2] = 2047; t[:, 5] = 4096
    p[:, 6] = -1; t[:, 6] = 4096
    z[::2, 7] = 255; z[1::2, 7] = 0; p[:, 7] = rng.integers(0, W, (N, 16, A)); p[:, 7, (np.arange(16) // S) % 2 == 1] = -1
    t[1::4, 7] = 4081; t[3::4, 7] = 4080
    w[1::2, 7, :, 0] = 0; w[1::2, 7, :, 1] = 254 * rng.integers(0, 2, (N // 2, 16)); w[1::2, 7, 0, 1] = 255; w[1::2, 7, 0, 2] = rng.integers(1, 2048, N // 2)
    return pack(z, w, t, p, s)
def setup_inputs_sparse(rng):
    z, w, t = parts(rng); t = rng.choice(np.array([900, 4096]), (N, 8, 1, 1)); t[:, 0] = 4096
    p = np.where(rng.random((N, 8, 16, A)) < 0.06, rng.integers(0, W, (N, 8, 16, A)), -1); p[rng.integers(0, N)] = -1
    s = loose(rng); s[:, rng.permutation(8)[:4]] = -1
    return pack(z, w, t, p, s)
def setup_inputs_spread(rng):
    z = np.minimum((np.exp2(8.0 * rng.random((N, 8, 1, W))) * rng.random((N, 8, 16, W))).astype(np.int64), 255)
    w = np.minimum(np.exp2(8.0 * rng.random((N, 8, 16, 3))).astype(np.int64), 255); w[..., 2] = np.minimum(np.exp2(11.0 * rng.random((N, 8, 16))).astype(np.int64), 2047)
    t = np.minimum(np.exp2(7.0 + 5.0 * rng.random((N, 8, 1, 1))).astype(np.int64), 4096)
    ps = []
    for i in range(2):
        nm = np.minimum((W * rng.random((N, 8, 16, A)) ** 3).astype(np.int64), W - 1)
        ps.append(np.where(rng.random((N, 8, 16, A)) < rng.random((N, 8, 1, A)), nm, -1))
    return pack(z, w, t, ps[0], ps[1])
def check_inputs(d):
    bad = []; v = np.asarray(d["tz"]).astype(np.float32)
    if not (np.min(v) >= 0 and np.max(v) <= 255 and np.all(v == np.floor(v))): bad.append("tz: whole numbers from 0 to 255")
    for k, lo, hi in (("tp", -1, W - 1), ("sd", -1, W - 1), ("th", 0, 4096)):
        if np.min(d[k]) < lo or np.max(d[k]) > hi: bad.append("range of " + k)
    w = np.asarray(d["hw"])
    if np.min(w) < 0 or np.max(w[..., :2]) > 255 or np.max(w[..., 2]) > 2047: bad.append("range of hw")
    t = np.asarray(d["th"]).reshape(-1, 16)
    if np.any(t != t[:, :1]): bad.append("th: one number a group")
    return bad
def reference(tz, tp, sd, hw, th):
    z = tz.astype(np.float32).astype(np.int32).reshape(N, 8, 16, W); w = hw.astype(np.int32).reshape(N, 8, 16, 3); lim = th.astype(np.int32).reshape(N, 8, 16)[:, :, :1]
    p = tp.astype(np.int32).reshape(N, 8, 16, A); s = sd.astype(np.int32).reshape(N, 8, 16, A); lower = np.arange(A)[None, :] < np.arange(A)[:, None]
    for t in range(RO):
        for r in range(N):
            q = (r + 1 + t) % N; x = S * q + t // N
            hi = np.zeros((8, 16, A), np.int32); lo = np.full((8, 16, A), 255, np.int32)
            for j in range(16):
                n = p[r, :, j]; on = (n >= 0)[:, None, :]; v = np.take_along_axis(z[j // S], np.maximum(n, 0)[:, None, :], 2)
                hi = np.where(on, np.maximum(hi, v), hi); lo = np.where(on, np.minimum(lo, v), lo)
            e = (hi + lo) >> 1; c = e
            best = np.full((8, A), 4097); name = np.zeros((8, A), np.int64)
            for k in range(H):
                u1 = np.add.reduce(w[q, :, :, 0:1] * c, axis=1) & (W - 1); u2 = np.add.reduce(w[q, :, :, 1:2] * c, axis=1) & (W - 1)
                h = (((u1 * u2) >> 5)[:, None, :] + w[q, :, :, 2:3] * u2[:, None, :]) & (W - 1)
                v = np.take_along_axis(z[q], h.reshape(8, 1, 16 * A), 2).reshape(8, 16, 16, A)
                d = np.add.reduce(np.abs(v - e[:, :, None, :]), axis=1)
                m = np.argmin(d, axis=1); dm = np.min(d, axis=1); n = np.take_along_axis(h, m[:, None, :], 1)[:, 0]
                less = dm < best; name = np.where(less, n, name); best = np.where(less, dm, best)
                c = (e + np.take_along_axis(z[q], n[:, None, :], 2)) >> 1
            n = np.where(best < lim[q], name, -1); p[r, :, x] = n
            low = (n[:, :, None] == n[:, None, :]) & (n >= 0)[:, :, None] & lower
            g, b = np.nonzero(np.count_nonzero(low, axis=2) == 1); a = np.argmax(low[g, b], axis=1)
            pa = p[r][g, :, a]; pb = p[r][g, :, b]; differ = (pa >= 0) & (pb >= 0) & (pa != pb); clash = np.any(differ, axis=1)[:, None]
            p[r][g, :, a] = np.where(clash, np.where(differ, -1, pa), np.where(pa >= 0, pa, pb))
            p[r][g, :, b] = np.where(clash, np.where(differ, -1, pb), s[r][g, :, b])
    return {"yp": p.reshape(N, 128, A).astype(np.float32)}

@@ -1,0 +1,573 @@
+from concourse.bass import DstId, RemoteDMATransfer
+from concourse.mybir import AluOpType as OP, AxisListType, ActivationFunctionType as AF
+
+BLK = 4112
+KV, KC = 80, 32
+EV = (1, 3)
+BIG = 16777216.0
+LAT = 0.1
+F32, BF, I32, U16, F16 = "float32", "bfloat16", "int32", "uint16", "float16"
+
+SCRATCH = {"TW": ("sbuf", [128, 8 * BLK], BF), "D": ("dram", [8, 128, 32], I32)}
+WIDTH, PLACE, _used = {"TW": 8 * BLK, "D": 1}, {}, {}
+for _n, _w, _d in (("NL", 256, I32), ("HT", 4, I32), ("HS", 16, I32), ("FO", 4096, BF), ("FI", 4096, BF), ("P", 512, F32), ("TP", 256, I32), ("SD", 256, I32), ("YO", 256, F32)):
+    SCRATCH[_n], WIDTH[_n] = ("sbuf", [128, _w], _d), _w
+for _k in range(8):
+    SCRATCH["B%d" % _k], WIDTH["B%d" % _k] = ("psum", [128, 512], F32), 512
+SPEC = ((BF, 1, "FA 2048 FB 2048 HI 2048 LO 2048 ER 2048 XV 2048 AX 2048 EB 128"), (F16, 1, "HB 16 HX 128 C 128"), (U16, 1, "OF 128 JU 16 L1U 8 L2U 8"),
+        (F32, 1, "SE 128 E2 128 SC 128 LT 128 VAL 8 M1 8 M2 8 GG 128 PR 128 PK 128"),
+        (I32, 1, "EI 128 UI 16 UA 16 VP 8 HN 128 KI 8 J 8 R 24 I1 128 I2 128 BA 8 BK 8 PI 8 L1 8 MI 8"),
+        (F32, 0, "Y1 16 Y2 16 SEC 16 DD 16 DS 16 LF 16 EE 16 LSF 16 SN 256 Q 256 MN 256 QN 256 SP 256 SPS 256 SX 256 PC 256 S 256 HF 16 cone 512 cid 128 "
+                 "cb1 128 cblk 128 cg1 8 cg 8 cmi 128 cmk 128 cm0 128 cj 1 cq 1 cs 1 cn 1 cpar 1 cnpar 1 ceb 1 clb 1 cba 16 cb2 16 cbf 16 cio 256 ci2 256 "
+                 "clc 256 cth 512 cw0f 16 coh 32 cohi 32 cbt 16 csc 1 cc 8 cnegf 128 ntx 4 XM 128 XS 512 th 4 hcol 4 WF 64 cbm0 128"),
+        (I32, 0, "HST 1024 cpi 1 cpj 1 cpq 1 cpt 1 cbai 16 cpc 24 cR 24 kd 16"),
+        (BF, 0, "BE 256 BO 256 QA 1024 QX 1024 QB 1024 ND 256 cib 128 cnb 128 cblb 128 cgk 8 cmh 512 cml 512 WB 64"),
+        (U16, 0, "NO 256 EO 256 LC 256 LU 16 LSU 16"), (F16, 0, "cw0 16 cw1 16 cneg 128 cih 128 cbm 128 WH 64 ZZ 64 KM 512"))
+ARENA = {F32: "af", BF: "ab", I32: "ai", U16: "au", F16: "ah"}
+for _d, _half, _s in SPEC:
+    _it = _s.split()
+    for _n, _w in zip(_it[::2], _it[1::2]):
+        for _t in (("_0", "_1") if _half else ("",)):
+            _a, _step = ARENA[_d], 16 if _d in (F32, I32) else 32
+            PLACE[_n + _t], WIDTH[_n + _t] = (_a, _used.get(_a, 0)), int(_w)
+            _used[_a] = _used.get(_a, 0) - (-int(_w) // _step) * _step
+for _d in ARENA:
+    SCRATCH[ARENA[_d]] = ("sbuf", [128, _used[ARENA[_d]]], _d)
+SEMAPHORES = ["qv", "qs", "qt", "qg", "stg", "dtz", "dhw", "dtp", "dsd", "dnl", "dyp", "nm", "hs", "ft", "tb0", "tbx", "rel", "loc"]
+
+
+def helper_of(rc, T, topo):
+    for c in topo.cores_of(rc):
+        if topo.die(c) != topo.die(rc) and c not in T.cores and all(topo.may_write(c, d) for d in T.cores if d != rc):
+            return c
+    return None
+
+
+def send(g, T, topo, core, dst, out, in_, rsem, engines=None):
+    rid, pid = topo.addr(dst, core)
+    eng = topo.engines(core, dst) if engines is None else engines
+    m = 0
+    for e in eng:
+        m |= 1 << e
+    g.remote_dma(out, in_, T.sem[rsem], T.sem.loc, pid, rid, m)
+    return len(eng)
+
+
+def relay_engines(rc, hc, topo, T):
+    off = topo.engines(rc, T.cores[0] if T.cores[0] != rc else T.cores[1])
+    e = [x for x in topo.engines(rc, hc) if x not in off]
+    return e if len(e) in (1, 2, 4, 8, 16) else topo.engines(rc, hc)
+
+
+def rank_program(g, core, T, topo):
+    N = len(T.cores)
+    r = T.rank_of(core)
+    if r is not None:
+        main(g, core, T, topo, r, N)
+        return
+    for s in range(N):
+        if helper_of(T.cores[s], T, topo) == core:
+            blk = T.TW[:, BLK * s + 16:BLK * (s + 1)]
+            g.wait_ge(T.sem.rel, len(relay_engines(T.cores[s], core, topo, T)))
+            tot = 0
+            for o in (1, 2, 4, 6):
+                tot += send(g, T, topo, core, T.cores[(s - o) % N], blk, blk, "tb0" if o == 1 else "tbx")
+            g.wait_ge(T.sem.loc, tot)
+
+
+def is_bank(n):
+    return n[0] == "B" and n[1:].isdigit()
+
+
+def overlap(x, y):
+    if x[1] >= y[2] or y[1] >= x[2] or x[3] >= y[4] or y[3] >= x[4]:
+        return False
+    return not (x[5] == y[5] and x[5] > 1 and (x[3] - y[3]) % x[5])
+
+
+def covers(x, y):
+    return x[5] == 1 and x[1] <= y[1] and x[2] >= y[2] and x[3] <= y[3] and x[4] >= y[4]
+
+
+def schedule(ops):
+    n = len(ops)
+    preds, succs, acc, lastg = [set() for _ in ops], [[] for _ in ops], {}, None
+    for i, (q, rd, wr, _, _, _) in enumerate(ops):
+        if q == "g":
+            if lastg is not None:
+                preds[i].add(lastg)
+            lastg = i
+        for keys, w in ((rd, False), (wr, True)):
+            for x in keys:
+                lst = acc.setdefault(x[0], [])
+                if is_bank(x[0]):
+                    preds[i].update(e[2] for e in lst)
+                    acc[x[0]] = [(x, True, i)]
+                    continue
+                preds[i].update(e[2] for e in lst if (w or e[1]) and overlap(x, e[0]))
+                acc[x[0]] = [e for e in lst if not (w and covers(x, e[0]))] + [(x, w, i)]
+        preds[i].discard(i)
+    for i in range(n):
+        for j in preds[i]:
+            succs[j].append(i)
+    prio = [0.0] * n
+    for i in range(n - 1, -1, -1):
+        prio[i] = ops[i][4] + max([prio[j] + LAT for j in succs[i]] + [0.0])
+    left = [len(p) for p in preds]
+    start, fin, free = [0.0] * n, [0.0] * n, {}
+    ready = {i: ops[i][5] for i in range(n) if not left[i]}
+    while ready:
+        t0, _, i = min((max(ready[i], free.get(ops[i][0], 0.0)), -prio[i], i) for i in ready)
+        del ready[i]
+        q = ops[i][0]
+        start[i], fin[i] = t0, t0 + ops[i][4]
+        if q != "x":
+            free[q] = fin[i]
+        for j in succs[i]:
+            left[j] -= 1
+            if not left[j]:
+                ready[j] = max([ops[j][5]] + [fin[k] + (0.0 if ops[k][0] == "t" == ops[j][0] else LAT) for k in preds[j]])
+    return [ops[i] for i in sorted(range(n), key=lambda i: (start[i], i))]
+
+
+def main(g, core, T, topo, r, N):
+    eng = {"v": g.vector, "s": g.scalar, "t": g.tensor, "g": g, "y": g.sync}
+    qsem = {"v": "qv", "s": "qs", "t": "qt", "g": "qg"}
+    cnt = {"v": 0, "s": 0, "t": 0, "g": 0}
+    known = {q: {} for q in eng}
+    snaps, acc, ops = {}, {}, []
+
+    def need(q, sem, val):
+        k = known[q]
+        if k.get(sem, 0) >= val:
+            return
+        eng[q].wait_ge(T.sem[sem], val)
+        for s, v in snaps.get((sem, val), {}).items():
+            if k.get(s, 0) < v:
+                k[s] = v
+        k[sem] = val
+
+    def order(q, reads, writes):
+        todo = {}
+        for keys, w in ((reads, False), (writes, True)):
+            for x in keys:
+                keep = []
+                for e in acc.get(x[0], []):
+                    y, ew, eq, sem, val = e
+                    if is_bank(x[0]):
+                        hit = eq != q or ((ew or w) and overlap(x, y) if q != "t" else x[6:] != y[6:])
+                        drop = eq != q
+                    else:
+                        hit = (ew or w) and overlap(x, y)
+                        drop = w and covers(x, y)
+                    if hit and todo.get(sem, 0) < val:
+                        todo[sem] = val
+                    if not drop:
+                        keep.append(e)
+                acc[x[0]] = keep
+        for sem in sorted(todo, key=lambda s: (s == qsem.get(q), s)):
+            need(q, sem, todo[sem])
+
+    def note(q, reads, writes, sem, val):
+        for keys, w in ((reads, False), (writes, True)):
+            for x in keys:
+                lst = acc.setdefault(x[0], [])
+                lst[:] = [e for e in lst if not (e[0] == x and e[1] == w and e[2] == q and e[3] == sem)]
+                lst.append((x, w, q, sem, val))
+        snaps[(sem, val)] = dict(known.get(q, {}))
+
+    def rec(q, rd, wr, call, cost):
+        def emit():
+            order(q, rd, wr)
+            i = call()
+            if i is not None:
+                cnt[q] += 1
+                i.then_inc(T.sem[qsem[q]], 1)
+                note(q, rd, wr, qsem[q], cnt[q])
+        ops.append([q, rd, wr, emit, cost, 0.0])
+
+    def ext(writes, sem, val, when):
+        ops.append(["x", [], writes, lambda: note("ext", [], writes, sem, val), 0.01, when])
+
+    def A(n, c0=0, c1=None, st=1, p0=0, p1=128):
+        c1 = WIDTH[n] if c1 is None else c1
+        b, o = PLACE.get(n, (n, 0))
+        return (T[b][p0:p1, o + c0:o + c1] if st == 1 else T[b][p0:p1, o + c0:o + c1:st], [(n, p0, p1, c0, c1, st)], -(-(c1 - c0) // st))
+
+    def IND(w, o):
+        return (w[0].indirect(o[0]), w[1] + o[1], 16 * o[2], True)
+
+    def vcost(out, ins, per):
+        if any(len(o) > 3 for o in [out] + ins):
+            return 0.05 + 0.0015 * (2.5 if len(out) > 3 else 1) * out[2]
+        return 0.064 * max(1.0, per * out[2] / 64.0)
+
+    def copy(out, in_):
+        rec("v", in_[1], out[1], lambda: g.vector.tensor_copy(out[0], in_[0]), vcost(out, [in_], 1))
+
+    def tt(out, a, b, o):
+        wr, rd = out[1], a[1] + b[1]
+        if len(out) > 3:
+            wr, rd = out[1][:1], rd + out[1]
+        two = not (is_bank(a[1][0][0]) or is_bank(b[1][0][0]))
+        rec("v", rd, wr, lambda: g.vector.tensor_tensor(out[0], a[0], b[0], o), vcost(out, [a, b], 2 if two else 1))
+
+    def ts(out, a, s1, s2, o1, o2=None):
+        rd = a[1] + [k for s in (s1, s2) if isinstance(s, tuple) for k in s[1]]
+        v1 = s1[0] if isinstance(s1, tuple) else s1
+        v2 = s2[0] if isinstance(s2, tuple) else s2
+        if o2 is None:
+            rec("v", rd, out[1], lambda: g.vector.tensor_scalar(out[0], a[0], v1, v2, o1), vcost(out, [a], 1))
+        else:
+            rec("v", rd, out[1], lambda: g.vector.tensor_scalar(out[0], a[0], v1, v2, o1, o2), vcost(out, [a], 1))
+
+    def scan(out, d0, d1, init, o1, o2, per=1):
+        rec("v", d0[1] + d1[1], out[1], lambda: g.vector.tensor_tensor_scan(out[0], d0[0], d1[0], init, o1, o2), vcost(out, [], per))
+
+    def act(out, in_, f, bias=None):
+        c = 0.065 + 0.0015 * out[2] if len(in_) > 3 else 0.064 * max(1.0, out[2] / 64.0)
+        if bias is None:
+            rec("s", in_[1], out[1], lambda: g.scalar.activation(out[0], in_[0], f), c)
+        else:
+            rec("s", in_[1], out[1], lambda: g.scalar.activation(out[0], in_[0], f, bias=bias), c)
+
+    def mm(out, l, rh, start=True, stop=True, f32=False):
+        rec("t", l[1] + rh[1], [out[1][0] + l[1][0][1:3]], lambda: g.tensor.matmul(out[0], l[0], rh[0], start, stop), 0.001 * max(64, out[2]) * (4 if f32 else 1))
+
+    def ms(out, c):
+        rec("v", [], out[1], lambda: g.vector.memset(out[0], c), vcost(out, [], 1))
+
+    def iota(out, pat, base, cm, exact=False):
+        if exact:
+            rec("g", [], out[1], lambda: g.iota(out[0], pat, base, cm), 0.15 + 0.002 * out[2])
+        else:
+            rec("g", [], out[1], lambda: g.iota(out[0], pat, base, cm, allow_small_or_imprecise_dtypes=True), 0.15 + 0.002 * out[2])
+
+    def asel(out, in_, pat, cmp, fill, base, cm):
+        rec("g", in_[1], out[1], lambda: g.affine_select(out[0], in_[0], pat, cmp, fill, base, cm), 0.2 + 0.002 * out[2])
+
+    def remote(rd, f):
+        rec("g", rd, [], lambda: f(), 1.0)
+
+    hc = helper_of(core, T, topo)
+    qs = [(r + 1 + t) % N for t in range(4)]
+    others = [d for d in range(N) if d != r]
+    dkey = [("D", 0, 128, 0, 1, 1)]
+    own = A("TW", BLK * r + 16, BLK * (r + 1))
+    tot_loc = [0]
+
+    for k in range(8):
+        (g.sync if k % 2 == 0 else g.scalar).dma_start(T.D[:, 16 * k:16 * k + 16, :], T.tp[16 * k:16 * k + 16, :]).then_inc(T.sem.stg, 16)
+    g.scalar.dma_start(T.HT[:, 0:3], T.hw[:]).then_inc(T.sem.dhw, 16)
+    g.scalar.dma_start(T.HT[:, 3:4], T.th[:]).then_inc(T.sem.dhw, 16)
+    g.sync.dma_start(own[0], T.tz[:]).then_inc(T.sem.dtz, 16)
+    g.scalar.dma_start(T.TP[:], T.tp[:]).then_inc(T.sem.dtp, 16)
+    g.scalar.dma_start(T.SD[:], T.sd[:]).then_inc(T.sem.dsd, 16)
+    need("y", "stg", 128)
+    g.sync.dma_start(T.NL[:, 32 * r:32 * r + 32], T.D[r]).then_inc(T.sem.dnl, 16)
+    for k, sem, val, when in ((dkey, "stg", 128, 4.0), (A("HT")[1], "dhw", 32, 3.0), (own[1], "dtz", 16, 7.0), (A("TP")[1], "dtp", 16, 5.0),
+                              (A("SD")[1], "dsd", 16, 6.0), (A("NL", 32 * r, 32 * r + 32)[1], "dnl", 16, 7.0)):
+        ext(k, sem, val, when)
+
+    for q in range(N):
+        ms(A("TW", BLK * q, BLK * q + 16), -256.0)
+    ms(A("cone"), 1.0)
+    iota(A("cpi"), [[0, 1]], 0, 1, True)
+    iota(A("cmi"), [[0, 8], [1, 16]], 0, 0)
+    iota(A("clc"), [[1, 8], [16, 32]], 0, 0)
+    iota(A("cbf"), [[16, 16]], 0, 0)
+    asel(A("cid"), A("cone", 0, 128), [[-1, 128]], OP.is_equal, 0.0, 0, 1)
+
+    def fused(pairs, rsem):
+        tr = []
+        for i, (d, src, dst) in enumerate(pairs):
+            rid, pid = topo.addr(T.cores[d], core)
+            e = topo.engines(core, T.cores[d])
+            tr.append(RemoteDMATransfer(dst_ids=[DstId(rid=rid, pnc=pid)], dma_engine_mask=1 << e[i % len(e)], remote_sem=T.sem[rsem], srcs=[src], dsts=[dst]))
+        g.remote_dma_fused(tr, local_sem=T.sem.loc)
+        tot_loc[0] += len(tr)
+
+    def table_out(d, rsem, engines=None):
+        tot_loc[0] += send(g, T, topo, core, d, own[0], own[0], rsem, engines)
+
+    remote(dkey, lambda: fused([(d, T.D[d], T.NL[:, 32 * r:32 * r + 32]) for d in others], "nm"))
+    remote(A("HT")[1], lambda: fused([((r - 1 - t) % N, T.HT[:], T.HS[:, 4 * t:4 * t + 4]) for t in range(4)], "hs"))
+    for d in others:
+        ext(A("NL", 32 * d, 32 * d + 32)[1], "nm", N - 1, 8.0)
+    ext(A("HS")[1], "hs", 4, 9.0)
+    remote(own[1], lambda: table_out(hc, "rel", relay_engines(core, hc, topo, T)))
+    asel(A("cb1"), A("cone", 0, 128), [[-16, 8], [0, 16]], OP.is_ge, 0.0, 0, 1)
+    asel(A("cblk"), A("cb1"), [[16, 8], [0, 16]], OP.is_ge, 0.0, 15, -1)
+    asel(A("cg1"), A("cone", 0, 8), [[-16, 8]], OP.is_ge, 0.0, 0, 1)
+    asel(A("cg"), A("cg1"), [[16, 8]], OP.is_ge, 0.0, 15, -1)
+    iota(A("cbm0"), [[0, 8], [1, 16]], 0, 16)
+    iota(A("cohi"), [[1, 32]], 0, 0)
+    iota(A("cw0f"), [[0, 16]], 256, 1)
+    iota(A("cpc"), [[16, 3], [-256, 8]], 0, 0, True)
+    ts(A("NO"), A("NL"), 16.0, None, OP.add)
+    win = A("TW", BLK * r, BLK * (r + 1))
+    for i, d in enumerate(others + [r]):
+        o, a = A("FO", 512 * d, 512 * d + 512), IND(win, A("NO", 32 * d, 32 * d + 32))
+        if i % 2:
+            copy(o, a)
+        else:
+            act(o, a, AF.Copy)
+    remote(A("FO", 0, 512 * r)[1] + A("FO", 512 * r + 512, 4096)[1],
+           lambda: fused([(d, T.FO[:, 512 * d:512 * d + 512], T.FI[:, 512 * r:512 * r + 512]) for d in others], "ft"))
+    act(A("FI", 512 * r, 512 * r + 512), A("FO", 512 * r, 512 * r + 512), AF.Copy)
+    for d in others:
+        ext(A("FI", 512 * d, 512 * d + 512)[1], "ft", N - 1, 20.0)
+    for o in (3, 5, 7):
+        remote(own[1], lambda o=o: table_out(T.cores[(r - o) % N], "tbx"))
+    for q in others:
+        ext(A("TW", BLK * q + 16, BLK * (q + 1))[1], *(("tb0", 8, 24.0) if q == qs[0] else ("tbx", 48, 60.0)))
+    iota(A("cio"), [[1, 256]], 0, 0)
+    iota(A("ci2"), [[1, 256]], 0, 0)
+    ms(A("cth"), 14.0)
+    asel(A("cth"), A("cth"), [[0, 4], [1, 128]], OP.is_gt, 1000.0, 0, -1)
+
+    ts(A("cpj"), A("cpi"), 15, None, OP.bitwise_and)
+    ts(A("cpq"), A("cpj"), 1, None, OP.arith_shift_right)
+    ts(A("cpt"), A("cpi"), 4, 1, OP.arith_shift_right, OP.bitwise_and)
+    copy(A("cj"), A("cpj"))
+    copy(A("cq"), A("cpq"))
+    copy(A("cpar"), A("cpt"))
+    ts(A("cn"), A("cj"), -16.0, None, OP.mult)
+    ts(A("cR"), A("cpc"), A("cn"), None, OP.add)
+    ts(A("ceb"), A("cq"), float(BLK), 15.0, OP.mult, OP.add)
+    ts(A("cs"), A("cq"), 496.0, None, OP.mult)
+    ts(A("clb"), A("cj"), 8.0, A("cs"), OP.mult, OP.add)
+    ts(A("LC"), A("clc"), A("clb"), None, OP.add)
+    ts(A("cba"), A("cbf"), A("cj"), None, OP.add)
+    ts(A("cbai"), A("cba"), 4.0, None, OP.mult)
+    ts(A("cb2"), A("cba"), 256.0, None, OP.add)
+    for n, fill, first in (("cmh", 256.0, 0.0), ("cml", 0.0, 255.0)):
+        ms(A(n), fill)
+        ms(A(n, 0, 512, 16), first)
+    ms(A("cm0"), 0.0)
+    ms(A("cm0", 0, 128, 16), BIG)
+    ms(A("HST"), 0)
+    ms(A("cnegf"), -2048.0)
+    copy(A("cneg"), A("cnegf"))
+    copy(A("cib"), A("cid"))
+    copy(A("cih"), A("cid"))
+    copy(A("cbm"), A("cbm0"))
+    ts(A("cnb"), A("cid"), -1.0, None, OP.mult)
+    copy(A("cblb"), A("cblk"))
+    ts(A("cgk"), A("cg"), 2048.0, None, OP.mult)
+    ts(A("cmk"), A("cmi"), A("cj"), None, OP.is_equal)
+    ts(A("coh"), A("cohi"), A("cj"), None, OP.is_equal)
+    copy(A("cw0"), A("cw0f"))
+    ts(A("cw1"), A("cw0f"), 128.0, None, OP.add)
+    copy(A("HF"), A("HS"))
+    ts(A("kd"), A("HS"), 1, None, OP.bitwise_and)
+    for t in range(4):
+        for i in range(2):
+            ts(A("WF", 16 * t + 8 * i, 16 * t + 8 * i + 8), A("cg"), A("HF", 4 * t + i, 4 * t + i + 1), None, OP.mult)
+        copy(A("WB", 16 * t, 16 * t + 16), A("WF", 16 * t, 16 * t + 16))
+        ts(A("WH", 16 * t, 16 * t + 16), A("WF", 16 * t, 16 * t + 16), 0.5, None, OP.mult)
+        ts(A("th", t, t + 1), A("HF", 4 * t + 3, 4 * t + 4), 2048.0, None, OP.mult)
+        ts(A("hcol", t, t + 1), A("kd", 4 * t + 2, 4 * t + 3), -2048.0, 4196352.0, OP.mult, OP.add)
+        copy(A("ZZ", 16 * t, 16 * t + 8), A("cg"))
+        ts(A("ZZ", 16 * t + 8, 16 * t + 16), A("cg"), A("HF", 4 * t + 2, 4 * t + 3), None, OP.mult)
+        b = A("B%d" % (5 + t % 2), 0, 128, 1, 0, 16)
+        mm(b, A("ZZ", 16 * t, 16 * t + 16), A("cih"))
+        copy(A("KM", 128 * t, 128 * t + 128, 1, 0, 16), b)
+        x = float(2 * qs[t] + t // N)
+        ts(A("ntx", t, t + 1), A("cj"), x, None, OP.not_equal)
+        ts(A("XM"), A("cmi"), x, None, OP.is_equal)
+        tt(A("XS", 128 * t, 128 * t + 128), A("XM"), A("cblk"), OP.mult)
+    ts(A("P", 0, 256), A("TP"), 1.0, None, OP.add)
+    ts(A("S"), A("SD"), 1.0, None, OP.add)
+    for j in range(16):
+        ts(A("cbt", j, j + 1), A("cj"), float(j), float(2 ** (12 - j)) if j < 13 else (-1.0 if j == 13 else 0.0), OP.is_equal, OP.mult)
+    rec("v", A("cbt")[1], A("csc")[1], lambda: g.vector.tensor_reduce(A("csc")[0], A("cbt")[0], AxisListType.X, OP.add), 0.07)
+    ts(A("cnpar"), A("cpar"), -1.0, 1.0, OP.mult, OP.add)
+    ts(A("cc", 4, 5), A("cj"), 13.0, 1.0 / 2048, OP.is_lt, OP.mult)
+    ts(A("cc", 5, 6), A("cj"), 13.0, 1.0 / 4096, OP.is_equal, OP.mult)
+    tt(A("cc", 6, 7), A("cc", 4, 5), A("cc", 5, 6), OP.add)
+    ts(A("cc", 7, 8), A("cj"), 13.0, -1.0, OP.is_lt, OP.mult)
+    for i, m in ((0, "cnpar"), (1, "cpar")):
+        tt(A("cc", 2 * i, 2 * i + 1), A("cc", 6, 7), A(m), OP.mult)
+        tt(A("cc", 2 * i + 1, 2 * i + 2), A("cc", 7, 8), A(m), OP.mult)
+
+    def middle(h, t):
+        s = "_%d" % h
+        if t:
+            ts(A("EO", 128 * h, 128 * h + 128), A("P", 128 * h, 128 * h + 128), A("ceb"), None, OP.add)
+        for k in range(4):
+            c, o = 512 * k, 128 * h + 32 * k
+            src = IND(A("TW"), A("EO", o, o + 32)) if t else IND(A("FI"), A("LC", o, o + 32))
+            if k in EV:
+                copy(A("FA" + s, c, c + 512), src)
+            else:
+                act(A("FA" + s, c, c + 512), src, AF.Copy)
+            act(A("FB" + s, c, c + 512), A("FA" + s, c, c + 512), AF.Abs)
+            scan(A("HI" + s, c, c + 512), A("cmh"), A("FA" + s, c, c + 512), 0.0, OP.min, OP.max, 0.5)
+            scan(A("LO" + s, c, c + 512), A("cml"), A("FB" + s, c, c + 512), 255.0, OP.max, OP.min, 0.5)
+        tt(A("SE" + s), A("HI" + s, 15, 2048, 16), A("LO" + s, 15, 2048, 16), OP.add)
+        ts(A("EI" + s), A("SE" + s), 0.5, -0.25, OP.mult, OP.add)
+        copy(A("EB" + s), A("EI" + s))
+        for m in range(16):
+            if m % 8 < 5:
+                copy(A("ER" + s, m, 2048, 16), A("EB" + s))
+            else:
+                act(A("ER" + s, m, 2048, 16), A("EB" + s), AF.Copy)
+        ts(A("E2" + s, 0, KV), A("EI" + s, 0, KV), 2.0, 2047.5, OP.mult, OP.add)
+        ts(A("E2" + s, KV, 128), A("EI" + s, KV, 128), 2047.5, None, OP.add)
+
+    def hash_(h, p, t):
+        s, b = "_%d" % h, "B%d" % (5 + h)
+        u = A(b, 0, 16)
+        if p == 0:
+            mm(u, A("EB" + s), A("WB", 16 * t, 16 * t + 16))
+        else:
+            mm(u, A("cneg"), A("WH", 16 * t, 16 * t + 16), True, False)
+            mm(u, A("C" + s), A("WH", 16 * t, 16 * t + 16), False, True)
+        copy(A("UI" + s), u)
+        ts(A("UA" + s), A("UI" + s), 4095, None, OP.bitwise_and)
+        tt(A("VP" + s), A("UA" + s, 0, 8), A("UA" + s, 8, 16), OP.mult)
+        ts(A("UA" + s, 0, 8), A("VP" + s), 5, 4095, OP.arith_shift_right, OP.bitwise_and)
+        ts(A("HB" + s), A("UA" + s), -2048.0, None, OP.add)
+        x, y = A(b, 16, 144, 1, 0, 16), A("HX" + s, 0, 128, 1, 0, 16)
+        mm(x, A("HB" + s), A("cih"))
+        copy(y, x)
+        hh = A(b, 144, 272)
+        mm(hh, A("KM", 128 * t, 128 * t + 128, 1, 0, 16), y)
+        ts(A("HN" + s), hh, A("hcol", t, t + 1), None, OP.add)
+        d = A("HST", 512 * h + p, 512 * h + 512, 4)
+        ts(d, A("HN" + s), 4095, None, OP.bitwise_and)
+        copy(A("OF" + s), d)
+
+    def look(h, t):
+        s, kb = "_%d" % h, "B%d" % (3 + h)
+        w = A("TW", BLK * qs[t] + 16, BLK * qs[t] + BLK)
+        mm(A(kb, 0, 128), A("cih"), A("cbm"), True, False)
+        for c in range(0, KV, KC):
+            x = (16 * c, 16 * min(KV, c + KC))
+            tt(A("XV" + s, *x), IND(w, A("OF" + s, c, min(KV, c + KC))), A("ER" + s, *x), OP.subtract)
+            act(A("AX" + s, *x), A("XV" + s, *x), AF.Abs)
+        for i, c in enumerate(range(16 * KV, 2048, 512)):
+            n = min(512, 2048 - c)
+            b = A("B%d" % i, 0, n)
+            act(A("XV" + s, c, c + n), IND(w, A("OF" + s, c // 16, (c + n) // 16)), AF.Copy)
+            mm(b, A("cnb"), A("ER" + s, c, c + n), True, False)
+            mm(b, A("cib"), A("XV" + s, c, c + n), False, True)
+            act(A("AX" + s, c, c + n), b, AF.Abs)
+        for m in range(16):
+            mm(A(kb, m, 128, 16), A("AX" + s, m, 2048, 16), A("cgk"), False, m == 15)
+
+    def winner(h, p):
+        s = "_%d" % h
+        scan(A("SC" + s), A("cm0"), A("B%d" % (3 + h), 0, 128), BIG, OP.max, OP.min)
+        for k in range(8):
+            ts(A("LT" + s, 16 * k, 16 * k + 16), A("cmk", 0, 16), A("SC" + s, 16 * k + 15, 16 * k + 16), None, OP.mult)
+        sp = A("B%d" % (5 + h), 280, 288)
+        mm(sp, A("LT" + s), A("cg"), f32=True)
+        if p < 2:
+            copy(A("KI" + s), sp)
+            ts(A("J" + s), A("KI" + s), 2047, None, OP.bitwise_and)
+            copy(A("JU" + s, 0, 8), A("J" + s))
+            tt(A("C" + s), IND(A("XV" + s), A("JU" + s, 0, 8)), A("E2" + s), OP.add)
+        tt(A("R" + s, 8 * p, 8 * p + 8), sp, A("cR", 8 * p, 8 * p + 8), OP.add)
+
+    def names(h, t):
+        s, c0, c1 = "_%d" % h, 128 * h, 128 * h + 128
+        tt(A("BA" + s), A("R" + s, 0, 8), A("R" + s, 8, 16), OP.min)
+        tt(A("BK" + s), A("BA" + s), A("R" + s, 16, 24), OP.min)
+        ts(A("PI" + s), A("BK" + s), 4, 3, OP.arith_shift_right, OP.bitwise_and)
+        ts(A("MI" + s), A("BK" + s), 15, None, OP.bitwise_and)
+        ts(A("VAL" + s), A("BK" + s), A("th", t, t + 1), None, OP.is_lt)
+        tt(A("L1" + s), A("PI" + s), A("cbai", 8 * h, 8 * h + 8), OP.add)
+        ts(A("M1" + s), A("MI" + s), -16.0, None, OP.add)
+        copy(A("L1U" + s), A("L1" + s))
+        tt(A("M2" + s), A("M1" + s), A("VAL" + s), OP.mult)
+        ts(A("L2U" + s), A("M2" + s), 16.0, None, OP.add)
+        ts(A("GG" + s), IND(A("HST"), A("L1U" + s)), 1.0, 1.0, OP.mult, OP.add)
+        tt(A("PR" + s), IND(A("coh"), A("L2U" + s)), A("GG" + s), OP.mult)
+        nrep, nx = A("B7", c0, c1), A("B7", 256 + c0, 256 + c1)
+        mm(nrep, A("cblk"), A("PR" + s), f32=True)
+        mm(nx, A("XS", 128 * t, 128 * t + 128), A("PR" + s), f32=True)
+        ts(A("I1" + s), nrep, A("csc"), None, OP.mult)
+        ts(A("I2" + s), A("I1" + s), 4096, None, OP.bitwise_and)
+        ts(A("BE", c0, c1), A("I2" + s), A("cc", 0, 1), A("cc", 1, 2), OP.mult, OP.add)
+        ts(A("BO", c0, c1), A("I2" + s), A("cc", 2, 3), A("cc", 3, 4), OP.mult, OP.add)
+        tt(A("B3", 128 + c0, 128 + c1), nx, A("PK" + s), OP.add)
+        copy(A("P", c0, c1), A("B3", 128 + c0, 128 + c1))
+
+    def pairs(t):
+        ps = A("B3", 128, 384)
+        for banks, a0, b0, out in (((0, 1), 0, 0, "QA"), ((2, 4), 0, 128, "QX"), ((5, 6), 128, 128, "QB")):
+            for k in (0, 1, 4, 5, 2, 3, 6, 7):
+                src, p0 = "BE" if k % 2 == 0 else "BO", 32 * (k // 2)
+                mm(A("B%d" % banks[k // 4], 128 * (k % 4), 128 * (k % 4) + 128), A(src, a0, a0 + 128, 1, p0, p0 + 32), A(src, b0, b0 + 128, 1, p0, p0 + 32))
+            for i in range(2):
+                o, b = A(out, 512 * i, 512 * i + 512), A("B%d" % banks[i])
+                if out == "QX":
+                    act(o, b, AF.Relu, bias=-13.0)
+                else:
+                    tt(o, b, A("cth"), OP.is_ge)
+        for k in range(8):
+            mm(A("B7", 16 * k, 16 * k + 16), A("QA", 128 * k, 128 * k + 128), A("cw0"))
+        for k in range(8):
+            o = A("B4", 16 * k, 16 * k + 16)
+            mm(o, A("QX", 128 * k, 128 * k + 128), A("cw0"), True, False)
+            mm(o, A("QB", 128 * k, 128 * k + 128), A("cw1"), False, True)
+        for h, b in ((0, "B7"), (1, "B4")):
+            tt(A("LT_%d" % h), A(b, 0, 128), A("cmk"), OP.mult)
+        for h in range(2):
+            mm(A("B0", 8 * h, 8 * h + 8), A("LT_%d" % h), A("cg"), f32=True)
+        v = A("B0", 0, 16)
+        ts(A("Y1"), v, 256.0, None, OP.is_ge)
+        ts(A("Y2"), v, 512.0, None, OP.is_lt)
+        tt(A("DD"), v, A("cb2"), OP.subtract)
+        tt(A("SEC"), A("Y1"), A("Y2"), OP.mult)
+        tt(A("DS"), A("DD"), A("SEC"), OP.mult)
+        tt(A("LF"), A("DS"), A("cba"), OP.add)
+        copy(A("LU"), A("LF"))
+        ts(A("EE"), A("SEC"), -256.0, 256.0, OP.mult, OP.add)
+        tt(A("LSF"), A("LF"), A("EE"), OP.add)
+        copy(A("LSU"), A("LSF"))
+        copy(A("Q"), IND(A("P", 0, 256), A("LU")))
+        ne, cn, pn, nc = A("B2", 0, 256), A("B1", 0, 256), A("B6", 0, 256), A("B5", 0, 256)
+        tt(ne, ps, A("Q"), OP.not_equal)
+        tt(A("MN"), ps, A("Q"), OP.min)
+        tt(A("SP"), A("S"), ps, OP.subtract)
+        tt(A("QN"), ne, A("MN"), OP.mult)
+        ts(A("ND"), A("QN"), 0.0, None, OP.is_le)
+        mm(cn, A("cblb"), A("ND"))
+        tt(A("SN"), IND(A("cio"), A("LU")), A("ci2"), OP.not_equal)
+        tt(A("SPS"), A("SP"), A("SN"), OP.mult)
+        tt(pn, ps, A("ND"), OP.mult)
+        tt(A("QN"), A("Q"), A("ND"), OP.mult)
+        ts(nc, cn, 15.5, None, OP.is_ge)
+        tt(A("SX"), A("SPS"), nc, OP.mult)
+        tt(A("PC"), A("P", 0, 256), nc, OP.mult)
+        tt(A("P", 0, 256), A("SX"), pn, OP.add)
+        tt(IND(A("P"), A("LSU")), A("QN"), A("PC"), OP.max)
+
+    for t in range(4):
+        for h in range(2):
+            middle(h, t)
+            hash_(h, 0, t)
+            ts(A("PK_%d" % h), A("P", 128 * h, 128 * h + 128), A("ntx", t, t + 1), None, OP.mult)
+            look(h, t)
+        for p in range(3):
+            for h in range(2):
+                winner(h, p)
+                if p < 2:
+                    hash_(h, p + 1, t)
+                    look(h, t)
+                else:
+                    names(h, t)
+        pairs(t)
+    ts(A("YO"), A("P", 0, 256), -1.0, None, OP.add)
+
+    for o in schedule(ops):
+        o[3]()
+    order("y", A("YO")[1], [])
+    g.sync.dma_start(T.yp[:], T.YO[:]).then_inc(T.sem.dyp, 16)
+    need("y", "dyp", 16)
+    g.wait_ge(T.sem.loc, tot_loc[0])
+    for q in ("v", "s", "t", "g"):
+        need("y", qsem[q], cnt[q])

@@ -2,35 +2,45 @@ from concourse.bass import DstId, RemoteDMATransfer
 from concourse.mybir import AluOpType as OP, AxisListType, ActivationFunctionType as AF
 
 BLK = 4112
-KV, KC = 80, 32
-EV = (1, 3)
+ST = ((0, 6), (6, 11), (11, 16))
+LOOK = (("b", 0, 4), ("d", 8, 12), ("b", 4, 8), ("d", 12, 16))
+R0 = max(x[2] for x in LOOK if x[0] != "d")
+VSUB = 2
+MID = "svs"
+BANKS = {2: dict(key=(3, 4), hash=(5, 6), diff=((0, 1), (2, 7)), ps=(3, 128), QA=(0, 1), QX=(2, 7), QB=(5, 6), low=(0, 1), rest=(2, 1, 6, 7, 4)),
+         3: dict(key=(0, 1, 2), hash=(0, 1, 2), diff=((3, 7), (4, 7), (5, 7)), ps=(6, 0), QA=(3, 4), QX=(0, 1), QB=(5, 7), low=(3, 4), rest=(0, 1, 5, 7, 2)),
+         4: dict(key=(0, 1, 2, 3), hash=(0, 1, 2, 3), diff=((4,), (5,), (6,), (7,)), ps=(7, 256), QA=(4, 5), QX=(0, 1), QB=(2, 6), low=(4, 5), rest=(0, 1, 2, 6, 3))}[len(ST)]
 BIG = 16777216.0
-LAT = 0.1
+LAT, CY, GA, TF = 0.2, 0.00104, 1.56, 0.7
+SKEW, BONUS, SMALL, AHEAD, ROUNDS = 2.0, 10.0, 0.22, 0.3, 4
 F32, BF, I32, U16, F16 = "float32", "bfloat16", "int32", "uint16", "float16"
+NCS = sorted(set(b - a for a, b in ST))
 
 SCRATCH = {"TW": ("sbuf", [128, 8 * BLK], BF), "D": ("dram", [8, 128, 32], I32)}
-WIDTH, PLACE, _used = {"TW": 8 * BLK, "D": 1}, {}, {}
+WIDTH, PLACE, TWO, _used = {"TW": 8 * BLK, "D": 1}, {}, {"TW", "FO", "FI"}, {}
 for _n, _w, _d in (("NL", 256, I32), ("HT", 4, I32), ("HS", 16, I32), ("FO", 4096, BF), ("FI", 4096, BF), ("P", 512, F32), ("TP", 256, I32), ("SD", 256, I32), ("YO", 256, F32)):
     SCRATCH[_n], WIDTH[_n] = ("sbuf", [128, _w], _d), _w
 for _k in range(8):
     SCRATCH["B%d" % _k], WIDTH["B%d" % _k] = ("psum", [128, 512], F32), 512
-SPEC = ((BF, 1, "FA 2048 FB 2048 HI 2048 LO 2048 ER 2048 XV 2048 AX 2048 EB 128"), (F16, 1, "HB 16 HX 128 C 128"), (U16, 1, "OF 128 JU 16 L1U 8 L2U 8"),
-        (F32, 1, "SE 128 E2 128 SC 128 LT 128 VAL 8 M1 8 M2 8 GG 128 PR 128 PK 128"),
-        (I32, 1, "EI 128 UI 16 UA 16 VP 8 HN 128 KI 8 J 8 R 24 I1 128 I2 128 BA 8 BK 8 PI 8 L1 8 MI 8"),
-        (F32, 0, "Y1 16 Y2 16 SEC 16 DD 16 DS 16 LF 16 EE 16 LSF 16 SN 256 Q 256 MN 256 QN 256 SP 256 SPS 256 SX 256 PC 256 S 256 HF 16 cone 512 cid 128 "
-                 "cb1 128 cblk 128 cg1 8 cg 8 cmi 128 cmk 128 cm0 128 cj 1 cq 1 cs 1 cn 1 cpar 1 cnpar 1 ceb 1 clb 1 cba 16 cb2 16 cbf 16 cio 256 ci2 256 "
-                 "clc 256 cth 512 cw0f 16 coh 32 cohi 32 cbt 16 csc 1 cc 8 cnegf 128 ntx 4 XM 128 XS 512 th 4 hcol 4 WF 64 cbm0 128"),
-        (I32, 0, "HST 1024 cpi 1 cpj 1 cpq 1 cpt 1 cbai 16 cpc 24 cR 24 kd 16"),
-        (BF, 0, "BE 256 BO 256 QA 1024 QX 1024 QB 1024 ND 256 cib 128 cnb 128 cblb 128 cgk 8 cmh 512 cml 512 WB 64"),
-        (U16, 0, "NO 256 EO 256 LC 256 LU 16 LSU 16"), (F16, 0, "cw0 16 cw1 16 cneg 128 cih 128 cbm 128 WH 64 ZZ 64 KM 512"))
+SPEC = ((BF, 1, "ET 128"), (F16, 1, "HB 16"), (U16, 1, "JU 8 L1U 8 L2U 8"), (I32, 1, "UI 16 UA 16 VP 8 KI 16 J 8 BA 8 BB 8 BK 8 PI 8 L1 8 MI 8 cbai 8"),
+        (F32, 2, "cpm 128 cr 1 cr4 1"), (BF, 2, "cpb 128 SEL 2048"), (F16, 2, "cph 128"),
+        (F32, 0, "E2 256 SC 256 PR 256 LA 256 LT 256 Q 256 QN 256 SX 256 SP 256 PC 256 S 256 HF 16 cone 128 cid 128 cb1 128 cblk 128 cg1 8 cg 8 cgn 8 cmi 128 cmk 128 "
+                 "cm0 128 cj 1 cq 1 cs 1 cp 1 cbb 2 cpar 1 cnpar 1 ceb 1 clb 1 cb2 16 cbf 16 cbc 8 clc 256 ctf 128 cw0f 16 cbt 16 csc 1 cc 8 "
+                 "ntx 4 XM 128 XS 512 DX 512 th 4 hcol 4 cio 384 cth 512"),
+        (I32, 0, "HST 1024 HN 256 I1 256 I2 256 cpi 1 cpj 1 cpq 1 cpt 1 kd 16"),
+        (BF, 0, "FA 4096 FB 4096 HI 4096 LO 4096 IJ 4096 ER 4096 XV 4096 AX 4096 EB 256 OH 256 BE 256 BO 256 QA 1024 QX 1024 QB 1024 ND 256 MN 256 TT 256 SN 256 "
+                "cib 128 c2b 128 cnb 128 cblb 128 cmh 512 cml 512 ckp 512 ctri 512 cpen 128 csn 512 coh 512 XB 512 ZA 144 ZB 144 ZN 144"),
+        (U16, 0, "NO 256 EO 256 LC 256 OF 256 LSU 16"), (F16, 0, "C 256 HX 256 cw0 16 cw1 16 cneg 128 cih 128 cbm 384 WH 64 ZZ 64 KM 512"))
 ARENA = {F32: "af", BF: "ab", I32: "ai", U16: "au", F16: "ah"}
-for _d, _half, _s in SPEC:
+for _d, _each, _s in SPEC:
     _it = _s.split()
     for _n, _w in zip(_it[::2], _it[1::2]):
-        for _t in (("_0", "_1") if _half else ("",)):
+        for _t in ([""], ["_%d" % _k for _k in range(len(ST))], ["_%d" % _k for _k in NCS])[_each]:
             _a, _step = ARENA[_d], 16 if _d in (F32, I32) else 32
             PLACE[_n + _t], WIDTH[_n + _t] = (_a, _used.get(_a, 0)), int(_w)
             _used[_a] = _used.get(_a, 0) - (-int(_w) // _step) * _step
+            if _step == 32:
+                TWO.add(_n + _t)
 for _d in ARENA:
     SCRATCH[ARENA[_d]] = ("sbuf", [128, _used[ARENA[_d]]], _d)
 SEMAPHORES = ["qv", "qs", "qt", "qg", "stg", "dtz", "dhw", "dtp", "dsd", "dnl", "dyp", "nm", "hs", "ft", "tb0", "tbx", "rel", "loc"]
@@ -92,7 +102,7 @@ def covers(x, y):
 def schedule(ops):
     n = len(ops)
     preds, succs, acc, lastg = [set() for _ in ops], [[] for _ in ops], {}, None
-    for i, (q, rd, wr, _, _, _) in enumerate(ops):
+    for i, (q, rd, wr) in enumerate(o[:3] for o in ops):
         if q == "g":
             if lastg is not None:
                 preds[i].add(lastg)
@@ -110,24 +120,63 @@ def schedule(ops):
     for i in range(n):
         for j in preds[i]:
             succs[j].append(i)
+    queue, cost = [o[0] for o in ops], [o[4] for o in ops]
+
+    def lat(i, k):
+        return 0.0 if queue[k] == "t" == queue[i] or "x" in (queue[i], queue[k]) else LAT
+
+    def pack(turns, before, earliest):
+        start, fin, busy = [0.0] * n, [0.0] * n, {}
+        for i in turns:
+            q, t = queue[i], max([earliest[i]] + [fin[k] + lat(i, k) for k in before[i]])
+            if q != "x":
+                s = busy.setdefault(q, [])
+                lo, hi = 0, len(s)
+                while lo < hi:
+                    mid = (lo + hi) // 2
+                    if s[mid][1] <= t:
+                        lo = mid + 1
+                    else:
+                        hi = mid
+                while lo < len(s) and s[lo][0] < t + cost[i]:
+                    t = max(t, s[lo][1])
+                    lo += 1
+                s.insert(lo, (t, t + cost[i]))
+            start[i], fin[i] = t, t + cost[i]
+        return start, fin
+
     prio = [0.0] * n
     for i in range(n - 1, -1, -1):
-        prio[i] = ops[i][4] + max([prio[j] + LAT for j in succs[i]] + [0.0])
+        prio[i] = cost[i] + max([prio[j] + LAT for j in succs[i]] + [0.0])
+    prio = [p + SKEW * o[6] + BONUS * (o[4] < SMALL) for p, o in zip(prio, ops)]
     left = [len(p) for p in preds]
-    start, fin, free = [0.0] * n, [0.0] * n, {}
+    start, fin, free, turns = [0.0] * n, [0.0] * n, {}, []
     ready = {i: ops[i][5] for i in range(n) if not left[i]}
     while ready:
-        t0, _, i = min((max(ready[i], free.get(ops[i][0], 0.0)), -prio[i], i) for i in ready)
+        t0, _, i = min((max(ready[i], free.get(queue[i], 0.0)), -prio[i], i) for i in ready)
+        q = queue[i]
+        if q != "x":
+            soon = [j for j in ready if queue[j] == q and prio[j] > prio[i] and ready[j] < t0 + AHEAD * cost[i]]
+            if soon:
+                i = max(soon, key=lambda j: prio[j])
+                t0 = max(t0, ready[i])
         del ready[i]
-        q = ops[i][0]
-        start[i], fin[i] = t0, t0 + ops[i][4]
+        turns.append(i)
+        start[i], fin[i] = t0, t0 + cost[i]
         if q != "x":
             free[q] = fin[i]
         for j in succs[i]:
             left[j] -= 1
             if not left[j]:
-                ready[j] = max([ops[j][5]] + [fin[k] + (0.0 if ops[k][0] == "t" == ops[j][0] else LAT) for k in preds[j]])
-    return [ops[i] for i in sorted(range(n), key=lambda i: (start[i], i))]
+                ready[j] = max([ops[j][5]] + [fin[k] + lat(j, k) for k in preds[j]])
+    first, none, best = [o[5] for o in ops], [0.0] * n, (max(fin), start)
+    for _ in range(ROUNDS):
+        start, fin = pack(turns, preds, first)
+        if max(fin) < best[0]:
+            best = (max(fin), start)
+        start, fin = pack(sorted(range(n), key=lambda i: (-fin[i], -start[i], -i)), succs, none)
+        turns = sorted(range(n), key=lambda i: (-fin[i], -start[i], i))
+    return [ops[i] for i in sorted(range(n), key=lambda i: (best[1][i], i))]
 
 
 def main(g, core, T, topo, r, N):
@@ -135,7 +184,7 @@ def main(g, core, T, topo, r, N):
     qsem = {"v": "qv", "s": "qs", "t": "qt", "g": "qg"}
     cnt = {"v": 0, "s": 0, "t": 0, "g": 0}
     known = {q: {} for q in eng}
-    snaps, acc, ops = {}, {}, []
+    snaps, acc, ops, lead = {}, {}, [], [0]
 
     def need(q, sem, val):
         k = known[q]
@@ -184,10 +233,13 @@ def main(g, core, T, topo, r, N):
                 cnt[q] += 1
                 i.then_inc(T.sem[qsem[q]], 1)
                 note(q, rd, wr, qsem[q], cnt[q])
-        ops.append([q, rd, wr, emit, cost, 0.0])
+        ops.append([q, rd, wr, emit, cost, 0.0, lead[0]])
 
-    def ext(writes, sem, val, when):
-        ops.append(["x", [], writes, lambda: note("ext", [], writes, sem, val), 0.01, when])
+    def ext(writes, sem, val, when, after=False):
+        if after:
+            ops.append(["x", [(sem, 0, 1, 0, 1, 1)], writes, lambda: note("ext", [], writes, sem, val), when, 0.0, 0])
+        else:
+            ops.append(["x", [], writes, lambda: note("ext", [], writes, sem, val), 0.01, when, 0])
 
     def A(n, c0=0, c1=None, st=1, p0=0, p1=128):
         c1 = WIDTH[n] if c1 is None else c1
@@ -197,13 +249,15 @@ def main(g, core, T, topo, r, N):
     def IND(w, o):
         return (w[0].indirect(o[0]), w[1] + o[1], 16 * o[2], True)
 
-    def vcost(out, ins, per):
+    def vcost(out, ins, per=None):
         if any(len(o) > 3 for o in [out] + ins):
-            return 0.05 + 0.0015 * (2.5 if len(out) > 3 else 1) * out[2]
-        return 0.064 * max(1.0, per * out[2] / 64.0)
+            return 0.05 + CY * (3.8 if len(out) > 3 else GA) * out[2]
+        if per is None:
+            per = 0.5 if all(o[1][0][0] in TWO for o in [out] + ins) else 1
+        return CY * max(64.0, per * out[2])
 
     def copy(out, in_):
-        rec("v", in_[1], out[1], lambda: g.vector.tensor_copy(out[0], in_[0]), vcost(out, [in_], 1))
+        rec("v", in_[1], out[1], lambda: g.vector.tensor_copy(out[0], in_[0]), vcost(out, [in_]))
 
     def tt(out, a, b, o):
         wr, rd = out[1], a[1] + b[1]
@@ -217,25 +271,25 @@ def main(g, core, T, topo, r, N):
         v1 = s1[0] if isinstance(s1, tuple) else s1
         v2 = s2[0] if isinstance(s2, tuple) else s2
         if o2 is None:
-            rec("v", rd, out[1], lambda: g.vector.tensor_scalar(out[0], a[0], v1, v2, o1), vcost(out, [a], 1))
+            rec("v", rd, out[1], lambda: g.vector.tensor_scalar(out[0], a[0], v1, v2, o1), vcost(out, [a]))
         else:
-            rec("v", rd, out[1], lambda: g.vector.tensor_scalar(out[0], a[0], v1, v2, o1, o2), vcost(out, [a], 1))
+            rec("v", rd, out[1], lambda: g.vector.tensor_scalar(out[0], a[0], v1, v2, o1, o2), vcost(out, [a]))
 
-    def scan(out, d0, d1, init, o1, o2, per=1):
-        rec("v", d0[1] + d1[1], out[1], lambda: g.vector.tensor_tensor_scan(out[0], d0[0], d1[0], init, o1, o2), vcost(out, [], per))
+    def scan(out, d0, d1, init, o1, o2):
+        rec("v", d0[1] + d1[1], out[1], lambda: g.vector.tensor_tensor_scan(out[0], d0[0], d1[0], init, o1, o2), vcost(out, [d0, d1]))
 
-    def act(out, in_, f, bias=None):
-        c = 0.065 + 0.0015 * out[2] if len(in_) > 3 else 0.064 * max(1.0, out[2] / 64.0)
-        if bias is None:
-            rec("s", in_[1], out[1], lambda: g.scalar.activation(out[0], in_[0], f), c)
-        else:
-            rec("s", in_[1], out[1], lambda: g.scalar.activation(out[0], in_[0], f, bias=bias), c)
+    def act(out, in_, f, **kw):
+        c = 0.065 + CY * GA * out[2] if len(in_) > 3 else CY * max(64.0, out[2])
+        rd = in_[1] + [k for s in kw.values() if isinstance(s, tuple) for k in s[1]]
+        kw = {k: s[0] if isinstance(s, tuple) else s for k, s in kw.items()}
+        rec("s", rd, out[1], lambda: g.scalar.activation(out[0], in_[0], f, **kw), c)
 
-    def mm(out, l, rh, start=True, stop=True, f32=False):
-        rec("t", l[1] + rh[1], [out[1][0] + l[1][0][1:3]], lambda: g.tensor.matmul(out[0], l[0], rh[0], start, stop), 0.001 * max(64, out[2]) * (4 if f32 else 1))
+    def mm(out, l, rh, start=True, stop=True):
+        c = TF * CY * max(min(64, l[2]), out[2]) * (1 if l[1][0][0] in TWO else 4)
+        rec("t", l[1] + rh[1], [out[1][0] + l[1][0][1:3]], lambda: g.tensor.matmul(out[0], l[0], rh[0], start, stop), c)
 
     def ms(out, c):
-        rec("v", [], out[1], lambda: g.vector.memset(out[0], c), vcost(out, [], 1))
+        rec("v", [], out[1], lambda: g.vector.memset(out[0], c), vcost(out, []))
 
     def iota(out, pat, base, cm, exact=False):
         if exact:
@@ -246,8 +300,10 @@ def main(g, core, T, topo, r, N):
     def asel(out, in_, pat, cmp, fill, base, cm):
         rec("g", in_[1], out[1], lambda: g.affine_select(out[0], in_[0], pat, cmp, fill, base, cm), 0.2 + 0.002 * out[2])
 
-    def remote(rd, f):
+    def remote(rd, f, sem=None):
         rec("g", rd, [], lambda: f(), 1.0)
+        if sem:
+            ops[-1][2] = [(sem, 0, 1, 0, 1, 1)]
 
     hc = helper_of(core, T, topo)
     qs = [(r + 1 + t) % N for t in range(4)]
@@ -276,7 +332,7 @@ def main(g, core, T, topo, r, N):
     iota(A("cmi"), [[0, 8], [1, 16]], 0, 0)
     iota(A("clc"), [[1, 8], [16, 32]], 0, 0)
     iota(A("cbf"), [[16, 16]], 0, 0)
-    asel(A("cid"), A("cone", 0, 128), [[-1, 128]], OP.is_equal, 0.0, 0, 1)
+    asel(A("cid"), A("cone"), [[-1, 128]], OP.is_equal, 0.0, 0, 1)
 
     def fused(pairs, rsem):
         tr = []
@@ -290,20 +346,22 @@ def main(g, core, T, topo, r, N):
     def table_out(d, rsem, engines=None):
         tot_loc[0] += send(g, T, topo, core, d, own[0], own[0], rsem, engines)
 
-    remote(dkey, lambda: fused([(d, T.D[d], T.NL[:, 32 * r:32 * r + 32]) for d in others], "nm"))
-    remote(A("HT")[1], lambda: fused([((r - 1 - t) % N, T.HT[:], T.HS[:, 4 * t:4 * t + 4]) for t in range(4)], "hs"))
+    remote(dkey, lambda: fused([(d, T.D[d], T.NL[:, 32 * r:32 * r + 32]) for d in others], "nm"), "nm")
+    remote(A("HT")[1], lambda: fused([((r - 1 - t) % N, T.HT[:], T.HS[:, 4 * t:4 * t + 4]) for t in range(4)], "hs"), "hs")
     for d in others:
-        ext(A("NL", 32 * d, 32 * d + 32)[1], "nm", N - 1, 8.0)
-    ext(A("HS")[1], "hs", 4, 9.0)
+        ext(A("NL", 32 * d, 32 * d + 32)[1], "nm", N - 1, 3.0, True)
+    ext(A("HS")[1], "hs", 4, 3.0, True)
     remote(own[1], lambda: table_out(hc, "rel", relay_engines(core, hc, topo, T)))
-    asel(A("cb1"), A("cone", 0, 128), [[-16, 8], [0, 16]], OP.is_ge, 0.0, 0, 1)
+    asel(A("cb1"), A("cone"), [[-16, 8], [0, 16]], OP.is_ge, 0.0, 0, 1)
     asel(A("cblk"), A("cb1"), [[16, 8], [0, 16]], OP.is_ge, 0.0, 15, -1)
     asel(A("cg1"), A("cone", 0, 8), [[-16, 8]], OP.is_ge, 0.0, 0, 1)
     asel(A("cg"), A("cg1"), [[16, 8]], OP.is_ge, 0.0, 15, -1)
-    iota(A("cbm0"), [[0, 8], [1, 16]], 0, 16)
-    iota(A("cohi"), [[1, 32]], 0, 0)
-    iota(A("cw0f"), [[0, 16]], 256, 1)
-    iota(A("cpc"), [[16, 3], [-256, 8]], 0, 0, True)
+    for nc in NCS:
+        asel(A("cpm_%d" % nc, 0, 16 * nc), A("cone", 0, 16 * nc), [[-1, 16], [-16, nc]], OP.is_equal, 0.0, 0, 1)
+    iota(A("cw0f"), [[0, 16]], -1024, 1)
+    iota(A("cbc"), [[4, 8]], 0, 0)
+    iota(A("cio"), [[1, 384]], 0, 0)
+    asel(A("ctf"), A("cone"), [[-1, 128]], OP.is_ge, 0.0, 0, 1)
     ts(A("NO"), A("NL"), 16.0, None, OP.add)
     win = A("TW", BLK * r, BLK * (r + 1))
     for i, d in enumerate(others + [r]):
@@ -313,60 +371,73 @@ def main(g, core, T, topo, r, N):
         else:
             act(o, a, AF.Copy)
     remote(A("FO", 0, 512 * r)[1] + A("FO", 512 * r + 512, 4096)[1],
-           lambda: fused([(d, T.FO[:, 512 * d:512 * d + 512], T.FI[:, 512 * r:512 * r + 512]) for d in others], "ft"))
+           lambda: fused([(d, T.FO[:, 512 * d:512 * d + 512], T.FI[:, 512 * r:512 * r + 512]) for d in others], "ft"), "ft")
     act(A("FI", 512 * r, 512 * r + 512), A("FO", 512 * r, 512 * r + 512), AF.Copy)
     for d in others:
-        ext(A("FI", 512 * d, 512 * d + 512)[1], "ft", N - 1, 20.0)
+        ext(A("FI", 512 * d, 512 * d + 512)[1], "ft", N - 1, 8.0, True)
     for o in (3, 5, 7):
         remote(own[1], lambda o=o: table_out(T.cores[(r - o) % N], "tbx"))
     for q in others:
         ext(A("TW", BLK * q + 16, BLK * (q + 1))[1], *(("tb0", 8, 24.0) if q == qs[0] else ("tbx", 48, 60.0)))
-    iota(A("cio"), [[1, 256]], 0, 0)
-    iota(A("ci2"), [[1, 256]], 0, 0)
-    ms(A("cth"), 14.0)
-    asel(A("cth"), A("cth"), [[0, 4], [1, 128]], OP.is_gt, 1000.0, 0, -1)
 
     ts(A("cpj"), A("cpi"), 15, None, OP.bitwise_and)
     ts(A("cpq"), A("cpj"), 1, None, OP.arith_shift_right)
     ts(A("cpt"), A("cpi"), 4, 1, OP.arith_shift_right, OP.bitwise_and)
-    copy(A("cj"), A("cpj"))
-    copy(A("cq"), A("cpq"))
-    copy(A("cpar"), A("cpt"))
-    ts(A("cn"), A("cj"), -16.0, None, OP.mult)
-    ts(A("cR"), A("cpc"), A("cn"), None, OP.add)
+    for a, b in (("cj", "cpj"), ("cq", "cpq"), ("cpar", "cpt"), ("cp", "cpi")):
+        copy(A(a), A(b))
+    for h in range(2):
+        ts(A("cbb", h, h + 1), A("cp"), 256.0 + 128 * h, None, OP.add)
     ts(A("ceb"), A("cq"), float(BLK), 15.0, OP.mult, OP.add)
     ts(A("cs"), A("cq"), 496.0, None, OP.mult)
     ts(A("clb"), A("cj"), 8.0, A("cs"), OP.mult, OP.add)
     ts(A("LC"), A("clc"), A("clb"), None, OP.add)
-    ts(A("cba"), A("cbf"), A("cj"), None, OP.add)
-    ts(A("cbai"), A("cba"), 4.0, None, OP.mult)
-    ts(A("cb2"), A("cba"), 256.0, None, OP.add)
-    for n, fill, first in (("cmh", 256.0, 0.0), ("cml", 0.0, 255.0)):
+    ts(A("cb2"), A("cbf"), A("cj"), 256.0, OP.add, OP.add)
+    for n, fill, first in (("cmh", 256.0, 0.0), ("cml", 0.0, 255.0), ("ckp", 1.0, 0.0)):
         ms(A(n), fill)
         ms(A(n, 0, 512, 16), first)
     ms(A("cm0"), 0.0)
     ms(A("cm0", 0, 128, 16), BIG)
     ms(A("HST"), 0)
-    ms(A("cnegf"), -2048.0)
-    copy(A("cneg"), A("cnegf"))
+    ms(A("IJ"), 0.0)
+    ts(A("cneg"), A("cone"), -2048.0, None, OP.mult)
     copy(A("cib"), A("cid"))
     copy(A("cih"), A("cid"))
-    copy(A("cbm"), A("cbm0"))
+    copy(A("cbm"), A("cio"))
+    ts(A("c2b"), A("cid"), 2.0, None, OP.mult)
     ts(A("cnb"), A("cid"), -1.0, None, OP.mult)
+    ts(A("cgn"), A("cg"), -1.0, None, OP.mult)
     copy(A("cblb"), A("cblk"))
-    ts(A("cgk"), A("cg"), 2048.0, None, OP.mult)
+    for n, w in (("ZA", 512.0), ("ZB", 1024.0), ("ZN", -512.0)):
+        ms(A(n), 0.0)
+        ts(A(n, 15, 143, 16), A("cg"), w, None, OP.mult)
+    for nc in NCS:
+        z = "_%d" % nc
+        copy(A("cph" + z, 0, 16 * nc), A("cpm" + z, 0, 16 * nc))
+        copy(A("cpb" + z, 0, 16 * nc), A("cpm" + z, 0, 16 * nc))
+        ts(A("cr" + z), A("cj"), 16.0 * nc, None, OP.mult)
+        ts(A("cr4" + z), A("cj"), 4.0 * nc, None, OP.mult)
+        for m in range(16 if R0 < 16 else 0):
+            ts(A("SEL" + z, 16 * nc * R0 + m, 256 * nc, 16), A("cpb" + z, nc * R0, 16 * nc), -1.0, None, OP.mult)
+    for s, (c0, c1) in enumerate(ST):
+        ts(A("cbai_%d" % s), A("cbc"), A("cr4_%d" % (c1 - c0)), 64.0 * c0, OP.add, OP.add)
     ts(A("cmk"), A("cmi"), A("cj"), None, OP.is_equal)
-    ts(A("coh"), A("cohi"), A("cj"), None, OP.is_equal)
+    ts(A("cpen"), A("cmk"), -524288.0, 524288.0, OP.mult, OP.add)
+    ms(A("coh", 384, 512), 0.0)
+    ms(A("csn", 0, 256), 1.0)
+    ms(A("csn", 256, 512), 0.0)
+    for k in range(4):
+        ts(A("ctri", 128 * k, 128 * k + 128), A("ctf"), -64.0, None, OP.mult)
+        ts(A("cth", 128 * k, 128 * k + 128), A("ctf"), 64.0, 13.5, OP.mult, OP.add)
+        if k < 3:
+            copy(A("coh", 128 * k, 128 * k + 128), A("cmk"))
     copy(A("cw0"), A("cw0f"))
     ts(A("cw1"), A("cw0f"), 128.0, None, OP.add)
     copy(A("HF"), A("HS"))
     ts(A("kd"), A("HS"), 1, None, OP.bitwise_and)
     for t in range(4):
         for i in range(2):
-            ts(A("WF", 16 * t + 8 * i, 16 * t + 8 * i + 8), A("cg"), A("HF", 4 * t + i, 4 * t + i + 1), None, OP.mult)
-        copy(A("WB", 16 * t, 16 * t + 16), A("WF", 16 * t, 16 * t + 16))
-        ts(A("WH", 16 * t, 16 * t + 16), A("WF", 16 * t, 16 * t + 16), 0.5, None, OP.mult)
-        ts(A("th", t, t + 1), A("HF", 4 * t + 3, 4 * t + 4), 2048.0, None, OP.mult)
+            ts(A("WH", 16 * t + 8 * i, 16 * t + 8 * i + 8), A("cg"), A("HF", 4 * t + i, 4 * t + i + 1), 0.5, OP.mult, OP.mult)
+        ts(A("th", t, t + 1), A("HF", 4 * t + 3, 4 * t + 4), 512.0, -1.0, OP.mult, OP.add)
         ts(A("hcol", t, t + 1), A("kd", 4 * t + 2, 4 * t + 3), -2048.0, 4196352.0, OP.mult, OP.add)
         copy(A("ZZ", 16 * t, 16 * t + 8), A("cg"))
         ts(A("ZZ", 16 * t + 8, 16 * t + 16), A("cg"), A("HF", 4 * t + 2, 4 * t + 3), None, OP.mult)
@@ -375,8 +446,10 @@ def main(g, core, T, topo, r, N):
         copy(A("KM", 128 * t, 128 * t + 128, 1, 0, 16), b)
         x = float(2 * qs[t] + t // N)
         ts(A("ntx", t, t + 1), A("cj"), x, None, OP.not_equal)
+        ts(A("DX", 128 * t, 128 * t + 128), A("cid"), A("ntx", t, t + 1), None, OP.mult)
         ts(A("XM"), A("cmi"), x, None, OP.is_equal)
         tt(A("XS", 128 * t, 128 * t + 128), A("XM"), A("cblk"), OP.mult)
+        copy(A("XB", 128 * t, 128 * t + 128), A("XS", 128 * t, 128 * t + 128))
     ts(A("P", 0, 256), A("TP"), 1.0, None, OP.add)
     ts(A("S"), A("SD"), 1.0, None, OP.add)
     for j in range(16):
@@ -391,176 +464,224 @@ def main(g, core, T, topo, r, N):
         tt(A("cc", 2 * i, 2 * i + 1), A("cc", 6, 7), A(m), OP.mult)
         tt(A("cc", 2 * i + 1, 2 * i + 2), A("cc", 7, 8), A(m), OP.mult)
 
+    one = BANKS["key"] == BANKS["hash"]
+
+    def shape(h):
+        c0, c1 = ST[h]
+        return "_%d" % h, "_%d" % (c1 - c0), c1 - c0, 16 * c0, 16 * c1, 16 * (c1 - c0), 256 * c0
+
+    def place(h, k, p1=128):
+        na = shape(h)[5]
+        if k == 4 and not one:
+            return A("B%d" % BANKS["key"][h], 384, 384 + na)
+        c = (na if one else 0) + (16 + (k - 1) * na if k else 0)
+        return A("B%d" % BANKS["hash"][h], c, c + (na if k else 16), 1, 0, p1)
+
     def middle(h, t):
-        s = "_%d" % h
+        s, z, nc, a0, a1, na, x0 = shape(h)
         if t:
-            ts(A("EO", 128 * h, 128 * h + 128), A("P", 128 * h, 128 * h + 128), A("ceb"), None, OP.add)
-        for k in range(4):
-            c, o = 512 * k, 128 * h + 32 * k
-            src = IND(A("TW"), A("EO", o, o + 32)) if t else IND(A("FI"), A("LC", o, o + 32))
-            if k in EV:
-                copy(A("FA" + s, c, c + 512), src)
+            ts(A("EO", a0, a1), A("P", a0, a1), A("ceb"), None, OP.add)
+        cut = [a0 + 2 * (na * k // (2 * len(MID))) for k in range(len(MID) + 1)]
+        for k, e in enumerate(MID):
+            o, x = cut[k:k + 2], (16 * cut[k], 16 * cut[k + 1])
+            src = IND(A("TW"), A("EO", *o)) if t else IND(A("FI"), A("LC", *o))
+            if e == "v":
+                copy(A("FA", *x), src)
             else:
-                act(A("FA" + s, c, c + 512), src, AF.Copy)
-            act(A("FB" + s, c, c + 512), A("FA" + s, c, c + 512), AF.Abs)
-            scan(A("HI" + s, c, c + 512), A("cmh"), A("FA" + s, c, c + 512), 0.0, OP.min, OP.max, 0.5)
-            scan(A("LO" + s, c, c + 512), A("cml"), A("FB" + s, c, c + 512), 255.0, OP.max, OP.min, 0.5)
-        tt(A("SE" + s), A("HI" + s, 15, 2048, 16), A("LO" + s, 15, 2048, 16), OP.add)
-        ts(A("EI" + s), A("SE" + s), 0.5, -0.25, OP.mult, OP.add)
-        copy(A("EB" + s), A("EI" + s))
-        for m in range(16):
-            if m % 8 < 5:
-                copy(A("ER" + s, m, 2048, 16), A("EB" + s))
-            else:
-                act(A("ER" + s, m, 2048, 16), A("EB" + s), AF.Copy)
-        ts(A("E2" + s, 0, KV), A("EI" + s, 0, KV), 2.0, 2047.5, OP.mult, OP.add)
-        ts(A("E2" + s, KV, 128), A("EI" + s, KV, 128), 2047.5, None, OP.add)
+                act(A("FA", *x), src, AF.Copy)
+            act(A("FB", *x), A("FA", *x), AF.Abs)
+            for c in range(x[0], x[1], 512):
+                n = min(512, x[1] - c)
+                scan(A("HI", c, c + n), A("cmh", 0, n), A("FA", c, c + n), 0.0, OP.min, OP.max)
+                scan(A("LO", c, c + n), A("cml", 0, n), A("FB", c, c + n), 255.0, OP.max, OP.min)
+        se = place(h, 3)
+        mm(se, A("cib"), A("HI", x0 + 15, x0 + 16 * na, 16), True, False)
+        mm(se, A("cib"), A("LO", x0 + 15, x0 + 16 * na, 16), False, True)
+        ts(A("C", a0, a1), se, 2047.5, None, OP.add)
+        ts(A("EB", a0, a1), A("C", a0, a1), 0.5, -1024.0, OP.mult, OP.add)
+        db = "B%d" % BANKS["diff"][h][0]
+        et, ec, e2 = A(db, 0, 128, 1, 0, na), A(db, 128, 128 + na), place(h, 4)
+        mm(et, A("EB", a0, a1), A("cib"))
+        act(A("ET" + s, 0, 128, 1, 0, na), et, AF.Copy)
+        mm(ec, A("ET" + s, 0, 128, 1, 0, na), A("cpb" + z, 0, na, 1, 0, na))
+        act(A("IJ", x0, x0 + 16 * na, 16), ec, AF.Copy)
+        for c in range(x0, x0 + na * R0, 512):
+            n = min(512, x0 + na * R0 - c)
+            scan(A("ER", c, c + n), A("ckp", 0, n), A("IJ", c, c + n), 0.0, OP.mult, OP.add)
+        mm(e2, A("c2b"), A("EB", a0, a1), True, R0 == 16)
+        b, _, _, c, c1, _ = e2[1][0]
+        for k in range(R0, 16):
+            mm(A(b, c + k, c1, 16), A("cnb"), A("EB", a0 + k, a1, 16), False, k == 15)
+        act(A("E2", a0, a1), e2, AF.Identity, bias=2047.5)
 
     def hash_(h, p, t):
-        s, b = "_%d" % h, "B%d" % (5 + h)
-        u = A(b, 0, 16)
-        if p == 0:
-            mm(u, A("EB" + s), A("WB", 16 * t, 16 * t + 16))
-        else:
-            mm(u, A("cneg"), A("WH", 16 * t, 16 * t + 16), True, False)
-            mm(u, A("C" + s), A("WH", 16 * t, 16 * t + 16), False, True)
-        copy(A("UI" + s), u)
-        ts(A("UA" + s), A("UI" + s), 4095, None, OP.bitwise_and)
-        tt(A("VP" + s), A("UA" + s, 0, 8), A("UA" + s, 8, 16), OP.mult)
-        ts(A("UA" + s, 0, 8), A("VP" + s), 5, 4095, OP.arith_shift_right, OP.bitwise_and)
-        ts(A("HB" + s), A("UA" + s), -2048.0, None, OP.add)
-        x, y = A(b, 16, 144, 1, 0, 16), A("HX" + s, 0, 128, 1, 0, 16)
-        mm(x, A("HB" + s), A("cih"))
+        s, z, nc, a0, a1, na, x0 = shape(h)
+        u = place(h, 0, na)
+        mm(u, A("cneg", 0, na), A("WH", 16 * t, 16 * t + 16), True, False)
+        mm(u, A("C", a0, a1), A("WH", 16 * t, 16 * t + 16), False, True)
+
+        def part(n, c0=0, c1=16):
+            return A(n + s, c0, c1, 1, 0, na)
+        copy(part("UI"), u)
+        ts(part("UA"), part("UI"), 4095, None, OP.bitwise_and)
+        tt(part("VP", 0, 8), part("UA", 0, 8), part("UA", 8, 16), OP.mult)
+        ts(part("UA", 0, 8), part("VP", 0, 8), 5, 4095, OP.arith_shift_right, OP.bitwise_and)
+        ts(part("HB"), part("UA"), -2048.0, None, OP.add)
+        x, y, hh = place(h, 1, 16), A("HX", a0, a1, 1, 0, 16), place(h, 2)
+        mm(x, part("HB"), A("cph" + z, 0, na, 1, 0, na))
         copy(y, x)
-        hh = A(b, 144, 272)
         mm(hh, A("KM", 128 * t, 128 * t + 128, 1, 0, 16), y)
-        ts(A("HN" + s), hh, A("hcol", t, t + 1), None, OP.add)
-        d = A("HST", 512 * h + p, 512 * h + 512, 4)
-        ts(d, A("HN" + s), 4095, None, OP.bitwise_and)
-        copy(A("OF" + s), d)
+        ts(A("HN", a0, a1), hh, A("hcol", t, t + 1), None, OP.add)
+        d = A("HST", 4 * a0 + p, 4 * a1, 4)
+        ts(d, A("HN", a0, a1), 4095, None, OP.bitwise_and)
+        copy(A("OF", a0, a1), d)
 
-    def look(h, t):
-        s, kb = "_%d" % h, "B%d" % (3 + h)
+    def look(h, p, t):
+        s, z, nc, a0, a1, na, x0 = shape(h)
+        key = A("B%d" % BANKS["key"][h], 0, na)
         w = A("TW", BLK * qs[t] + 16, BLK * qs[t] + BLK)
-        mm(A(kb, 0, 128), A("cih"), A("cbm"), True, False)
-        for c in range(0, KV, KC):
-            x = (16 * c, 16 * min(KV, c + KC))
-            tt(A("XV" + s, *x), IND(w, A("OF" + s, c, min(KV, c + KC))), A("ER" + s, *x), OP.subtract)
-            act(A("AX" + s, *x), A("XV" + s, *x), AF.Abs)
-        for i, c in enumerate(range(16 * KV, 2048, 512)):
-            n = min(512, 2048 - c)
-            b = A("B%d" % i, 0, n)
-            act(A("XV" + s, c, c + n), IND(w, A("OF" + s, c // 16, (c + n) // 16)), AF.Copy)
-            mm(b, A("cnb"), A("ER" + s, c, c + n), True, False)
-            mm(b, A("cib"), A("XV" + s, c, c + n), False, True)
-            act(A("AX" + s, c, c + n), b, AF.Abs)
-        for m in range(16):
-            mm(A(kb, m, 128, 16), A("AX" + s, m, 2048, 16), A("cgk"), False, m == 15)
+        mm(key, A("cih"), A("cbm", 128 * p, 128 * p + na), True, False)
+        nd = 0
+        for i, (how, r0, r1) in enumerate(LOOK):
+            x = (x0 + na * r0, x0 + na * r1)
+            xv, ax, src = A("XV", *x), A("AX", *x), IND(w, A("OF", a0 + nc * r0, a0 + nc * r1))
+            if how == "d":
+                b = A("B%d" % BANKS["diff"][h][nd % len(BANKS["diff"][h])], 0, x[1] - x[0])
+                nd += 1
+                act(xv, src, AF.Copy)
+                mm(b, A("ET" + s, 0, 128, 1, 0, na), A("SEL" + z, na * r0, na * r1, 1, 0, na), True, False)
+                mm(b, A("cib"), xv, False, True)
+                act(ax, b, AF.Abs)
+            else:
+                for k in range(r0, r1, VSUB):
+                    e = min(r1, k + VSUB)
+                    y = (x0 + na * k, x0 + na * e)
+                    tt(A("XV", *y), IND(w, A("OF", a0 + nc * k, a0 + nc * e)), A("ER", *y), OP.subtract)
+                if how == "a":
+                    ts(ax, xv, 0.0, None, OP.max)
+                else:
+                    act(ax, xv, AF.Abs)
+            for k in range(r0, r1):
+                last, c = i == len(LOOK) - 1 and k == r1 - 1, x0 + na * k
+                if how == "a":
+                    mm(key, A("ZN", 15 - k, 143 - k), A("XV", c, c + na), False, False)
+                mm(key, A("ZB" if how == "a" else "ZA", 15 - k, 143 - k), A("AX", c, c + na), False, last)
 
-    def winner(h, p):
-        s = "_%d" % h
-        scan(A("SC" + s), A("cm0"), A("B%d" % (3 + h), 0, 128), BIG, OP.max, OP.min)
-        for k in range(8):
-            ts(A("LT" + s, 16 * k, 16 * k + 16), A("cmk", 0, 16), A("SC" + s, 16 * k + 15, 16 * k + 16), None, OP.mult)
-        sp = A("B%d" % (5 + h), 280, 288)
-        mm(sp, A("LT" + s), A("cg"), f32=True)
+    def winner(h, p, t):
+        s, z, nc, a0, a1, na, x0 = shape(h)
+        scan(A("SC", a0, a1), A("cm0", 0, na), A("B%d" % BANKS["key"][h], 0, na), BIG, OP.max, OP.min)
         if p < 2:
-            copy(A("KI" + s), sp)
-            ts(A("J" + s), A("KI" + s), 2047, None, OP.bitwise_and)
-            copy(A("JU" + s, 0, 8), A("J" + s))
-            tt(A("C" + s), IND(A("XV" + s), A("JU" + s, 0, 8)), A("E2" + s), OP.add)
-        tt(A("R" + s, 8 * p, 8 * p + 8), sp, A("cR", 8 * p, 8 * p + 8), OP.add)
+            k = A("KI" + s, 8 * p, 8 * p + nc)
+            copy(k, A("SC", a0 + 15, a1, 16))
+            ts(A("J" + s, 0, nc), k, 127, None, OP.bitwise_and)
+            ts(A("JU" + s, 0, nc), A("J" + s, 0, nc), A("cr" + z), None, OP.add)
+            tt(A("C", a0, a1), IND(A("XV", x0, x0 + 16 * na), A("JU" + s, 0, nc)), A("E2", a0, a1), OP.add)
+        if p == 1:
+            tt(A("BA" + s, 0, nc), A("KI" + s, 0, nc), A("KI" + s, 8, 8 + nc), OP.min)
+            ts(A("BB" + s, 0, nc), A("BA" + s, 0, nc), A("th", t, t + 1), None, OP.min)
+
+    psb, psc = "B%d" % BANKS["ps"][0], BANKS["ps"][1]
 
     def names(h, t):
-        s, c0, c1 = "_%d" % h, 128 * h, 128 * h + 128
-        tt(A("BA" + s), A("R" + s, 0, 8), A("R" + s, 8, 16), OP.min)
-        tt(A("BK" + s), A("BA" + s), A("R" + s, 16, 24), OP.min)
-        ts(A("PI" + s), A("BK" + s), 4, 3, OP.arith_shift_right, OP.bitwise_and)
-        ts(A("MI" + s), A("BK" + s), 15, None, OP.bitwise_and)
-        ts(A("VAL" + s), A("BK" + s), A("th", t, t + 1), None, OP.is_lt)
-        tt(A("L1" + s), A("PI" + s), A("cbai", 8 * h, 8 * h + 8), OP.add)
-        ts(A("M1" + s), A("MI" + s), -16.0, None, OP.add)
-        copy(A("L1U" + s), A("L1" + s))
-        tt(A("M2" + s), A("M1" + s), A("VAL" + s), OP.mult)
-        ts(A("L2U" + s), A("M2" + s), 16.0, None, OP.add)
-        ts(A("GG" + s), IND(A("HST"), A("L1U" + s)), 1.0, 1.0, OP.mult, OP.add)
-        tt(A("PR" + s), IND(A("coh"), A("L2U" + s)), A("GG" + s), OP.mult)
-        nrep, nx = A("B7", c0, c1), A("B7", 256 + c0, 256 + c1)
-        mm(nrep, A("cblk"), A("PR" + s), f32=True)
-        mm(nx, A("XS", 128 * t, 128 * t + 128), A("PR" + s), f32=True)
-        ts(A("I1" + s), nrep, A("csc"), None, OP.mult)
-        ts(A("I2" + s), A("I1" + s), 4096, None, OP.bitwise_and)
-        ts(A("BE", c0, c1), A("I2" + s), A("cc", 0, 1), A("cc", 1, 2), OP.mult, OP.add)
-        ts(A("BO", c0, c1), A("I2" + s), A("cc", 2, 3), A("cc", 3, 4), OP.mult, OP.add)
-        tt(A("B3", 128 + c0, 128 + c1), nx, A("PK" + s), OP.add)
-        copy(A("P", c0, c1), A("B3", 128 + c0, 128 + c1))
+        s, z, nc, a0, a1, na, x0 = shape(h)
 
-    def pairs(t):
-        ps = A("B3", 128, 384)
-        for banks, a0, b0, out in (((0, 1), 0, 0, "QA"), ((2, 4), 0, 128, "QX"), ((5, 6), 128, 128, "QB")):
-            for k in (0, 1, 4, 5, 2, 3, 6, 7):
-                src, p0 = "BE" if k % 2 == 0 else "BO", 32 * (k // 2)
-                mm(A("B%d" % banks[k // 4], 128 * (k % 4), 128 * (k % 4) + 128), A(src, a0, a0 + 128, 1, p0, p0 + 32), A(src, b0, b0 + 128, 1, p0, p0 + 32))
+        def part(n):
+            return A(n + s, 0, nc)
+        tt(part("BK"), A("SC", a0 + 15, a1, 16), part("BB"), OP.min)
+        ts(part("MI"), part("BK"), 511, None, OP.bitwise_and)
+        ts(part("PI"), part("BK"), 7, 3, OP.arith_shift_right, OP.bitwise_and)
+        copy(part("L2U"), part("MI"))
+        tt(part("L1"), part("PI"), part("cbai"), OP.add)
+        act(A("OH", a0, a1), IND(A("coh"), part("L2U")), AF.Copy)
+        copy(part("L1U"), part("L1"))
+        tt(A("PR", a0, a1), IND(A("HST"), part("L1U")), A("OH", a0, a1), OP.mult)
+        nrep, ps = place(h, 3), A(psb, psc + a0, psc + a1)
+        mm(nrep, A("cblb"), A("OH", a0, a1), True, False)
+        mm(nrep, A("cblk"), A("PR", a0, a1), False, True)
+        mm(ps, A("DX", 128 * t, 128 * t + 128), A("P", a0, a1), True, False)
+        mm(ps, A("XB", 128 * t, 128 * t + 128), A("OH", a0, a1), False, False)
+        mm(ps, A("XS", 128 * t, 128 * t + 128), A("PR", a0, a1), False, True)
+        ts(A("I1", a0, a1), nrep, A("csc"), None, OP.mult)
+        ts(A("I2", a0, a1), A("I1", a0, a1), 4096, None, OP.bitwise_and)
+        ts(A("BE", a0, a1), A("I2", a0, a1), A("cc", 0, 1), A("cc", 1, 2), OP.mult, OP.add)
+        ts(A("BO", a0, a1), A("I2", a0, a1), A("cc", 2, 3), A("cc", 3, 4), OP.mult, OP.add)
+        act(A("P", a0, a1), ps, AF.Copy)
+        act(A("P", 256 + a0, 256 + a1), ps, AF.Copy)
+
+    def same(out, a0, b0, onv):
+        banks, tri = BANKS[out], a0 == b0 and not onv
+        if tri:
             for i in range(2):
-                o, b = A(out, 512 * i, 512 * i + 512), A("B%d" % banks[i])
-                if out == "QX":
-                    act(o, b, AF.Relu, bias=-13.0)
-                else:
-                    tt(o, b, A("cth"), OP.is_ge)
+                mm(A("B%d" % banks[i]), A("cib"), A("ctri"), True, False)
+        for k in (0, 1, 4, 5, 2, 3, 6, 7):
+            src, p0 = "BE" if k % 2 == 0 else "BO", 32 * (k // 2)
+            mm(A("B%d" % banks[k // 4], 128 * (k % 4), 128 * (k % 4) + 128), A(src, a0, a0 + 128, 1, p0, p0 + 32), A(src, b0, b0 + 128, 1, p0, p0 + 32),
+               not tri, not tri or k % 4 == 3)
+        for i in range(2):
+            o, b = A(out, 512 * i, 512 * i + 512), A("B%d" % banks[i])
+            if onv:
+                tt(o, b, A("cth"), OP.is_ge)
+            else:
+                act(o, b, AF.Relu, bias=-13.0)
+
+    def lower(h):
+        bank, x = "B%d" % BANKS["low"][h], (128 * h, 128 * h + 128)
+        mm(A(bank, 0, 128), A("cib"), A("cpen"), True, False)
         for k in range(8):
-            mm(A("B7", 16 * k, 16 * k + 16), A("QA", 128 * k, 128 * k + 128), A("cw0"))
-        for k in range(8):
-            o = A("B4", 16 * k, 16 * k + 16)
-            mm(o, A("QX", 128 * k, 128 * k + 128), A("cw0"), True, False)
-            mm(o, A("QB", 128 * k, 128 * k + 128), A("cw1"), False, True)
-        for h, b in ((0, "B7"), (1, "B4")):
-            tt(A("LT_%d" % h), A(b, 0, 128), A("cmk"), OP.mult)
+            o = A(bank, 16 * k, 16 * k + 16)
+            mm(o, A("QX" if h else "QA", 128 * k, 128 * k + 128), A("cw0"), False, k == 7 and not h)
+            if h:
+                mm(o, A("QB", 128 * k, 128 * k + 128), A("cw1"), False, k == 7)
+        act(A("LA", *x), A(bank, 0, 128), AF.Abs, bias=1024.0)
+        act(A("LT", *x), A("LA", *x), AF.Relu, bias=A("cbb", h, h + 1), scale=-1.0)
+
+    def pairs():
+        ps, lb = A(psb, psc, psc + 256), "B%d" % BANKS["low"][0]
+        same("QX", 0, 128, False)
+        same("QB", 128, 128, True)
+        lower(1)
+        mm(A(lb, 128, 144), A("cid"), A("cb2"), True, False)
         for h in range(2):
-            mm(A("B0", 8 * h, 8 * h + 8), A("LT_%d" % h), A("cg"), f32=True)
-        v = A("B0", 0, 16)
-        ts(A("Y1"), v, 256.0, None, OP.is_ge)
-        ts(A("Y2"), v, 512.0, None, OP.is_lt)
-        tt(A("DD"), v, A("cb2"), OP.subtract)
-        tt(A("SEC"), A("Y1"), A("Y2"), OP.mult)
-        tt(A("DS"), A("DD"), A("SEC"), OP.mult)
-        tt(A("LF"), A("DS"), A("cba"), OP.add)
-        copy(A("LU"), A("LF"))
-        ts(A("EE"), A("SEC"), -256.0, 256.0, OP.mult, OP.add)
-        tt(A("LSF"), A("LF"), A("EE"), OP.add)
-        copy(A("LSU"), A("LSF"))
-        copy(A("Q"), IND(A("P", 0, 256), A("LU")))
-        ne, cn, pn, nc = A("B2", 0, 256), A("B1", 0, 256), A("B6", 0, 256), A("B5", 0, 256)
+            mm(A(lb, 128 + 8 * h, 136 + 8 * h), A("LT", 128 * h, 128 * h + 128), A("cgn"), False, h == 1)
+        tt(A("SP"), A("S"), ps, OP.subtract)
+        copy(A("LSU"), A(lb, 128, 144))
+        copy(A("Q"), IND(A("P"), A("LSU")))
+        act(A("SN"), IND(A("csn"), A("LSU")), AF.Copy)
+        ne, cn, pn, nd, nc = (A("B%d" % b, 0, 256) for b in BANKS["rest"])
         tt(ne, ps, A("Q"), OP.not_equal)
         tt(A("MN"), ps, A("Q"), OP.min)
-        tt(A("SP"), A("S"), ps, OP.subtract)
-        tt(A("QN"), ne, A("MN"), OP.mult)
-        ts(A("ND"), A("QN"), 0.0, None, OP.is_le)
-        mm(cn, A("cblb"), A("ND"))
-        tt(A("SN"), IND(A("cio"), A("LU")), A("ci2"), OP.not_equal)
-        tt(A("SPS"), A("SP"), A("SN"), OP.mult)
+        tt(A("TT"), ne, A("MN"), OP.mult)
+        ts(A("ND"), A("TT"), 0.0, None, OP.is_le)
+        mm(cn, A("cib"), A("SN"), True, False)
+        mm(cn, A("cblb"), A("ND"), False, True)
+        mm(nd, A("cib"), A("ND"))
+        act(nc, cn, AF.Relu, bias=-16.0)
         tt(pn, ps, A("ND"), OP.mult)
-        tt(A("QN"), A("Q"), A("ND"), OP.mult)
-        ts(nc, cn, 15.5, None, OP.is_ge)
-        tt(A("SX"), A("SPS"), nc, OP.mult)
+        tt(A("QN"), nd, A("Q"), OP.mult)
         tt(A("PC"), A("P", 0, 256), nc, OP.mult)
-        tt(A("P", 0, 256), A("SX"), pn, OP.add)
+        tt(A("SX"), A("SP"), nc, OP.mult)
+        tt(A("P", 0, 256), pn, A("SX"), OP.add)
         tt(IND(A("P"), A("LSU")), A("QN"), A("PC"), OP.max)
 
     for t in range(4):
-        for h in range(2):
+        for h in range(len(ST)):
+            lead[0] = len(ST) - 1 - h
             middle(h, t)
             hash_(h, 0, t)
-            ts(A("PK_%d" % h), A("P", 128 * h, 128 * h + 128), A("ntx", t, t + 1), None, OP.mult)
-            look(h, t)
+            look(h, 0, t)
         for p in range(3):
-            for h in range(2):
-                winner(h, p)
+            for h in range(len(ST)):
+                lead[0] = len(ST) - 1 - h
+                winner(h, p, t)
                 if p < 2:
                     hash_(h, p + 1, t)
-                    look(h, t)
+                    look(h, p + 1, t)
                 else:
                     names(h, t)
-        pairs(t)
+                    if ST[h][0] < 8 <= ST[h][1]:
+                        same("QA", 0, 0, False)
+                        lower(0)
+        pairs()
     ts(A("YO"), A("P", 0, 256), -1.0, None, OP.add)
 
     for o in schedule(ops):

@@ -2,19 +2,19 @@ from concourse.bass import DstId, RemoteDMATransfer
 from concourse.mybir import AluOpType as OP, AxisListType, ActivationFunctionType as AF
 
 BLK = 4112
-ST = ((0, 6), (6, 11), (11, 16))
-LOOK = (("b", 0, 4), ("d", 8, 12), ("b", 4, 8), ("d", 12, 16))
-R0 = max(x[2] for x in LOOK if x[0] != "d")
+NS, NC, NA = 4, 4, 64
+LOOK = (("v", 0, 4), ("s", 8, 12), ("v", 4, 8), ("s", 12, 16))
+R0 = max(x[2] for x in LOOK if x[0] == "v")
 VSUB = 2
-MID = "svs"
-BANKS = {2: dict(key=(3, 4), hash=(5, 6), diff=((0, 1), (2, 7)), ps=(3, 128), QA=(0, 1), QX=(2, 7), QB=(5, 6), low=(0, 1), rest=(2, 1, 6, 7, 4)),
-         3: dict(key=(0, 1, 2), hash=(0, 1, 2), diff=((3, 7), (4, 7), (5, 7)), ps=(6, 0), QA=(3, 4), QX=(0, 1), QB=(5, 7), low=(3, 4), rest=(0, 1, 5, 7, 2)),
-         4: dict(key=(0, 1, 2, 3), hash=(0, 1, 2, 3), diff=((4,), (5,), (6,), (7,)), ps=(7, 256), QA=(4, 5), QX=(0, 1), QB=(2, 6), low=(4, 5), rest=(0, 1, 2, 6, 3))}[len(ST)]
+MID = ("vs", "sv", "ss", "sv")
+PARTS = ((0, 16), (16, 32))
+SAME = (((4, 5),), ((4, 5), (6, 7)))
 BIG = 16777216.0
-LAT, CY, GA, TF = 0.2, 0.00104, 1.56, 0.7
-SKEW, BONUS, SMALL, AHEAD, ROUNDS = 2.0, 10.0, 0.22, 0.3, 4
+LAT, CY, GA, TF, SMALL, ROUNDS = 0.2, 0.001, 1.56, 0.65, 0.22, 2
+TRIES = [(1.0 + 0.1 * a, b) for a in range(10) for b in (2.0, 3.0, 4.0, 6.0)]
+CASES = ((0.2, 0.2, 0.8), (0.06, 0.3, 0.8), (0.2, 0.2, 1.3))
+CHOSEN = []
 F32, BF, I32, U16, F16 = "float32", "bfloat16", "int32", "uint16", "float16"
-NCS = sorted(set(b - a for a, b in ST))
 
 SCRATCH = {"TW": ("sbuf", [128, 8 * BLK], BF), "D": ("dram", [8, 128, 32], I32)}
 WIDTH, PLACE, TWO, _used = {"TW": 8 * BLK, "D": 1}, {}, {"TW", "FO", "FI"}, {}
@@ -23,19 +23,19 @@ for _n, _w, _d in (("NL", 256, I32), ("HT", 4, I32), ("HS", 16, I32), ("FO", 409
 for _k in range(8):
     SCRATCH["B%d" % _k], WIDTH["B%d" % _k] = ("psum", [128, 512], F32), 512
 SPEC = ((BF, 1, "ET 128"), (F16, 1, "HB 16"), (U16, 1, "JU 8 L1U 8 L2U 8"), (I32, 1, "UI 16 UA 16 VP 8 KI 16 J 8 BA 8 BB 8 BK 8 PI 8 L1 8 MI 8 cbai 8"),
-        (F32, 2, "cpm 128 cr 1 cr4 1"), (BF, 2, "cpb 128 SEL 2048"), (F16, 2, "cph 128"),
-        (F32, 0, "E2 256 SC 256 PR 256 LA 256 LT 256 Q 256 QN 256 SX 256 SP 256 PC 256 S 256 HF 16 cone 128 cid 128 cb1 128 cblk 128 cg1 8 cg 8 cgn 8 cmi 128 cmk 128 "
-                 "cm0 128 cj 1 cq 1 cs 1 cp 1 cbb 2 cpar 1 cnpar 1 ceb 1 clb 1 cb2 16 cbf 16 cbc 8 clc 256 ctf 128 cw0f 16 cbt 16 csc 1 cc 8 "
-                 "ntx 4 XM 128 XS 512 DX 512 th 4 hcol 4 cio 384 cth 512"),
+        (F32, 0, "E2 256 SC 256 PR 256 LA 256 LT 256 Q 256 QN 256 SX 256 PN 256 SP 256 PW 512 PC 256 S 256 HF 16 cone 128 cid 128 cb1 128 cblk 128 "
+                 "cg1 8 cg 8 cmi 128 cmk 128 cm0 128 cj 1 cq 1 cs 4 cp 1 cbb 2 cpar 1 cnpar 1 ceb 1 clb 4 cb2 16 cbf 16 cbc 8 clc 256 ctf 128 cw0f 16 "
+                 "cbt 16 csc 1 cc 8 ntx 4 XM 128 XS 512 DX 512 th 4 hcol 4 cio 384 cth 512 cpm 64 cr 1 cr4 1"),
         (I32, 0, "HST 1024 HN 256 I1 256 I2 256 cpi 1 cpj 1 cpq 1 cpt 1 kd 16"),
-        (BF, 0, "FA 4096 FB 4096 HI 4096 LO 4096 IJ 4096 ER 4096 XV 4096 AX 4096 EB 256 OH 256 BE 256 BO 256 QA 1024 QX 1024 QB 1024 ND 256 MN 256 TT 256 SN 256 "
-                "cib 128 c2b 128 cnb 128 cblb 128 cmh 512 cml 512 ckp 512 ctri 512 cpen 128 csn 512 coh 512 XB 512 ZA 144 ZB 144 ZN 144"),
-        (U16, 0, "NO 256 EO 256 LC 256 OF 256 LSU 16"), (F16, 0, "C 256 HX 256 cw0 16 cw1 16 cneg 128 cih 128 cbm 384 WH 64 ZZ 64 KM 512"))
+        (BF, 0, "FA 4096 FB 4096 HI 4096 LO 4096 IJ 4096 ER 4096 XV 4096 AX 4096 EB 256 OH 256 BE 256 BO 256 QA 1024 QX 1024 QB 1024 ND 256 MN 256 "
+                "TT 256 SN 256 c8i 128 c8b 128 n8i 128 n8b 128 ck 256 cib 128 c2b 128 cnb 128 cblb 128 cmh 512 cml 512 ckp 512 ctri 512 cpen 128 "
+                "csn 512 coh 512 XB 512 ZA 144 cpb 64 SEL 1024"),
+        (U16, 0, "NO 256 EO 256 LC 256 OF 256 LSU 16"), (F16, 0, "C 256 HX 256 cw0 16 cw1 16 cneg 128 cih 128 cbm 384 WH 64 ZZ 64 KM 512 cph 64"))
 ARENA = {F32: "af", BF: "ab", I32: "ai", U16: "au", F16: "ah"}
 for _d, _each, _s in SPEC:
     _it = _s.split()
     for _n, _w in zip(_it[::2], _it[1::2]):
-        for _t in ([""], ["_%d" % _k for _k in range(len(ST))], ["_%d" % _k for _k in NCS])[_each]:
+        for _t in (["_%d" % _k for _k in range(NS)] if _each else [""]):
             _a, _step = ARENA[_d], 16 if _d in (F32, I32) else 32
             PLACE[_n + _t], WIDTH[_n + _t] = (_a, _used.get(_a, 0)), int(_w)
             _used[_a] = _used.get(_a, 0) - (-int(_w) // _step) * _step
@@ -43,7 +43,7 @@ for _d, _each, _s in SPEC:
                 TWO.add(_n + _t)
 for _d in ARENA:
     SCRATCH[ARENA[_d]] = ("sbuf", [128, _used[ARENA[_d]]], _d)
-SEMAPHORES = ["qv", "qs", "qt", "qg", "stg", "dtz", "dhw", "dtp", "dsd", "dnl", "dyp", "nm", "hs", "ft", "tb0", "tbx", "rel", "loc"]
+SEMAPHORES = ["qv", "qs", "qt", "qg", "stg", "dt0", "dt1", "dhw", "dtp", "dsd", "dnl", "dyp", "nm", "hs", "ft0", "ft1", "tb0", "tbx", "rel0", "rel1", "loc"]
 
 
 def helper_of(rc, T, topo):
@@ -78,10 +78,13 @@ def rank_program(g, core, T, topo):
     for s in range(N):
         if helper_of(T.cores[s], T, topo) == core:
             blk = T.TW[:, BLK * s + 16:BLK * (s + 1)]
-            g.wait_ge(T.sem.rel, len(relay_engines(T.cores[s], core, topo, T)))
             tot = 0
-            for o in (1, 2, 4, 6):
-                tot += send(g, T, topo, core, T.cores[(s - o) % N], blk, blk, "tb0" if o == 1 else "tbx")
+            for i in range(2):
+                half = T.TW[:, BLK * s + 16 + 2048 * i:BLK * s + 2064 + 2048 * i]
+                g.wait_ge(T.sem["rel%d" % i], len(relay_engines(T.cores[s], core, topo, T)))
+                tot += send(g, T, topo, core, T.cores[(s - 1) % N], half, half, "tb0")
+            for o in (2, 4, 6):
+                tot += send(g, T, topo, core, T.cores[(s - o) % N], blk, blk, "tbx")
             g.wait_ge(T.sem.loc, tot)
 
 
@@ -123,7 +126,9 @@ def schedule(ops):
     queue, cost = [o[0] for o in ops], [o[4] for o in ops]
 
     def lat(i, k):
-        return 0.0 if queue[k] == "t" == queue[i] or "x" in (queue[i], queue[k]) else LAT
+        if queue[k] == "t" == queue[i]:
+            return LAT if ops[i][2][0][6:] != ops[k][2][0][6:] else 0.0
+        return 0.0 if "x" in (queue[i], queue[k]) else LAT
 
     def pack(turns, before, earliest):
         start, fin, busy = [0.0] * n, [0.0] * n, {}
@@ -147,36 +152,44 @@ def schedule(ops):
 
     prio = [0.0] * n
     for i in range(n - 1, -1, -1):
-        prio[i] = cost[i] + max([prio[j] + LAT for j in succs[i]] + [0.0])
-    prio = [p + SKEW * o[6] + BONUS * (o[4] < SMALL) for p, o in zip(prio, ops)]
-    left = [len(p) for p in preds]
-    start, fin, free, turns = [0.0] * n, [0.0] * n, {}, []
-    ready = {i: ops[i][5] for i in range(n) if not left[i]}
-    while ready:
-        t0, _, i = min((max(ready[i], free.get(queue[i], 0.0)), -prio[i], i) for i in ready)
-        q = queue[i]
-        if q != "x":
-            soon = [j for j in ready if queue[j] == q and prio[j] > prio[i] and ready[j] < t0 + AHEAD * cost[i]]
-            if soon:
-                i = max(soon, key=lambda j: prio[j])
-                t0 = max(t0, ready[i])
-        del ready[i]
-        turns.append(i)
-        start[i], fin[i] = t0, t0 + cost[i]
-        if q != "x":
-            free[q] = fin[i]
-        for j in succs[i]:
-            left[j] -= 1
-            if not left[j]:
-                ready[j] = max([ops[j][5]] + [fin[k] + lat(j, k) for k in preds[j]])
-    first, none, best = [o[5] for o in ops], [0.0] * n, (max(fin), start)
-    for _ in range(ROUNDS):
-        start, fin = pack(turns, preds, first)
-        if max(fin) < best[0]:
-            best = (max(fin), start)
-        start, fin = pack(sorted(range(n), key=lambda i: (-fin[i], -start[i], -i)), succs, none)
-        turns = sorted(range(n), key=lambda i: (-fin[i], -start[i], i))
-    return [ops[i] for i in sorted(range(n), key=lambda i: (best[1][i], i))]
+        prio[i] = cost[i] + max([prio[j] + lat(i, j) for j in succs[i]] + [0.0])
+    first, none = [o[5] for o in ops], [0.0] * n
+
+    def attempt(skew, bonus):
+        urge = [p + skew * o[6] + bonus * (o[4] < SMALL) for p, o in zip(prio, ops)]
+        left = [len(p) for p in preds]
+        start, fin, free = [0.0] * n, [0.0] * n, {}
+        ready = {i: first[i] for i in range(n) if not left[i]}
+        while ready:
+            t0, _, i = min((max(ready[i], free.get(queue[i], 0.0)), -urge[i], i) for i in ready)
+            del ready[i]
+            start[i], fin[i] = t0, t0 + cost[i]
+            if queue[i] != "x":
+                free[queue[i]] = fin[i]
+            for j in succs[i]:
+                left[j] -= 1
+                if not left[j]:
+                    ready[j] = max([first[j]] + [fin[k] + lat(j, k) for k in preds[j]])
+        best = (max(fin), start)
+        for _ in range(ROUNDS):
+            start, fin = pack(sorted(range(n), key=lambda i: (-fin[i], -start[i], -i)), succs, none)
+            start, fin = pack(sorted(range(n), key=lambda i: (-fin[i], -start[i], i)), preds, first)
+            best = min(best, (max(fin), start))
+        return sorted(range(n), key=lambda i: (best[1][i], i))
+
+    def length(turns, own, other, tensor):
+        fin, free = [0.0] * n, {}
+        for i in turns:
+            q = queue[i]
+            t = max([first[i], free.get(q, 0.0)] + [fin[k] + (lat(i, k) and (own if queue[k] == q else other)) for k in preds[i]])
+            fin[i] = t + cost[i] * (tensor if q == "t" else 1.0)
+            if q != "x":
+                free[q] = fin[i]
+        return max(fin)
+
+    if not CHOSEN:
+        CHOSEN.append(min(TRIES, key=lambda x: sum(length(t, *c) for t in [attempt(*x)] for c in CASES)))
+    return [ops[i] for i in attempt(*CHOSEN[0])]
 
 
 def main(g, core, T, topo, r, N):
@@ -246,6 +259,9 @@ def main(g, core, T, topo, r, N):
         b, o = PLACE.get(n, (n, 0))
         return (T[b][p0:p1, o + c0:o + c1] if st == 1 else T[b][p0:p1, o + c0:o + c1:st], [(n, p0, p1, c0, c1, st)], -(-(c1 - c0) // st))
 
+    def B(k, c0=0, c1=512, st=1, p1=128):
+        return A("B%d" % k, c0, c1, st, 0, p1)
+
     def IND(w, o):
         return (w[0].indirect(o[0]), w[1] + o[1], 16 * o[2], True)
 
@@ -310,19 +326,22 @@ def main(g, core, T, topo, r, N):
     others = [d for d in range(N) if d != r]
     dkey = [("D", 0, 128, 0, 1, 1)]
     own = A("TW", BLK * r + 16, BLK * (r + 1))
+    halves = [A("TW", BLK * r + 16 + 2048 * i, BLK * r + 2064 + 2048 * i) for i in range(2)]
     tot_loc = [0]
 
     for k in range(8):
-        (g.sync if k % 2 == 0 else g.scalar).dma_start(T.D[:, 16 * k:16 * k + 16, :], T.tp[16 * k:16 * k + 16, :]).then_inc(T.sem.stg, 16)
+        for i, (y0, y1) in enumerate(PARTS):
+            (g.sync if (k + i) % 2 == 0 else g.scalar).dma_start(T.D[:, 16 * k:16 * k + 16, y0:y1], T.tp[16 * k:16 * k + 16, 8 * y0:8 * y1]).then_inc(T.sem.stg, 16)
+    g.sync.dma_start(halves[0][0], T.tz[:, 0:2048]).then_inc(T.sem.dt0, 16)
+    g.scalar.dma_start(halves[1][0], T.tz[:, 2048:4096]).then_inc(T.sem.dt1, 16)
     g.scalar.dma_start(T.HT[:, 0:3], T.hw[:]).then_inc(T.sem.dhw, 16)
     g.scalar.dma_start(T.HT[:, 3:4], T.th[:]).then_inc(T.sem.dhw, 16)
-    g.sync.dma_start(own[0], T.tz[:]).then_inc(T.sem.dtz, 16)
-    g.scalar.dma_start(T.TP[:], T.tp[:]).then_inc(T.sem.dtp, 16)
-    g.scalar.dma_start(T.SD[:], T.sd[:]).then_inc(T.sem.dsd, 16)
-    need("y", "stg", 128)
+    need("y", "stg", 128 * len(PARTS))
     g.sync.dma_start(T.NL[:, 32 * r:32 * r + 32], T.D[r]).then_inc(T.sem.dnl, 16)
-    for k, sem, val, when in ((dkey, "stg", 128, 4.0), (A("HT")[1], "dhw", 32, 3.0), (own[1], "dtz", 16, 7.0), (A("TP")[1], "dtp", 16, 5.0),
-                              (A("SD")[1], "dsd", 16, 6.0), (A("NL", 32 * r, 32 * r + 32)[1], "dnl", 16, 7.0)):
+    g.sync.dma_start(T.TP[:], T.tp[:]).then_inc(T.sem.dtp, 16)
+    g.sync.dma_start(T.SD[:], T.sd[:]).then_inc(T.sem.dsd, 16)
+    for k, sem, val, when in ((dkey, "stg", 128 * len(PARTS), 4.0), (A("HT")[1], "dhw", 32, 4.0), (halves[0][1], "dt0", 16, 5.0), (halves[1][1], "dt1", 16, 6.5),
+                              (A("TP")[1], "dtp", 16, 8.0), (A("SD")[1], "dsd", 16, 8.0), (A("NL", 32 * r, 32 * r + 32)[1], "dnl", 16, 7.0)):
         ext(k, sem, val, when)
 
     for q in range(N):
@@ -330,9 +349,10 @@ def main(g, core, T, topo, r, N):
     ms(A("cone"), 1.0)
     iota(A("cpi"), [[0, 1]], 0, 1, True)
     iota(A("cmi"), [[0, 8], [1, 16]], 0, 0)
-    iota(A("clc"), [[1, 8], [16, 32]], 0, 0)
     iota(A("cbf"), [[16, 16]], 0, 0)
     asel(A("cid"), A("cone"), [[-1, 128]], OP.is_equal, 0.0, 0, 1)
+    asel(A("cg1"), A("cone", 0, 8), [[-16, 8]], OP.is_ge, 0.0, 0, 1)
+    asel(A("cg"), A("cg1"), [[16, 8]], OP.is_ge, 0.0, 15, -1)
 
     def fused(pairs, rsem):
         tr = []
@@ -343,42 +363,44 @@ def main(g, core, T, topo, r, N):
         g.remote_dma_fused(tr, local_sem=T.sem.loc)
         tot_loc[0] += len(tr)
 
-    def table_out(d, rsem, engines=None):
-        tot_loc[0] += send(g, T, topo, core, d, own[0], own[0], rsem, engines)
+    def table_out(d, x, rsem, engines=None):
+        tot_loc[0] += send(g, T, topo, core, d, x[0], x[0], rsem, engines)
 
     remote(dkey, lambda: fused([(d, T.D[d], T.NL[:, 32 * r:32 * r + 32]) for d in others], "nm"), "nm")
-    remote(A("HT")[1], lambda: fused([((r - 1 - t) % N, T.HT[:], T.HS[:, 4 * t:4 * t + 4]) for t in range(4)], "hs"), "hs")
     for d in others:
         ext(A("NL", 32 * d, 32 * d + 32)[1], "nm", N - 1, 3.0, True)
+    for i in range(2):
+        remote(halves[i][1], lambda i=i: table_out(hc, halves[i], "rel%d" % i, relay_engines(core, hc, topo, T)))
+    remote(A("HT")[1], lambda: fused([((r - 1 - t) % N, T.HT[:], T.HS[:, 4 * t:4 * t + 4]) for t in range(4)], "hs"), "hs")
     ext(A("HS")[1], "hs", 4, 3.0, True)
-    remote(own[1], lambda: table_out(hc, "rel", relay_engines(core, hc, topo, T)))
+    for y0, y1 in PARTS:
+        iota(A("clc", 8 * y0, 8 * y1), [[1, 8], [16, y1 - y0]], 128 * y0, 0)
+    asel(A("cpm"), A("cone", 0, NA), [[-1, 16], [-16, NC]], OP.is_equal, 0.0, 0, 1)
     asel(A("cb1"), A("cone"), [[-16, 8], [0, 16]], OP.is_ge, 0.0, 0, 1)
     asel(A("cblk"), A("cb1"), [[16, 8], [0, 16]], OP.is_ge, 0.0, 15, -1)
-    asel(A("cg1"), A("cone", 0, 8), [[-16, 8]], OP.is_ge, 0.0, 0, 1)
-    asel(A("cg"), A("cg1"), [[16, 8]], OP.is_ge, 0.0, 15, -1)
-    for nc in NCS:
-        asel(A("cpm_%d" % nc, 0, 16 * nc), A("cone", 0, 16 * nc), [[-1, 16], [-16, nc]], OP.is_equal, 0.0, 0, 1)
-    iota(A("cw0f"), [[0, 16]], -1024, 1)
-    iota(A("cbc"), [[4, 8]], 0, 0)
-    iota(A("cio"), [[1, 384]], 0, 0)
-    asel(A("ctf"), A("cone"), [[-1, 128]], OP.is_ge, 0.0, 0, 1)
     ts(A("NO"), A("NL"), 16.0, None, OP.add)
     win = A("TW", BLK * r, BLK * (r + 1))
-    for i, d in enumerate(others + [r]):
-        o, a = A("FO", 512 * d, 512 * d + 512), IND(win, A("NO", 32 * d, 32 * d + 32))
-        if i % 2:
-            copy(o, a)
-        else:
-            act(o, a, AF.Copy)
-    remote(A("FO", 0, 512 * r)[1] + A("FO", 512 * r + 512, 4096)[1],
-           lambda: fused([(d, T.FO[:, 512 * d:512 * d + 512], T.FI[:, 512 * r:512 * r + 512]) for d in others], "ft"), "ft")
-    act(A("FI", 512 * r, 512 * r + 512), A("FO", 512 * r, 512 * r + 512), AF.Copy)
-    for d in others:
-        ext(A("FI", 512 * d, 512 * d + 512)[1], "ft", N - 1, 8.0, True)
+    for i, (y0, y1) in enumerate(PARTS):
+        def slot(n, d, y0=y0, y1=y1):
+            return A(n, 128 * y0 + 16 * (y1 - y0) * d, 128 * y0 + 16 * (y1 - y0) * (d + 1))
+        for k, d in enumerate(others + [r]):
+            o, a = slot("FI" if d == r else "FO", d), IND(win, A("NO", 32 * d + y0, 32 * d + y1))
+            if k % 2:
+                copy(o, a)
+            else:
+                act(o, a, AF.Copy)
+        remote([k for d in others for k in slot("FO", d)[1]], lambda slot=slot, i=i: fused([(d, slot("FO", d)[0], slot("FI", r)[0]) for d in others], "ft%d" % i), "ft%d" % i)
+        for d in others:
+            ext(slot("FI", d)[1], "ft%d" % i, N - 1, 3.0 + 0.16 * (y1 - y0), True)
+        if i == 0:
+            iota(A("cio"), [[1, 384]], 0, 0)
     for o in (3, 5, 7):
-        remote(own[1], lambda o=o: table_out(T.cores[(r - o) % N], "tbx"))
+        remote(own[1], lambda o=o: table_out(T.cores[(r - o) % N], own, "tbx"))
+    iota(A("cw0f"), [[0, 16]], -1024, -1)
+    iota(A("cbc"), [[4, 8]], 0, 0)
+    asel(A("ctf"), A("cone"), [[-1, 128]], OP.is_ge, 0.0, 0, 1)
     for q in others:
-        ext(A("TW", BLK * q + 16, BLK * (q + 1))[1], *(("tb0", 8, 24.0) if q == qs[0] else ("tbx", 48, 60.0)))
+        ext(A("TW", BLK * q + 16, BLK * (q + 1))[1], *(("tb0", 16, 21.0) if q == qs[0] else ("tbx", 48, 55.0)))
 
     ts(A("cpj"), A("cpi"), 15, None, OP.bitwise_and)
     ts(A("cpq"), A("cpj"), 1, None, OP.arith_shift_right)
@@ -386,12 +408,13 @@ def main(g, core, T, topo, r, N):
     for a, b in (("cj", "cpj"), ("cq", "cpq"), ("cpar", "cpt"), ("cp", "cpi")):
         copy(A(a), A(b))
     for h in range(2):
-        ts(A("cbb", h, h + 1), A("cp"), 256.0 + 128 * h, None, OP.add)
+        ts(A("cbb", h, h + 1), A("cp"), -1.0, 383.0 + 128 * h, OP.mult, OP.add)
     ts(A("ceb"), A("cq"), float(BLK), 15.0, OP.mult, OP.add)
-    ts(A("cs"), A("cq"), 496.0, None, OP.mult)
-    ts(A("clb"), A("cj"), 8.0, A("cs"), OP.mult, OP.add)
-    ts(A("LC"), A("clc"), A("clb"), None, OP.add)
-    ts(A("cb2"), A("cbf"), A("cj"), 256.0, OP.add, OP.add)
+    for i, (y0, y1) in enumerate(PARTS):
+        ts(A("cs", i, i + 1), A("cq"), 16.0 * (y1 - y0 - 1), None, OP.mult)
+        ts(A("clb", i, i + 1), A("cj"), 8.0, A("cs", i, i + 1), OP.mult, OP.add)
+        ts(A("LC", 8 * y0, 8 * y1), A("clc", 8 * y0, 8 * y1), A("clb", i, i + 1), None, OP.add)
+    ts(A("cb2"), A("cbf"), A("cj"), None, OP.add)
     for n, fill, first in (("cmh", 256.0, 0.0), ("cml", 0.0, 255.0), ("ckp", 1.0, 0.0)):
         ms(A(n), fill)
         ms(A(n, 0, 512, 16), first)
@@ -405,33 +428,34 @@ def main(g, core, T, topo, r, N):
     copy(A("cbm"), A("cio"))
     ts(A("c2b"), A("cid"), 2.0, None, OP.mult)
     ts(A("cnb"), A("cid"), -1.0, None, OP.mult)
-    ts(A("cgn"), A("cg"), -1.0, None, OP.mult)
     copy(A("cblb"), A("cblk"))
-    for n, w in (("ZA", 512.0), ("ZB", 1024.0), ("ZN", -512.0)):
-        ms(A(n), 0.0)
-        ts(A(n, 15, 143, 16), A("cg"), w, None, OP.mult)
-    for nc in NCS:
-        z = "_%d" % nc
-        copy(A("cph" + z, 0, 16 * nc), A("cpm" + z, 0, 16 * nc))
-        copy(A("cpb" + z, 0, 16 * nc), A("cpm" + z, 0, 16 * nc))
-        ts(A("cr" + z), A("cj"), 16.0 * nc, None, OP.mult)
-        ts(A("cr4" + z), A("cj"), 4.0 * nc, None, OP.mult)
-        for m in range(16 if R0 < 16 else 0):
-            ts(A("SEL" + z, 16 * nc * R0 + m, 256 * nc, 16), A("cpb" + z, nc * R0, 16 * nc), -1.0, None, OP.mult)
-    for s, (c0, c1) in enumerate(ST):
-        ts(A("cbai_%d" % s), A("cbc"), A("cr4_%d" % (c1 - c0)), 64.0 * c0, OP.add, OP.add)
+    ms(A("ZA"), 0.0)
+    ts(A("ZA", 15, 143, 16), A("cg"), 512.0, None, OP.mult)
+    copy(A("cph"), A("cpm"))
+    copy(A("cpb"), A("cpm"))
+    ts(A("cr"), A("cj"), 16.0 * NC, None, OP.mult)
+    ts(A("cr4"), A("cj"), 4.0 * NC, None, OP.mult)
+    for m in range(16):
+        ts(A("SEL", NA * R0 + m, 16 * NA, 16), A("cpb", NC * R0, NA), -1.0, None, OP.mult)
+    for h in range(NS):
+        ts(A("cbai_%d" % h), A("cbc"), A("cr4"), 4.0 * NA * h, OP.add, OP.add)
     ts(A("cmk"), A("cmi"), A("cj"), None, OP.is_equal)
     ts(A("cpen"), A("cmk"), -524288.0, 524288.0, OP.mult, OP.add)
     ms(A("coh", 384, 512), 0.0)
-    ms(A("csn", 0, 256), 1.0)
-    ms(A("csn", 256, 512), 0.0)
+    ms(A("ck", 0, 128), -131072.0)
+    ms(A("ck", 128, 256), 139264.0)
+    for n, w in (("c8", 8192.0), ("n8", -8192.0)):
+        ts(A(n + "i"), A("cid"), w, None, OP.mult)
+        ts(A(n + "b"), A("cblk"), w, None, OP.mult)
+    ms(A("csn", 0, 128), 0.0)
+    ms(A("csn", 128, 512), 1.0)
     for k in range(4):
         ts(A("ctri", 128 * k, 128 * k + 128), A("ctf"), -64.0, None, OP.mult)
         ts(A("cth", 128 * k, 128 * k + 128), A("ctf"), 64.0, 13.5, OP.mult, OP.add)
         if k < 3:
             copy(A("coh", 128 * k, 128 * k + 128), A("cmk"))
     copy(A("cw0"), A("cw0f"))
-    ts(A("cw1"), A("cw0f"), 128.0, None, OP.add)
+    ts(A("cw1"), A("cw0f"), -128.0, None, OP.add)
     copy(A("HF"), A("HS"))
     ts(A("kd"), A("HS"), 1, None, OP.bitwise_and)
     for t in range(4):
@@ -441,7 +465,7 @@ def main(g, core, T, topo, r, N):
         ts(A("hcol", t, t + 1), A("kd", 4 * t + 2, 4 * t + 3), -2048.0, 4196352.0, OP.mult, OP.add)
         copy(A("ZZ", 16 * t, 16 * t + 8), A("cg"))
         ts(A("ZZ", 16 * t + 8, 16 * t + 16), A("cg"), A("HF", 4 * t + 2, 4 * t + 3), None, OP.mult)
-        b = A("B%d" % (5 + t % 2), 0, 128, 1, 0, 16)
+        b = B(5 + t % 2, 0, 128, 1, 16)
         mm(b, A("ZZ", 16 * t, 16 * t + 16), A("cih"))
         copy(A("KM", 128 * t, 128 * t + 128, 1, 0, 16), b)
         x = float(2 * qs[t] + t // N)
@@ -450,7 +474,8 @@ def main(g, core, T, topo, r, N):
         ts(A("XM"), A("cmi"), x, None, OP.is_equal)
         tt(A("XS", 128 * t, 128 * t + 128), A("XM"), A("cblk"), OP.mult)
         copy(A("XB", 128 * t, 128 * t + 128), A("XS", 128 * t, 128 * t + 128))
-    ts(A("P", 0, 256), A("TP"), 1.0, None, OP.add)
+    ts(A("P", 256, 512), A("TP"), 1.0, None, OP.add)
+    ms(A("P", 0, 256), 0.0)
     ts(A("S"), A("SD"), 1.0, None, OP.add)
     for j in range(16):
         ts(A("cbt", j, j + 1), A("cj"), float(j), float(2 ** (12 - j)) if j < 13 else (-1.0 if j == 13 else 0.0), OP.is_equal, OP.mult)
@@ -464,27 +489,21 @@ def main(g, core, T, topo, r, N):
         tt(A("cc", 2 * i, 2 * i + 1), A("cc", 6, 7), A(m), OP.mult)
         tt(A("cc", 2 * i + 1, 2 * i + 2), A("cc", 7, 8), A(m), OP.mult)
 
-    one = BANKS["key"] == BANKS["hash"]
-
     def shape(h):
-        c0, c1 = ST[h]
-        return "_%d" % h, "_%d" % (c1 - c0), c1 - c0, 16 * c0, 16 * c1, 16 * (c1 - c0), 256 * c0
+        return "_%d" % h, NA * h, NA * h + NA, 16 * NA * h
 
     def place(h, k, p1=128):
-        na = shape(h)[5]
-        if k == 4 and not one:
-            return A("B%d" % BANKS["key"][h], 384, 384 + na)
-        c = (na if one else 0) + (16 + (k - 1) * na if k else 0)
-        return A("B%d" % BANKS["hash"][h], c, c + (na if k else 16), 1, 0, p1)
+        c = NA + (16 + (k - 1) * NA if k else 0)
+        return B(h, c, c + (NA if k else 16), 1, p1)
 
     def middle(h, t):
-        s, z, nc, a0, a1, na, x0 = shape(h)
+        s, a0, a1, x0 = shape(h)
         if t:
-            ts(A("EO", a0, a1), A("P", a0, a1), A("ceb"), None, OP.add)
-        cut = [a0 + 2 * (na * k // (2 * len(MID))) for k in range(len(MID) + 1)]
-        for k, e in enumerate(MID):
+            ts(A("EO", a0, a1), A("P", 256 + a0, 256 + a1), A("ceb"), None, OP.add)
+        cut = [a0 + 2 * (NA * k // (2 * len(MID[h]))) for k in range(len(MID[h]) + 1)]
+        for k, e in enumerate(MID[h]):
             o, x = cut[k:k + 2], (16 * cut[k], 16 * cut[k + 1])
-            src = IND(A("TW"), A("EO", *o)) if t else IND(A("FI"), A("LC", *o))
+            src = IND(A("TW"), A("EO", *o)) if t else IND(A("FI", 0, 128 * min(y1 for y0, y1 in PARTS if 8 * y1 >= a1)), A("LC", *o))
             if e == "v":
                 copy(A("FA", *x), src)
             else:
@@ -495,40 +514,41 @@ def main(g, core, T, topo, r, N):
                 scan(A("HI", c, c + n), A("cmh", 0, n), A("FA", c, c + n), 0.0, OP.min, OP.max)
                 scan(A("LO", c, c + n), A("cml", 0, n), A("FB", c, c + n), 255.0, OP.max, OP.min)
         se = place(h, 3)
-        mm(se, A("cib"), A("HI", x0 + 15, x0 + 16 * na, 16), True, False)
-        mm(se, A("cib"), A("LO", x0 + 15, x0 + 16 * na, 16), False, True)
+        mm(se, A("cib"), A("HI", x0 + 15, x0 + 16 * NA, 16), True, False)
+        mm(se, A("cib"), A("LO", x0 + 15, x0 + 16 * NA, 16), False, True)
         ts(A("C", a0, a1), se, 2047.5, None, OP.add)
         ts(A("EB", a0, a1), A("C", a0, a1), 0.5, -1024.0, OP.mult, OP.add)
-        db = "B%d" % BANKS["diff"][h][0]
-        et, ec, e2 = A(db, 0, 128, 1, 0, na), A(db, 128, 128 + na), place(h, 4)
+        et, ec = B(4 + h, 0, 128, 1, NA), B(4 + h, 128, 128 + NA)
         mm(et, A("EB", a0, a1), A("cib"))
-        act(A("ET" + s, 0, 128, 1, 0, na), et, AF.Copy)
-        mm(ec, A("ET" + s, 0, 128, 1, 0, na), A("cpb" + z, 0, na, 1, 0, na))
-        act(A("IJ", x0, x0 + 16 * na, 16), ec, AF.Copy)
-        for c in range(x0, x0 + na * R0, 512):
-            n = min(512, x0 + na * R0 - c)
+        act(A("ET" + s, 0, 128, 1, 0, NA), et, AF.Copy)
+        mm(ec, A("ET" + s, 0, 128, 1, 0, NA), A("cpb", 0, NA, 1, 0, NA))
+        act(A("IJ", x0, x0 + 16 * NA, 16), ec, AF.Copy)
+        for c in range(x0, x0 + NA * R0, 512):
+            n = min(512, x0 + NA * R0 - c)
             scan(A("ER", c, c + n), A("ckp", 0, n), A("IJ", c, c + n), 0.0, OP.mult, OP.add)
-        mm(e2, A("c2b"), A("EB", a0, a1), True, R0 == 16)
-        b, _, _, c, c1, _ = e2[1][0]
+
+    def restore(h):
+        s, a0, a1, x0 = shape(h)
+        mm(B(4 + h, 0, NA), A("c2b"), A("EB", a0, a1), True, False)
         for k in range(R0, 16):
-            mm(A(b, c + k, c1, 16), A("cnb"), A("EB", a0 + k, a1, 16), False, k == 15)
-        act(A("E2", a0, a1), e2, AF.Identity, bias=2047.5)
+            mm(B(4 + h, k, NA, 16), A("cnb"), A("EB", a0 + k, a1, 16), False, k == 15)
+        act(A("E2", a0, a1), B(4 + h, 0, NA), AF.Identity, bias=2047.5)
 
     def hash_(h, p, t):
-        s, z, nc, a0, a1, na, x0 = shape(h)
-        u = place(h, 0, na)
-        mm(u, A("cneg", 0, na), A("WH", 16 * t, 16 * t + 16), True, False)
+        s, a0, a1, x0 = shape(h)
+        u = place(h, 0, NA)
+        mm(u, A("cneg", 0, NA), A("WH", 16 * t, 16 * t + 16), True, False)
         mm(u, A("C", a0, a1), A("WH", 16 * t, 16 * t + 16), False, True)
 
         def part(n, c0=0, c1=16):
-            return A(n + s, c0, c1, 1, 0, na)
+            return A(n + s, c0, c1, 1, 0, NA)
         copy(part("UI"), u)
         ts(part("UA"), part("UI"), 4095, None, OP.bitwise_and)
         tt(part("VP", 0, 8), part("UA", 0, 8), part("UA", 8, 16), OP.mult)
         ts(part("UA", 0, 8), part("VP", 0, 8), 5, 4095, OP.arith_shift_right, OP.bitwise_and)
         ts(part("HB"), part("UA"), -2048.0, None, OP.add)
         x, y, hh = place(h, 1, 16), A("HX", a0, a1, 1, 0, 16), place(h, 2)
-        mm(x, part("HB"), A("cph" + z, 0, na, 1, 0, na))
+        mm(x, part("HB"), A("cph", 0, NA, 1, 0, NA))
         copy(y, x)
         mm(hh, A("KM", 128 * t, 128 * t + 128, 1, 0, 16), y)
         ts(A("HN", a0, a1), hh, A("hcol", t, t + 1), None, OP.add)
@@ -537,56 +557,45 @@ def main(g, core, T, topo, r, N):
         copy(A("OF", a0, a1), d)
 
     def look(h, p, t):
-        s, z, nc, a0, a1, na, x0 = shape(h)
-        key = A("B%d" % BANKS["key"][h], 0, na)
-        w = A("TW", BLK * qs[t] + 16, BLK * qs[t] + BLK)
-        mm(key, A("cih"), A("cbm", 128 * p, 128 * p + na), True, False)
-        nd = 0
+        s, a0, a1, x0 = shape(h)
+        key, w = B(h, 0, NA), A("TW", BLK * qs[t] + 16, BLK * qs[t] + BLK)
+        mm(key, A("cih"), A("cbm", 128 * p, 128 * p + NA), True, False)
         for i, (how, r0, r1) in enumerate(LOOK):
-            x = (x0 + na * r0, x0 + na * r1)
-            xv, ax, src = A("XV", *x), A("AX", *x), IND(w, A("OF", a0 + nc * r0, a0 + nc * r1))
-            if how == "d":
-                b = A("B%d" % BANKS["diff"][h][nd % len(BANKS["diff"][h])], 0, x[1] - x[0])
-                nd += 1
-                act(xv, src, AF.Copy)
-                mm(b, A("ET" + s, 0, 128, 1, 0, na), A("SEL" + z, na * r0, na * r1, 1, 0, na), True, False)
+            x = (x0 + NA * r0, x0 + NA * r1)
+            xv, ax = A("XV", *x), A("AX", *x)
+            if how == "s":
+                b = B(4 + h, 0, x[1] - x[0])
+                act(xv, IND(w, A("OF", a0 + NC * r0, a0 + NC * r1)), AF.Copy)
+                mm(b, A("ET" + s, 0, 128, 1, 0, NA), A("SEL", NA * r0, NA * r1, 1, 0, NA), True, False)
                 mm(b, A("cib"), xv, False, True)
                 act(ax, b, AF.Abs)
             else:
                 for k in range(r0, r1, VSUB):
                     e = min(r1, k + VSUB)
-                    y = (x0 + na * k, x0 + na * e)
-                    tt(A("XV", *y), IND(w, A("OF", a0 + nc * k, a0 + nc * e)), A("ER", *y), OP.subtract)
-                if how == "a":
-                    ts(ax, xv, 0.0, None, OP.max)
-                else:
-                    act(ax, xv, AF.Abs)
+                    y = (x0 + NA * k, x0 + NA * e)
+                    tt(A("XV", *y), IND(w, A("OF", a0 + NC * k, a0 + NC * e)), A("ER", *y), OP.subtract)
+                act(ax, xv, AF.Abs)
             for k in range(r0, r1):
-                last, c = i == len(LOOK) - 1 and k == r1 - 1, x0 + na * k
-                if how == "a":
-                    mm(key, A("ZN", 15 - k, 143 - k), A("XV", c, c + na), False, False)
-                mm(key, A("ZB" if how == "a" else "ZA", 15 - k, 143 - k), A("AX", c, c + na), False, last)
+                mm(key, A("ZA", 15 - k, 143 - k), A("AX", x0 + NA * k, x0 + NA * k + NA), False, i == len(LOOK) - 1 and k == r1 - 1)
 
     def winner(h, p, t):
-        s, z, nc, a0, a1, na, x0 = shape(h)
-        scan(A("SC", a0, a1), A("cm0", 0, na), A("B%d" % BANKS["key"][h], 0, na), BIG, OP.max, OP.min)
+        s, a0, a1, x0 = shape(h)
+        scan(A("SC", a0, a1), A("cm0", 0, NA), B(h, 0, NA), BIG, OP.max, OP.min)
         if p < 2:
-            k = A("KI" + s, 8 * p, 8 * p + nc)
+            k = A("KI" + s, 8 * p, 8 * p + NC)
             copy(k, A("SC", a0 + 15, a1, 16))
-            ts(A("J" + s, 0, nc), k, 127, None, OP.bitwise_and)
-            ts(A("JU" + s, 0, nc), A("J" + s, 0, nc), A("cr" + z), None, OP.add)
-            tt(A("C", a0, a1), IND(A("XV", x0, x0 + 16 * na), A("JU" + s, 0, nc)), A("E2", a0, a1), OP.add)
+            ts(A("J" + s, 0, NC), k, 127, None, OP.bitwise_and)
+            ts(A("JU" + s, 0, NC), A("J" + s, 0, NC), A("cr"), None, OP.add)
+            tt(A("C", a0, a1), IND(A("XV", x0, x0 + 16 * NA), A("JU" + s, 0, NC)), A("E2", a0, a1), OP.add)
         if p == 1:
-            tt(A("BA" + s, 0, nc), A("KI" + s, 0, nc), A("KI" + s, 8, 8 + nc), OP.min)
-            ts(A("BB" + s, 0, nc), A("BA" + s, 0, nc), A("th", t, t + 1), None, OP.min)
-
-    psb, psc = "B%d" % BANKS["ps"][0], BANKS["ps"][1]
+            tt(A("BA" + s, 0, NC), A("KI" + s, 0, NC), A("KI" + s, 8, 8 + NC), OP.min)
+            ts(A("BB" + s, 0, NC), A("BA" + s, 0, NC), A("th", t, t + 1), None, OP.min)
 
     def names(h, t):
-        s, z, nc, a0, a1, na, x0 = shape(h)
+        s, a0, a1, x0 = shape(h)
 
         def part(n):
-            return A(n + s, 0, nc)
+            return A(n + s, 0, NC)
         tt(part("BK"), A("SC", a0 + 15, a1, 16), part("BB"), OP.min)
         ts(part("MI"), part("BK"), 511, None, OP.bitwise_and)
         ts(part("PI"), part("BK"), 7, 3, OP.arith_shift_right, OP.bitwise_and)
@@ -595,94 +604,86 @@ def main(g, core, T, topo, r, N):
         act(A("OH", a0, a1), IND(A("coh"), part("L2U")), AF.Copy)
         copy(part("L1U"), part("L1"))
         tt(A("PR", a0, a1), IND(A("HST"), part("L1U")), A("OH", a0, a1), OP.mult)
-        nrep, ps = place(h, 3), A(psb, psc + a0, psc + a1)
+        nrep, ps, c = place(h, 3), B(2 * (a0 // 128), 384 + a0 % 128, 384 + a0 % 128 + NA), 128 - 256 * (a0 // 128)
         mm(nrep, A("cblb"), A("OH", a0, a1), True, False)
         mm(nrep, A("cblk"), A("PR", a0, a1), False, True)
-        mm(ps, A("DX", 128 * t, 128 * t + 128), A("P", a0, a1), True, False)
+        ts(A("I1", a0, a1), nrep, A("csc"), None, OP.mult)
+        mm(ps, A("DX", 128 * t, 128 * t + 128), A("P", 256 + a0, 256 + a1), True, False)
         mm(ps, A("XB", 128 * t, 128 * t + 128), A("OH", a0, a1), False, False)
         mm(ps, A("XS", 128 * t, 128 * t + 128), A("PR", a0, a1), False, True)
-        ts(A("I1", a0, a1), nrep, A("csc"), None, OP.mult)
         ts(A("I2", a0, a1), A("I1", a0, a1), 4096, None, OP.bitwise_and)
         ts(A("BE", a0, a1), A("I2", a0, a1), A("cc", 0, 1), A("cc", 1, 2), OP.mult, OP.add)
         ts(A("BO", a0, a1), A("I2", a0, a1), A("cc", 2, 3), A("cc", 3, 4), OP.mult, OP.add)
-        act(A("P", a0, a1), ps, AF.Copy)
-        act(A("P", 256 + a0, 256 + a1), ps, AF.Copy)
+        act(A("PW", 256 + a0, 256 + a1), ps, AF.Copy)
+        act(A("PW", c + a0, c + a1), ps, AF.Copy)
 
-    def same(out, a0, b0, onv):
-        banks, tri = BANKS[out], a0 == b0 and not onv
-        if tri:
-            for i in range(2):
-                mm(A("B%d" % banks[i]), A("cib"), A("ctri"), True, False)
-        for k in (0, 1, 4, 5, 2, 3, 6, 7):
-            src, p0 = "BE" if k % 2 == 0 else "BO", 32 * (k // 2)
-            mm(A("B%d" % banks[k // 4], 128 * (k % 4), 128 * (k % 4) + 128), A(src, a0, a0 + 128, 1, p0, p0 + 32), A(src, b0, b0 + 128, 1, p0, p0 + 32),
-               not tri, not tri or k % 4 == 3)
-        for i in range(2):
-            o, b = A(out, 512 * i, 512 * i + 512), A("B%d" % banks[i])
-            if onv:
-                tt(o, b, A("cth"), OP.is_ge)
-            else:
-                act(o, b, AF.Relu, bias=-13.0)
-
-    def lower(h):
-        bank, x = "B%d" % BANKS["low"][h], (128 * h, 128 * h + 128)
-        mm(A(bank, 0, 128), A("cib"), A("cpen"), True, False)
-        for k in range(8):
-            o = A(bank, 16 * k, 16 * k + 16)
-            mm(o, A("QX" if h else "QA", 128 * k, 128 * k + 128), A("cw0"), False, k == 7 and not h)
-            if h:
-                mm(o, A("QB", 128 * k, 128 * k + 128), A("cw1"), False, k == 7)
-        act(A("LA", *x), A(bank, 0, 128), AF.Abs, bias=1024.0)
-        act(A("LT", *x), A("LA", *x), AF.Relu, bias=A("cbb", h, h + 1), scale=-1.0)
-
-    def pairs():
-        ps, lb = A(psb, psc, psc + 256), "B%d" % BANKS["low"][0]
-        same("QX", 0, 128, False)
-        same("QB", 128, 128, True)
-        lower(1)
-        mm(A(lb, 128, 144), A("cid"), A("cb2"), True, False)
-        for h in range(2):
-            mm(A(lb, 128 + 8 * h, 136 + 8 * h), A("LT", 128 * h, 128 * h + 128), A("cgn"), False, h == 1)
-        tt(A("SP"), A("S"), ps, OP.subtract)
-        copy(A("LSU"), A(lb, 128, 144))
-        copy(A("Q"), IND(A("P"), A("LSU")))
-        act(A("SN"), IND(A("csn"), A("LSU")), AF.Copy)
-        ne, cn, pn, nd, nc = (A("B%d" % b, 0, 256) for b in BANKS["rest"])
-        tt(ne, ps, A("Q"), OP.not_equal)
-        tt(A("MN"), ps, A("Q"), OP.min)
-        tt(A("TT"), ne, A("MN"), OP.mult)
-        ts(A("ND"), A("TT"), 0.0, None, OP.is_le)
-        mm(cn, A("cib"), A("SN"), True, False)
-        mm(cn, A("cblb"), A("ND"), False, True)
-        mm(nd, A("cib"), A("ND"))
-        act(nc, cn, AF.Relu, bias=-16.0)
-        tt(pn, ps, A("ND"), OP.mult)
-        tt(A("QN"), nd, A("Q"), OP.mult)
-        tt(A("PC"), A("P", 0, 256), nc, OP.mult)
-        tt(A("SX"), A("SP"), nc, OP.mult)
-        tt(A("P", 0, 256), pn, A("SX"), OP.add)
-        tt(IND(A("P"), A("LSU")), A("QN"), A("PC"), OP.max)
+    def pairs(h):
+        a0, a1, kb = 128 * h, 128 * h + 128, 2 * h + 1
+        ps, low = B(2 * h, 384, 512), B(kb, 0, 128)
+        for i, banks in enumerate(SAME[h]):
+            onv = i == 1
+            tri = i == h and not onv
+            for b in banks if tri else ():
+                mm(B(b), A("cib"), A("ctri"), True, False)
+            for k in (0, 1, 4, 5, 2, 3, 6, 7):
+                src, p0, c = "BE" if k % 2 == 0 else "BO", 32 * (k // 2), 128 * (k % 4)
+                mm(B(banks[k // 4], c, c + 128), A(src, 128 * i, 128 * i + 128, 1, p0, p0 + 32), A(src, a0, a1, 1, p0, p0 + 32), not tri, not tri or k % 4 == 3)
+            for j, b in enumerate(banks):
+                o = A(("QA", "QX", "QB")[h + i], 512 * j, 512 * j + 512)
+                if onv:
+                    tt(o, B(b), A("cth"), OP.is_ge)
+                else:
+                    act(o, B(b), AF.Relu, bias=-13.0)
+        mm(low, A("cib"), A("cpen"), True, False)
+        for i in range(h + 1):
+            for k in range(8):
+                mm(B(kb, 16 * k, 16 * k + 16), A(("QA", "QX", "QB")[h + i], 128 * k, 128 * k + 128), A("cw%d" % i), False, k == 7 and i == h)
+        la, lt, ls, lu = A("LA", a0, a1), A("LT", a0, a1), B(kb, 128, 136), A("LSU", 8 * h, 8 * h + 8)
+        act(la, low, AF.Abs, bias=1279.0)
+        act(lt, la, AF.Relu, bias=A("cbb", h, h + 1), scale=-1.0)
+        mm(ls, A("cid"), A("cb2", 0, 8), True, False)
+        mm(ls, lt, A("cg"), False, True)
+        copy(lu, ls)
+        q, sn, mn, t2, nd, pn, qn, pc, s1, p1 = (A(n, a0, a1) for n in ("Q", "SN", "MN", "TT", "ND", "PN", "QN", "PC", "SX", "SP"))
+        ne, yes, no = (B(kb, 128 * k, 128 * k + 128) for k in range(3))
+        copy(q, IND(A("PW", 256 - a1, 256 + a1), lu))
+        act(sn, IND(A("csn"), lu), AF.Copy)
+        tt(ne, ps, q, OP.not_equal)
+        tt(mn, ps, q, OP.min)
+        tt(t2, ne, mn, OP.mult)
+        ts(nd, t2, 0.0, None, OP.is_le)
+        for o, w, c in ((yes, "c8", 0), (no, "n8", 128)):
+            mm(o, A("cib"), A("ck", c, c + 128), True, False)
+            mm(o, A(w + "i"), sn, False, False)
+            mm(o, A(w + "b"), nd, False, True)
+        tt(pn, ps, nd, OP.mult)
+        tt(qn, q, nd, OP.mult)
+        tt(s1, yes, A("S", a0, a1), OP.min)
+        tt(p1, no, pn, OP.min)
+        tt(pc, yes, A("PW", 256 + a0, 256 + a1), OP.min)
+        tt(A("P", 256 + a0, 256 + a1), s1, p1, OP.max)
+        tt(IND(A("P", 256 - a1, 256 + a1), lu), qn, pc, OP.max)
 
     for t in range(4):
-        for h in range(len(ST)):
-            lead[0] = len(ST) - 1 - h
+        for h in range(NS):
+            lead[0] = NS - 1 - h
             middle(h, t)
             hash_(h, 0, t)
             look(h, 0, t)
+            restore(h)
         for p in range(3):
-            for h in range(len(ST)):
-                lead[0] = len(ST) - 1 - h
+            for h in range(NS):
+                lead[0] = NS - 1 - h
                 winner(h, p, t)
                 if p < 2:
                     hash_(h, p + 1, t)
                     look(h, p + 1, t)
                 else:
                     names(h, t)
-                    if ST[h][0] < 8 <= ST[h][1]:
-                        same("QA", 0, 0, False)
-                        lower(0)
-        pairs()
-    ts(A("YO"), A("P", 0, 256), -1.0, None, OP.add)
+                    if h % 2:
+                        lead[0] = 1
+                        pairs(h // 2)
+    ts(A("YO"), A("P", 256, 512), -1.0, None, OP.add)
 
     for o in schedule(ops):
         o[3]()

@@ -1,36 +1,35 @@
 from concourse.bass import DstId, RemoteDMATransfer
-from concourse.mybir import AluOpType as OP, AxisListType, ActivationFunctionType as AF
+from concourse.mybir import AluOpType as OP, ActivationFunctionType as AF
 
 BLK = 4112
 NS, NC, NA = 4, 4, 64
-LOOK = (("v", 0, 4), ("s", 8, 12), ("v", 4, 8), ("s", 12, 16))
-R0 = max(x[2] for x in LOOK if x[0] == "v")
-VSUB = 2
-MID = ("vs", "sv", "ss", "sv")
+LOOK = (("s", 9, 13), ("v", 0, 5), ("s", 13, 16), ("v", 5, 9))
+R0 = max(x[2] for x in LOOK if x[0] != "s")
+VSUB = 8
+MID = ("vs", "sv", "vs", "sv")
 PARTS = ((0, 16), (16, 32))
-SAME = (((4, 5),), ((4, 5), (6, 7)))
+UNITS = ((0, 128), (128, 256))
+SAME = ("v", "v", "sv", "vv")
 BIG = 16777216.0
-LAT, CY, GA, TF, SMALL, ROUNDS = 0.2, 0.001, 1.56, 0.65, 0.22, 2
-TRIES = [(1.0 + 0.1 * a, b) for a in range(10) for b in (2.0, 3.0, 4.0, 6.0)]
-CASES = ((0.2, 0.2, 0.8), (0.06, 0.3, 0.8), (0.2, 0.2, 1.3))
+LAT, CY, GA, TF, SMALL, ROUNDS, SKEW, BONUS = 0.25, 0.001, 1.56, 0.65, 0.22, 2, 1.1, 2.0
 CHOSEN = []
 F32, BF, I32, U16, F16 = "float32", "bfloat16", "int32", "uint16", "float16"
 
 SCRATCH = {"TW": ("sbuf", [128, 8 * BLK], BF), "D": ("dram", [8, 128, 32], I32)}
 WIDTH, PLACE, TWO, _used = {"TW": 8 * BLK, "D": 1}, {}, {"TW", "FO", "FI"}, {}
-for _n, _w, _d in (("NL", 256, I32), ("HT", 4, I32), ("HS", 16, I32), ("FO", 4096, BF), ("FI", 4096, BF), ("P", 512, F32), ("TP", 256, I32), ("SD", 256, I32), ("YO", 256, F32)):
+for _n, _w, _d in (("NL", 256, I32), ("HT", 4, I32), ("HS", 16, I32), ("FO", 4096, BF), ("FI", 4096, BF), ("P", 640, F32), ("TP", 256, I32), ("SD", 256, I32), ("YO", 256, F32)):
     SCRATCH[_n], WIDTH[_n] = ("sbuf", [128, _w], _d), _w
 for _k in range(8):
     SCRATCH["B%d" % _k], WIDTH["B%d" % _k] = ("psum", [128, 512], F32), 512
-SPEC = ((BF, 1, "ET 128"), (F16, 1, "HB 16"), (U16, 1, "JU 8 L1U 8 L2U 8"), (I32, 1, "UI 16 UA 16 VP 8 KI 16 J 8 BA 8 BB 8 BK 8 PI 8 L1 8 MI 8 cbai 8"),
-        (F32, 0, "E2 256 SC 256 PR 256 LA 256 LT 256 Q 256 QN 256 SX 256 PN 256 SP 256 PW 512 PC 256 S 256 HF 16 cone 128 cid 128 cb1 128 cblk 128 "
-                 "cg1 8 cg 8 cmi 128 cmk 128 cm0 128 cj 1 cq 1 cs 4 cp 1 cbb 2 cpar 1 cnpar 1 ceb 1 clb 4 cb2 16 cbf 16 cbc 8 clc 256 ctf 128 cw0f 16 "
-                 "cbt 16 csc 1 cc 8 ntx 4 XM 128 XS 512 DX 512 th 4 hcol 4 cio 384 cth 512 cpm 64 cr 1 cr4 1"),
-        (I32, 0, "HST 1024 HN 256 I1 256 I2 256 cpi 1 cpj 1 cpq 1 cpt 1 kd 16"),
-        (BF, 0, "FA 4096 FB 4096 HI 4096 LO 4096 IJ 4096 ER 4096 XV 4096 AX 4096 EB 256 OH 256 BE 256 BO 256 QA 1024 QX 1024 QB 1024 ND 256 MN 256 "
-                "TT 256 SN 256 c8i 128 c8b 128 n8i 128 n8b 128 ck 256 cib 128 c2b 128 cnb 128 cblb 128 cmh 512 cml 512 ckp 512 ctri 512 cpen 128 "
-                "csn 512 coh 512 XB 512 ZA 144 cpb 64 SEL 1024"),
-        (U16, 0, "NO 256 EO 256 LC 256 OF 256 LSU 16"), (F16, 0, "C 256 HX 256 cw0 16 cw1 16 cneg 128 cih 128 cbm 384 WH 64 ZZ 64 KM 512 cph 64"))
+SPEC = ((BF, 1, "ET 128 Q3 64 QA 512 QB 512"), (F16, 1, "QH 64"), (U16, 1, "JU 8 LU 8 LS 8"), (I32, 1, "KI 16 J 8 BA 8 BB 8 BK 8 L 8"), (F32, 1, "SQ 64"),
+        (F32, 0, "E2 256 SC 256 LA 128 LT 128 Q 256 QN 256 SP 256 PW 640 PO 256 PC 256 S 256 HF 16 cone 128 cid 128 cb1 128 cblk 128 "
+                 "cg1 8 cg 8 cmi 128 cmk 128 cm0 128 cj 1 cq 1 cs 4 cp 3 cbb 4 ceb 1 clb 4 cb2 16 cbf 16 clc 256 cw0f 16 cc 8 ntx 4 XM 128 DX 512 "
+                 "th 4 THK 16 ctk 4 cio 192 cpm 64 cr 1 hs 32 xb 4 csq 128 ctm 128 chh 128 chl 128 cb3 8 cng 8"),
+        (I32, 0, "HST 1024 HN 256 cpi 1 cpj 1 cpq 1 wx 128 wh 128 wl 128 hi 8"),
+        (BF, 0, "FA 4096 FB 4096 HI 4096 LO 4096 IJ 4096 ER 4096 XV 4096 AX 4096 EB 256 NE 256 MN 256 CL 256 SN 256 c8i 128 n8i 128 n8b 128 c8n 128 ck 384 "
+                "cib 128 c2b 128 cnb 128 cmh 512 cml 512 ckp 512 cpen 128 csn 640 coh 16 ZA 144 ZB 144 ZC 144 cpb 64 SEL 1024 c4n 128 CT 1024 GM 512 GN 1024 QZ 1024"),
+        (U16, 0, "NO 256 EO 256 LC 256 OF 256 PU 4"),
+        (F16, 0, "C 256 HG 256 PR 256 LH 128 cw0 16 cw1 16 cih 128 cbm 192 WX 512 WH 512 WL 512 DN 512 DK 128 XS 512 c4k 64 cz 64 csel 128 cblh 128 cgn 8 cb3h 8 c1 2"))
 ARENA = {F32: "af", BF: "ab", I32: "ai", U16: "au", F16: "ah"}
 for _d, _each, _s in SPEC:
     _it = _s.split()
@@ -102,9 +101,8 @@ def covers(x, y):
     return x[5] == 1 and x[1] <= y[1] and x[2] >= y[2] and x[3] <= y[3] and x[4] >= y[4]
 
 
-def schedule(ops):
-    n = len(ops)
-    preds, succs, acc, lastg = [set() for _ in ops], [[] for _ in ops], {}, None
+def depends(ops):
+    preds, acc, runs, lastg = [set() for _ in ops], {}, {}, None
     for i, (q, rd, wr) in enumerate(o[:3] for o in ops):
         if q == "g":
             if lastg is not None:
@@ -114,12 +112,26 @@ def schedule(ops):
             for x in keys:
                 lst = acc.setdefault(x[0], [])
                 if is_bank(x[0]):
-                    preds[i].update(e[2] for e in lst)
-                    acc[x[0]] = [(x, True, i)]
+                    run = runs.setdefault(x[0], [q, [], []])
+                    if run[0] != q:
+                        run[:] = [q, [e[2] for e in run[2]][-1:] if run[0] == "t" else [e[2] for e in run[2]], []]
+                    preds[i].update(run[1])
+                    preds[i].update([e[2] for e in run[2]][-1:] if q == "t" else [e[2] for e in run[2] if (w or e[1]) and overlap(x, e[0])])
+                    run[2].append((x, w, i))
                     continue
                 preds[i].update(e[2] for e in lst if (w or e[1]) and overlap(x, e[0]))
                 acc[x[0]] = [e for e in lst if not (w and covers(x, e[0]))] + [(x, w, i)]
         preds[i].discard(i)
+    return preds
+
+
+def schedule(ops):
+    n = len(ops)
+    preds, succs = depends(ops), [[] for _ in ops]
+    if CHOSEN and len(CHOSEN[0]) == n:
+        place = {j: k for k, j in enumerate(CHOSEN[0])}
+        if all(place[j] < place[i] for i in range(n) for j in preds[i]):
+            return [ops[i] for i in CHOSEN[0]]
     for i in range(n):
         for j in preds[i]:
             succs[j].append(i)
@@ -154,42 +166,27 @@ def schedule(ops):
     for i in range(n - 1, -1, -1):
         prio[i] = cost[i] + max([prio[j] + lat(i, j) for j in succs[i]] + [0.0])
     first, none = [o[5] for o in ops], [0.0] * n
-
-    def attempt(skew, bonus):
-        urge = [p + skew * o[6] + bonus * (o[4] < SMALL) for p, o in zip(prio, ops)]
-        left = [len(p) for p in preds]
-        start, fin, free = [0.0] * n, [0.0] * n, {}
-        ready = {i: first[i] for i in range(n) if not left[i]}
-        while ready:
-            t0, _, i = min((max(ready[i], free.get(queue[i], 0.0)), -urge[i], i) for i in ready)
-            del ready[i]
-            start[i], fin[i] = t0, t0 + cost[i]
-            if queue[i] != "x":
-                free[queue[i]] = fin[i]
-            for j in succs[i]:
-                left[j] -= 1
-                if not left[j]:
-                    ready[j] = max([first[j]] + [fin[k] + lat(j, k) for k in preds[j]])
-        best = (max(fin), start)
-        for _ in range(ROUNDS):
-            start, fin = pack(sorted(range(n), key=lambda i: (-fin[i], -start[i], -i)), succs, none)
-            start, fin = pack(sorted(range(n), key=lambda i: (-fin[i], -start[i], i)), preds, first)
-            best = min(best, (max(fin), start))
-        return sorted(range(n), key=lambda i: (best[1][i], i))
-
-    def length(turns, own, other, tensor):
-        fin, free = [0.0] * n, {}
-        for i in turns:
-            q = queue[i]
-            t = max([first[i], free.get(q, 0.0)] + [fin[k] + (lat(i, k) and (own if queue[k] == q else other)) for k in preds[i]])
-            fin[i] = t + cost[i] * (tensor if q == "t" else 1.0)
-            if q != "x":
-                free[q] = fin[i]
-        return max(fin)
-
-    if not CHOSEN:
-        CHOSEN.append(min(TRIES, key=lambda x: sum(length(t, *c) for t in [attempt(*x)] for c in CASES)))
-    return [ops[i] for i in attempt(*CHOSEN[0])]
+    urge = [p + SKEW * o[6] + BONUS * (o[4] < SMALL) for p, o in zip(prio, ops)]
+    left = [len(p) for p in preds]
+    start, fin, free = [0.0] * n, [0.0] * n, {}
+    ready = {i: first[i] for i in range(n) if not left[i]}
+    while ready:
+        t0, _, i = min((max(ready[i], free.get(queue[i], 0.0)), -urge[i], i) for i in ready)
+        del ready[i]
+        start[i], fin[i] = t0, t0 + cost[i]
+        if queue[i] != "x":
+            free[queue[i]] = fin[i]
+        for j in succs[i]:
+            left[j] -= 1
+            if not left[j]:
+                ready[j] = max([first[j]] + [fin[k] + lat(j, k) for k in preds[j]])
+    best = (max(fin), start)
+    for _ in range(ROUNDS):
+        start, fin = pack(sorted(range(n), key=lambda i: (-fin[i], -start[i], -i)), succs, none)
+        start, fin = pack(sorted(range(n), key=lambda i: (-fin[i], -start[i], i)), preds, first)
+        best = min(best, (max(fin), start))
+    CHOSEN[:] = [sorted(range(n), key=lambda i: (best[1][i], i))]
+    return [ops[i] for i in CHOSEN[0]]
 
 
 def main(g, core, T, topo, r, N):
@@ -323,7 +320,7 @@ def main(g, core, T, topo, r, N):
 
     hc = helper_of(core, T, topo)
     qs = [(r + 1 + t) % N for t in range(4)]
-    others = [d for d in range(N) if d != r]
+    others = [(r + o) % N for o in range(1, N)]
     dkey = [("D", 0, 128, 0, 1, 1)]
     own = A("TW", BLK * r + 16, BLK * (r + 1))
     halves = [A("TW", BLK * r + 16 + 2048 * i, BLK * r + 2064 + 2048 * i) for i in range(2)]
@@ -344,7 +341,7 @@ def main(g, core, T, topo, r, N):
                               (A("TP")[1], "dtp", 16, 8.0), (A("SD")[1], "dsd", 16, 8.0), (A("NL", 32 * r, 32 * r + 32)[1], "dnl", 16, 7.0)):
         ext(k, sem, val, when)
 
-    for q in range(N):
+    for q in [r] + others:
         ms(A("TW", BLK * q, BLK * q + 16), -256.0)
     ms(A("cone"), 1.0)
     iota(A("cpi"), [[0, 1]], 0, 1, True)
@@ -393,22 +390,21 @@ def main(g, core, T, topo, r, N):
         for d in others:
             ext(slot("FI", d)[1], "ft%d" % i, N - 1, 3.0 + 0.16 * (y1 - y0), True)
         if i == 0:
-            iota(A("cio"), [[1, 384]], 0, 0)
+            iota(A("cio"), [[1024, 3], [1, NA]], -1024, 0)
     for o in (3, 5, 7):
         remote(own[1], lambda o=o: table_out(T.cores[(r - o) % N], own, "tbx"))
     iota(A("cw0f"), [[0, 16]], -1024, -1)
-    iota(A("cbc"), [[4, 8]], 0, 0)
-    asel(A("ctf"), A("cone"), [[-1, 128]], OP.is_ge, 0.0, 0, 1)
+    iota(A("ctk"), [[16, NC]], 15 - 2048, 0)
+    iota(A("cb3"), [[-240, 8]], 0, 0)
     for q in others:
         ext(A("TW", BLK * q + 16, BLK * (q + 1))[1], *(("tb0", 16, 21.0) if q == qs[0] else ("tbx", 48, 55.0)))
 
     ts(A("cpj"), A("cpi"), 15, None, OP.bitwise_and)
     ts(A("cpq"), A("cpj"), 1, None, OP.arith_shift_right)
-    ts(A("cpt"), A("cpi"), 4, 1, OP.arith_shift_right, OP.bitwise_and)
-    for a, b in (("cj", "cpj"), ("cq", "cpq"), ("cpar", "cpt"), ("cp", "cpi")):
+    for a, b in (("cj", "cpj"), ("cq", "cpq")):
         copy(A(a), A(b))
-    for h in range(2):
-        ts(A("cbb", h, h + 1), A("cp"), -1.0, 383.0 + 128 * h, OP.mult, OP.add)
+    copy(A("cp", 0, 1), A("cpi"))
+    ts(A("cp", 1, 2), A("cpi"), -64.0, None, OP.add)
     ts(A("ceb"), A("cq"), float(BLK), 15.0, OP.mult, OP.add)
     for i, (y0, y1) in enumerate(PARTS):
         ts(A("cs", i, i + 1), A("cq"), 16.0 * (y1 - y0 - 1), None, OP.mult)
@@ -418,88 +414,125 @@ def main(g, core, T, topo, r, N):
     for n, fill, first in (("cmh", 256.0, 0.0), ("cml", 0.0, 255.0), ("ckp", 1.0, 0.0)):
         ms(A(n), fill)
         ms(A(n, 0, 512, 16), first)
-    ms(A("cm0"), 0.0)
+    ms(A("cm0"), -BIG)
     ms(A("cm0", 0, 128, 16), BIG)
-    ms(A("HST"), 0)
-    ms(A("IJ"), 0.0)
-    ts(A("cneg"), A("cone"), -2048.0, None, OP.mult)
-    copy(A("cib"), A("cid"))
-    copy(A("cih"), A("cid"))
-    copy(A("cbm"), A("cio"))
-    ts(A("c2b"), A("cid"), 2.0, None, OP.mult)
-    ts(A("cnb"), A("cid"), -1.0, None, OP.mult)
-    copy(A("cblb"), A("cblk"))
-    ms(A("ZA"), 0.0)
-    ts(A("ZA", 15, 143, 16), A("cg"), 512.0, None, OP.mult)
-    copy(A("cph"), A("cpm"))
-    copy(A("cpb"), A("cpm"))
-    ts(A("cr"), A("cj"), 16.0 * NC, None, OP.mult)
-    ts(A("cr4"), A("cj"), 4.0 * NC, None, OP.mult)
-    for m in range(16):
-        ts(A("SEL", NA * R0 + m, 16 * NA, 16), A("cpb", NC * R0, NA), -1.0, None, OP.mult)
     for h in range(NS):
-        ts(A("cbai_%d" % h), A("cbc"), A("cr4"), 4.0 * NA * h, OP.add, OP.add)
+        ms(A("IJ", 16 * NA * h, 16 * NA * h + NA * R0), 0.0)
+    copy(A("cih"), A("cid"))
+    copy(A("cblh"), A("cblk"))
+    for n, src, w in (("cib", "cid", 1.0), ("c4n", "cid", -4096.0), ("c8i", "cid", 8192.0), ("n8i", "cid", -8192.0),
+                      ("n8b", "cblk", -8192.0), ("chh", "cblk", 16.0), ("chl", "cblk", 0.5), ("cpb", "cpm", 1.0), ("cng", "cg", -1.0)):
+        act(A(n), A(src), AF.Copy, scale=w)
+    for n, w, how in (("ZA", 4096.0, "vs"), ("ZB", 8192.0, "b"), ("ZC", -4096.0, "b")):
+        if any(x[0] in how for x in LOOK):
+            ms(A(n), 0.0)
+            ts(A(n, 15, 143, 16), A("cg"), w, None, OP.mult)
+    ts(A("cr"), A("cj"), 16.0 * NC, None, OP.mult)
+    ts(A("cbm"), A("cio"), A("cr"), None, OP.add)
+    for m in range(16):
+        act(A("SEL", NA * R0 + m, 16 * NA, 16), A("cpb", NC * R0, NA), AF.Copy, scale=-1.0)
     ts(A("cmk"), A("cmi"), A("cj"), None, OP.is_equal)
-    ts(A("cpen"), A("cmk"), -524288.0, 524288.0, OP.mult, OP.add)
-    ms(A("coh", 384, 512), 0.0)
-    ms(A("ck", 0, 128), -131072.0)
-    ms(A("ck", 128, 256), 139264.0)
-    for n, w in (("c8", 8192.0), ("n8", -8192.0)):
-        ts(A(n + "i"), A("cid"), w, None, OP.mult)
-        ts(A(n + "b"), A("cblk"), w, None, OP.mult)
-    ms(A("csn", 0, 128), 0.0)
-    ms(A("csn", 128, 512), 1.0)
-    for k in range(4):
-        ts(A("ctri", 128 * k, 128 * k + 128), A("ctf"), -64.0, None, OP.mult)
-        ts(A("cth", 128 * k, 128 * k + 128), A("ctf"), 64.0, 13.5, OP.mult, OP.add)
-        if k < 3:
-            copy(A("coh", 128 * k, 128 * k + 128), A("cmk"))
-    copy(A("cw0"), A("cw0f"))
-    ts(A("cw1"), A("cw0f"), -128.0, None, OP.add)
+    ts(A("hi", 3, 4), A("cpj"), 3, None, OP.bitwise_and)
+    ts(A("hi", 4, 5), A("cpj"), 2, None, OP.arith_shift_right)
+    ts(A("cs", 2, 3), A("hi", 3, 4), 16.0, None, OP.mult)
+    tt(A("cs", 3, 4), A("cs", 2, 3), A("hi", 4, 5), OP.add)
+    ts(A("PU", 0, NC), A("cbf", 0, NC), 0.25, A("cs", 3, 4), OP.mult, OP.add)
+    ms(A("c4k"), 4096.0)
+    ts(A("cp", 2, 3), A("cj"), float(R0), 1.0, OP.is_lt, OP.add)
+    act(A("c2b"), A("cid"), AF.Copy, scale=A("cp", 2, 3))
+    ms(A("c1"), 1.0)
+    ts(A("cc", 0, 1), A("cj"), -1.0, 1.0, OP.mult, OP.add)
+    ts(A("cc", 1, 2), A("cj"), 2.0, -4096.0, OP.is_lt, OP.mult)
+    ts(A("ctm"), A("cmi"), A("cc", 0, 1), A("cc", 1, 2), OP.not_equal, OP.mult)
+    tt(A("csel"), A("ctm"), A("cblk"), OP.mult)
+    ts(A("cc", 2, 3), A("cj"), 2.0, 1.0 / 64, OP.is_equal, OP.mult)
+    ts(A("cc", 3, 4), A("cj"), 2.0, -1.0 / 64, OP.is_lt, OP.mult)
+    tt(A("cc", 4, 5), A("cc", 2, 3), A("cc", 3, 4), OP.add)
+    ts(A("csq"), A("cblk"), A("cc", 4, 5), None, OP.mult)
+    ts(A("cc", 5, 6), A("cj"), 2.0, 4196352.0, OP.is_ge, OP.mult)
+    ts(A("cc", 6, 7), A("cc", 5, 6), 4196352.0, None, OP.add)
     copy(A("HF"), A("HS"))
-    ts(A("kd"), A("HS"), 1, None, OP.bitwise_and)
     for t in range(4):
-        for i in range(2):
-            ts(A("WH", 16 * t + 8 * i, 16 * t + 8 * i + 8), A("cg"), A("HF", 4 * t + i, 4 * t + i + 1), 0.5, OP.mult, OP.mult)
-        ts(A("th", t, t + 1), A("HF", 4 * t + 3, 4 * t + 4), 512.0, -1.0, OP.mult, OP.add)
-        ts(A("hcol", t, t + 1), A("kd", 4 * t + 2, 4 * t + 3), -2048.0, 4196352.0, OP.mult, OP.add)
-        copy(A("ZZ", 16 * t, 16 * t + 8), A("cg"))
-        ts(A("ZZ", 16 * t + 8, 16 * t + 16), A("cg"), A("HF", 4 * t + 2, 4 * t + 3), None, OP.mult)
-        b = B(5 + t % 2, 0, 128, 1, 16)
-        mm(b, A("ZZ", 16 * t, 16 * t + 16), A("cih"))
-        copy(A("KM", 128 * t, 128 * t + 128, 1, 0, 16), b)
+        w1, w2, k, th = (A("HF", 4 * t + i, 4 * t + i + 1) for i in range(4))
+        c0, c1 = 128 * t, 128 * t + 128
+
+        def col(i, t=t):
+            return A("hs", 8 * t + i, 8 * t + i + 1)
+        tt(col(4), w1, w2, OP.add)
+        ts(A("WX", c0, c1), A("chl"), col(4), None, OP.mult)
+        ts(A("WX", c0, c1, 16), A("cg"), w1, 0.5, OP.mult, OP.mult)
+        ts(A("WX", c0 + 1, c1, 16), A("cg"), w2, 0.5, OP.mult, OP.mult)
+        ts(col(5), col(4), 64.0, None, OP.mult)
+        ts(A("DK"), A("cih"), k, None, OP.mult)
+        b = B(4 + t, 0, 128)
+        mm(b, A("cblh"), A("DK"))
+        ts(A("wx"), b, w2, col(5), OP.mult, OP.add)
+        ts(A("wh"), A("wx"), 5, 127, OP.arith_shift_right, OP.bitwise_and)
+        ts(A("wl"), A("wx"), 31, None, OP.bitwise_and)
+        tt(A("WH", c0, c1), A("wh"), A("chh"), OP.mult)
+        tt(A("WL", c0, c1), A("wl"), A("chl"), OP.mult)
+        sx, sa, sl = (B(4 + t, 128 + i, 129 + i) for i in range(3))
+        mm(sx, A("WX", c0, c1), A("c1", 0, 1))
+        mm(sl, A("WL", c0, c1), A("c1", 0, 1))
+        mm(sa, A("WH", c0, c1), A("c1", 0, 1), True, False)
+        mm(sa, A("WL", c0, c1), A("c1", 0, 1), False, True)
+        ts(col(0), sx, -0.5, 1024.5 + 1.0 / 8192, OP.mult, OP.add)
+        ts(col(1), sx, -2048.0, A("cc", 6, 7), OP.mult, OP.add)
+        ts(A("hi", 0, 1), sl, -2048.0, 2048.0, OP.mult, OP.add)
+        ts(A("hi", 1, 2), A("hi", 0, 1), 4095, None, OP.bitwise_and)
+        ts(col(3), A("hi", 1, 2), -2048.0 - 31.0 / 64, None, OP.add)
+        ts(A("hi", 2, 3), sa, -2303.0 / 4096 / 8, 6100.0 / 8, OP.mult, OP.add)
+        ts(col(6), A("hi", 2, 3), 8.0, None, OP.mult)
+        ts(col(2), sl, 2303.0 / 4096, col(6), OP.mult, OP.add)
+        ts(A("DN", c0, c1), A("cih"), col(6), None, OP.mult)
+        ts(A("th", t, t + 1), th, 4096.0, A("cr"), OP.mult, OP.add)
+        ts(A("THK", 4 * t, 4 * t + NC), A("ctk"), A("th", t, t + 1), None, OP.add)
         x = float(2 * qs[t] + t // N)
         ts(A("ntx", t, t + 1), A("cj"), x, None, OP.not_equal)
-        ts(A("DX", 128 * t, 128 * t + 128), A("cid"), A("ntx", t, t + 1), None, OP.mult)
+        ts(A("xb", t, t + 1), A("cj"), x, 2049.0, OP.is_equal, OP.mult)
+        act(A("DX", c0, c1), A("cid"), AF.Copy, scale=A("ntx", t, t + 1))
         ts(A("XM"), A("cmi"), x, None, OP.is_equal)
-        tt(A("XS", 128 * t, 128 * t + 128), A("XM"), A("cblk"), OP.mult)
-        copy(A("XB", 128 * t, 128 * t + 128), A("XS", 128 * t, 128 * t + 128))
+        tt(A("XS", c0, c1), A("XM"), A("cblk"), OP.mult)
     ts(A("P", 256, 512), A("TP"), 1.0, None, OP.add)
-    ms(A("P", 0, 256), 0.0)
+    for n in ("P", "PW"):
+        ms(A(n, 0, 256), 0.0)
+        ms(A(n, 512, 640), 0.0)
     ts(A("S"), A("SD"), 1.0, None, OP.add)
-    for j in range(16):
-        ts(A("cbt", j, j + 1), A("cj"), float(j), float(2 ** (12 - j)) if j < 13 else (-1.0 if j == 13 else 0.0), OP.is_equal, OP.mult)
-    rec("v", A("cbt")[1], A("csc")[1], lambda: g.vector.tensor_reduce(A("csc")[0], A("cbt")[0], AxisListType.X, OP.add), 0.07)
-    ts(A("cnpar"), A("cpar"), -1.0, 1.0, OP.mult, OP.add)
-    ts(A("cc", 4, 5), A("cj"), 13.0, 1.0 / 2048, OP.is_lt, OP.mult)
-    ts(A("cc", 5, 6), A("cj"), 13.0, 1.0 / 4096, OP.is_equal, OP.mult)
-    tt(A("cc", 6, 7), A("cc", 4, 5), A("cc", 5, 6), OP.add)
-    ts(A("cc", 7, 8), A("cj"), 13.0, -1.0, OP.is_lt, OP.mult)
-    for i, m in ((0, "cnpar"), (1, "cpar")):
-        tt(A("cc", 2 * i, 2 * i + 1), A("cc", 6, 7), A(m), OP.mult)
-        tt(A("cc", 2 * i + 1, 2 * i + 2), A("cc", 7, 8), A(m), OP.mult)
+    for h in range(NS):
+        ts(A("HST", 256 * h + 128, 256 * h + 192), A("cio", NA, 2 * NA), -2.0, -2.0 - 2 * NA * h, OP.mult, OP.add)
+    copy(A("coh"), A("cmk", 0, 16))
+    ts(A("cpen"), A("cmk"), -524288.0, 524288.0, OP.mult, OP.add)
+    ms(A("ck", 0, 128), 0.0)
+    ms(A("ck", 128, 384), 8192.0)
+    ts(A("ctm"), A("cid"), -262144.0, None, OP.mult)
+    tt(A("c8n"), A("ctm"), A("n8b"), OP.subtract)
+    ms(A("csn"), 0.0)
+    ms(A("csn", 256, 512), 1.0)
+    for k in range(8):
+        act(A("GM", NA * k, NA * k + NA), A("cone", 0, NA), AF.Copy, scale=A("cg", k, k + 1))
+        act(A("GN", 128 * k, 128 * k + 128), A("cone"), AF.Copy, scale=A("cng", k, k + 1))
+    for i in range(2):
+        ts(A("CT", 512 * i, 512 * i + NA), A("cio", NA, 2 * NA), A("cp", i, i + 1), 0.5, OP.is_le, OP.mult)
+        for k in (1, 2, 4):
+            act(A("CT", 512 * i + NA * k, 512 * i + 2 * NA * k), A("CT", 512 * i, 512 * i + NA * k), AF.Copy)
+    copy(A("cw0"), A("cw0f"))
+    ts(A("cw1"), A("cw0f"), -128.0, None, OP.add)
+    for u, (b0, b1) in enumerate(UNITS[:-1]):
+        ts(A("cbb", u, u + 1), A("cp", 0, 1), -1.0, 255.0 + b1 - b0, OP.mult, OP.add)
+    n = float(UNITS[-1][1] - UNITS[-1][0])
+    ts(A("cbb", 2, 3), A("cp", 0, 1), -1.0, -1280.0, OP.mult, OP.add)
+    ts(A("cbb", 3, 4), A("cp", 0, 1), -1.0, n - 1024.0, OP.mult, OP.add)
+    ts(A("cc", 7, 8), A("cj"), 16 * (n - 1024.0) - 120.0, None, OP.add)
+    copy(A("cb3h"), A("cb3"))
+    ts(A("cgn"), A("cg"), -1.0, None, OP.mult)
 
     def shape(h):
         return "_%d" % h, NA * h, NA * h + NA, 16 * NA * h
 
-    def place(h, k, p1=128):
-        c = NA + (16 + (k - 1) * NA if k else 0)
-        return B(h, c, c + (NA if k else 16), 1, p1)
-
     def middle(h, t):
         s, a0, a1, x0 = shape(h)
         if t:
-            ts(A("EO", a0, a1), A("P", 256 + a0, 256 + a1), A("ceb"), None, OP.add)
+            ts(A("EO", a0, a1), A("P", 256 + a0, 256 + a1), 0.0, A("ceb"), OP.max, OP.add)
         cut = [a0 + 2 * (NA * k // (2 * len(MID[h]))) for k in range(len(MID[h]) + 1)]
         for k, e in enumerate(MID[h]):
             o, x = cut[k:k + 2], (16 * cut[k], 16 * cut[k + 1])
@@ -513,58 +546,64 @@ def main(g, core, T, topo, r, N):
                 n = min(512, x[1] - c)
                 scan(A("HI", c, c + n), A("cmh", 0, n), A("FA", c, c + n), 0.0, OP.min, OP.max)
                 scan(A("LO", c, c + n), A("cml", 0, n), A("FB", c, c + n), 255.0, OP.max, OP.min)
-        se = place(h, 3)
+        se = B(h, 128, 128 + NA)
         mm(se, A("cib"), A("HI", x0 + 15, x0 + 16 * NA, 16), True, False)
         mm(se, A("cib"), A("LO", x0 + 15, x0 + 16 * NA, 16), False, True)
         ts(A("C", a0, a1), se, 2047.5, None, OP.add)
         ts(A("EB", a0, a1), A("C", a0, a1), 0.5, -1024.0, OP.mult, OP.add)
-        et, ec = B(4 + h, 0, 128, 1, NA), B(4 + h, 128, 128 + NA)
-        mm(et, A("EB", a0, a1), A("cib"))
+
+    def spread(h, step):
+        s, a0, a1, x0 = shape(h)
+        et = B(4 + h, 128, 256, 1, NA)
+        if step == 0:
+            act(A("IJ", x0, x0 + 16 * NA, 16), IND(A("EB", a0, a1), A("PU", 0, NC)), AF.Copy)
+            mm(et, A("EB", a0, a1), A("cib"))
+            return
         act(A("ET" + s, 0, 128, 1, 0, NA), et, AF.Copy)
-        mm(ec, A("ET" + s, 0, 128, 1, 0, NA), A("cpb", 0, NA, 1, 0, NA))
-        act(A("IJ", x0, x0 + 16 * NA, 16), ec, AF.Copy)
         for c in range(x0, x0 + NA * R0, 512):
             n = min(512, x0 + NA * R0 - c)
             scan(A("ER", c, c + n), A("ckp", 0, n), A("IJ", c, c + n), 0.0, OP.mult, OP.add)
 
     def restore(h):
         s, a0, a1, x0 = shape(h)
-        mm(B(4 + h, 0, NA), A("c2b"), A("EB", a0, a1), True, False)
-        for k in range(R0, 16):
-            mm(B(4 + h, k, NA, 16), A("cnb"), A("EB", a0 + k, a1, 16), False, k == 15)
+        mm(B(4 + h, 0, NA), A("ET" + s, 0, 128, 1, 0, NA), A("c2b", 0, NA, 1, 0, NA))
         act(A("E2", a0, a1), B(4 + h, 0, NA), AF.Identity, bias=2047.5)
 
     def hash_(h, p, t):
         s, a0, a1, x0 = shape(h)
-        u = place(h, 0, NA)
-        mm(u, A("cneg", 0, NA), A("WH", 16 * t, 16 * t + 16), True, False)
-        mm(u, A("C", a0, a1), A("WH", 16 * t, 16 * t + 16), False, True)
-
-        def part(n, c0=0, c1=16):
-            return A(n + s, c0, c1, 1, 0, NA)
-        copy(part("UI"), u)
-        ts(part("UA"), part("UI"), 4095, None, OP.bitwise_and)
-        tt(part("VP", 0, 8), part("UA", 0, 8), part("UA", 8, 16), OP.mult)
-        ts(part("UA", 0, 8), part("VP", 0, 8), 5, 4095, OP.arith_shift_right, OP.bitwise_and)
-        ts(part("HB"), part("UA"), -2048.0, None, OP.add)
-        x, y, hh = place(h, 1, 16), A("HX", a0, a1, 1, 0, 16), place(h, 2)
-        mm(x, part("HB"), A("cph", 0, NA, 1, 0, NA))
-        copy(y, x)
-        mm(hh, A("KM", 128 * t, 128 * t + 128, 1, 0, 16), y)
-        ts(A("HN", a0, a1), hh, A("hcol", t, t + 1), None, OP.add)
-        d = A("HST", 4 * a0 + p, 4 * a1, 4)
-        ts(d, A("HN", a0, a1), 4095, None, OP.bitwise_and)
+        c0, c1 = 128 * t, 128 * t + 128
+        x, hh = B(h, NA, 2 * NA), B(4 + h, 0, NA)
+        c, wx, wh, wl, dn = A("C", a0, a1), A("WX", c0, c1), A("WH", c0, c1), A("WL", c0, c1), A("DN", c0, c1)
+        mm(x, wx, c)
+        ts(A("QH" + s), x, 1.0 / 4096, A("hs", 8 * t, 8 * t + 1), OP.mult, OP.add)
+        mm(hh, wh, c)
+        if p == 0:
+            spread(h, 0)
+        act(A("Q3" + s), hh, AF.Identity, bias=A("hs", 8 * t + 2, 8 * t + 3), scale=1.0 / 4096)
+        if p == 0:
+            spread(h, 1)
+        mm(x, wx, c, True, False)
+        mm(x, A("csel"), A("QH" + s), False, True)
+        act(A("SQ" + s), x, AF.Square, bias=A("hs", 8 * t + 1, 8 * t + 2))
+        mm(hh, dn, A("c4k"), True, False)
+        mm(hh, wh, c, False, False)
+        mm(hh, A("c4n"), A("Q3" + s), False, False)
+        mm(hh, wl, c, False, False)
+        mm(hh, A("csq"), A("SQ" + s), False, True)
+        ts(A("HN", a0, a1), hh, A("hs", 8 * t + 3, 8 * t + 4), None, OP.add)
+        k = 4 * a0 + NA * ((p + 3) % 4)
+        d = A("HST", k, k + NA)
+        ts(d, IND(A("HN", a0, a1), A("PU", 0, NC)), 4095, None, OP.bitwise_and)
         copy(A("OF", a0, a1), d)
 
     def look(h, p, t):
         s, a0, a1, x0 = shape(h)
         key, w = B(h, 0, NA), A("TW", BLK * qs[t] + 16, BLK * qs[t] + BLK)
-        mm(key, A("cih"), A("cbm", 128 * p, 128 * p + NA), True, False)
         for i, (how, r0, r1) in enumerate(LOOK):
             x = (x0 + NA * r0, x0 + NA * r1)
             xv, ax = A("XV", *x), A("AX", *x)
             if how == "s":
-                b = B(4 + h, 0, x[1] - x[0])
+                b = B(4 + h, 0, x[1] - x[0]) if i else B(h, 512 - x[1] + x[0], 512)
                 act(xv, IND(w, A("OF", a0 + NC * r0, a0 + NC * r1)), AF.Copy)
                 mm(b, A("ET" + s, 0, 128, 1, 0, NA), A("SEL", NA * r0, NA * r1, 1, 0, NA), True, False)
                 mm(b, A("cib"), xv, False, True)
@@ -574,9 +613,17 @@ def main(g, core, T, topo, r, N):
                     e = min(r1, k + VSUB)
                     y = (x0 + NA * k, x0 + NA * e)
                     tt(A("XV", *y), IND(w, A("OF", a0 + NC * k, a0 + NC * e)), A("ER", *y), OP.subtract)
-                act(ax, xv, AF.Abs)
+                if how == "v":
+                    act(ax, xv, AF.Abs)
+                else:
+                    ts(ax, xv, 0.0, None, OP.max)
+            if i == 0:
+                mm(key, A("cih"), A("cbm", NA * p, NA * p + NA), True, False)
             for k in range(r0, r1):
-                mm(key, A("ZA", 15 - k, 143 - k), A("AX", x0 + NA * k, x0 + NA * k + NA), False, i == len(LOOK) - 1 and k == r1 - 1)
+                if how == "b":
+                    mm(key, A("ZC", 15 - k, 143 - k), A("XV", x0 + NA * k, x0 + NA * k + NA), False, False)
+            for k in range(r0, r1):
+                mm(key, A("ZB" if how == "b" else "ZA", 15 - k, 143 - k), A("AX", x0 + NA * k, x0 + NA * k + NA), False, i == len(LOOK) - 1 and k == r1 - 1)
 
     def winner(h, p, t):
         s, a0, a1, x0 = shape(h)
@@ -584,85 +631,97 @@ def main(g, core, T, topo, r, N):
         if p < 2:
             k = A("KI" + s, 8 * p, 8 * p + NC)
             copy(k, A("SC", a0 + 15, a1, 16))
-            ts(A("J" + s, 0, NC), k, 127, None, OP.bitwise_and)
-            ts(A("JU" + s, 0, NC), A("J" + s, 0, NC), A("cr"), None, OP.add)
+            ts(A("J" + s, 0, NC), k, 1023, None, OP.bitwise_and)
+            copy(A("JU" + s, 0, NC), A("J" + s, 0, NC))
             tt(A("C", a0, a1), IND(A("XV", x0, x0 + 16 * NA), A("JU" + s, 0, NC)), A("E2", a0, a1), OP.add)
         if p == 1:
             tt(A("BA" + s, 0, NC), A("KI" + s, 0, NC), A("KI" + s, 8, 8 + NC), OP.min)
-            ts(A("BB" + s, 0, NC), A("BA" + s, 0, NC), A("th", t, t + 1), None, OP.min)
+            tt(A("BB" + s, 0, NC), A("BA" + s, 0, NC), A("THK", 4 * t, 4 * t + NC), OP.min)
 
     def names(h, t):
         s, a0, a1, x0 = shape(h)
-
-        def part(n):
-            return A(n + s, 0, NC)
-        tt(part("BK"), A("SC", a0 + 15, a1, 16), part("BB"), OP.min)
-        ts(part("MI"), part("BK"), 511, None, OP.bitwise_and)
-        ts(part("PI"), part("BK"), 7, 3, OP.arith_shift_right, OP.bitwise_and)
-        copy(part("L2U"), part("MI"))
-        tt(part("L1"), part("PI"), part("cbai"), OP.add)
-        act(A("OH", a0, a1), IND(A("coh"), part("L2U")), AF.Copy)
-        copy(part("L1U"), part("L1"))
-        tt(A("PR", a0, a1), IND(A("HST"), part("L1U")), A("OH", a0, a1), OP.mult)
-        nrep, ps, c = place(h, 3), B(2 * (a0 // 128), 384 + a0 % 128, 384 + a0 % 128 + NA), 128 - 256 * (a0 // 128)
-        mm(nrep, A("cblb"), A("OH", a0, a1), True, False)
-        mm(nrep, A("cblk"), A("PR", a0, a1), False, True)
-        ts(A("I1", a0, a1), nrep, A("csc"), None, OP.mult)
+        bk, ps = A("BK" + s, 0, NC), B(h, 192, 192 + NA)
+        tt(bk, A("SC", a0 + 15, a1, 16), A("BB" + s, 0, NC), OP.min)
+        ts(A("L" + s, 0, NC), bk, 4, 255, OP.arith_shift_right, OP.bitwise_and)
+        ts(A("L" + s, NC, 2 * NC), bk, 15, None, OP.bitwise_and)
+        copy(A("LU" + s), A("L" + s))
+        ts(A("HG", a0, a1), IND(A("HST", 4 * a0, 4 * a1), A("LU" + s, 0, NC)), -2048.0, None, OP.add)
+        tt(A("PR", a0, a1), IND(A("coh"), A("LU" + s, NC, 2 * NC)), A("HG", a0, a1), OP.mult)
         mm(ps, A("DX", 128 * t, 128 * t + 128), A("P", 256 + a0, 256 + a1), True, False)
-        mm(ps, A("XB", 128 * t, 128 * t + 128), A("OH", a0, a1), False, False)
         mm(ps, A("XS", 128 * t, 128 * t + 128), A("PR", a0, a1), False, True)
-        ts(A("I2", a0, a1), A("I1", a0, a1), 4096, None, OP.bitwise_and)
-        ts(A("BE", a0, a1), A("I2", a0, a1), A("cc", 0, 1), A("cc", 1, 2), OP.mult, OP.add)
-        ts(A("BO", a0, a1), A("I2", a0, a1), A("cc", 2, 3), A("cc", 3, 4), OP.mult, OP.add)
-        act(A("PW", 256 + a0, 256 + a1), ps, AF.Copy)
-        act(A("PW", c + a0, c + a1), ps, AF.Copy)
+        act(A("PW", 256 + a0, 256 + a1), ps, AF.Relu, bias=A("xb", t, t + 1))
+        act(A("PO", a0, a1), ps, AF.Relu, bias=A("xb", t, t + 1))
 
-    def pairs(h):
-        a0, a1, kb = 128 * h, 128 * h + 128, 2 * h + 1
-        ps, low = B(2 * h, 384, 512), B(kb, 0, 128)
-        for i, banks in enumerate(SAME[h]):
-            onv = i == 1
-            tri = i == h and not onv
-            for b in banks if tri else ():
-                mm(B(b), A("cib"), A("ctri"), True, False)
-            for k in (0, 1, 4, 5, 2, 3, 6, 7):
-                src, p0, c = "BE" if k % 2 == 0 else "BO", 32 * (k // 2), 128 * (k % 4)
-                mm(B(banks[k // 4], c, c + 128), A(src, 128 * i, 128 * i + 128, 1, p0, p0 + 32), A(src, a0, a1, 1, p0, p0 + 32), not tri, not tri or k % 4 == 3)
-            for j, b in enumerate(banks):
-                o = A(("QA", "QX", "QB")[h + i], 512 * j, 512 * j + 512)
-                if onv:
-                    tt(o, B(b), A("cth"), OP.is_ge)
-                else:
-                    act(o, B(b), AF.Relu, bias=-13.0)
-        mm(low, A("cib"), A("cpen"), True, False)
-        for i in range(h + 1):
+    def blocks(h):
+        return [(i, min(128, NA * h + NA - 128 * i)) for i in range(h // 2 + 1)]
+
+    def compare(h):
+        s, a0, a1, x0 = shape(h)
+        for i, na in blocks(h):
+            bank, how, tri = (4 + h, 2 + h)[i], SAME[h][i], i == h // 2
+            d, ct = B(bank, 0, 512, 1, na), A("CT", 512 * (h % 2), 512 * (h % 2) + 512, 1, 0, na)
+            if tri and how != "v":
+                mm(d, A("cib", 0, na, 1, 0, na), ct, True, False)
+            mm(d, A("PR", 128 * i, 128 * i + na), A("GM"), not tri or how == "v", False)
             for k in range(8):
-                mm(B(kb, 16 * k, 16 * k + 16), A(("QA", "QX", "QB")[h + i], 128 * k, 128 * k + 128), A("cw%d" % i), False, k == 7 and i == h)
-        la, lt, ls, lu = A("LA", a0, a1), A("LT", a0, a1), B(kb, 128, 136), A("LSU", 8 * h, 8 * h + 8)
-        act(la, low, AF.Abs, bias=1279.0)
-        act(lt, la, AF.Relu, bias=A("cbb", h, h + 1), scale=-1.0)
-        mm(ls, A("cid"), A("cb2", 0, 8), True, False)
-        mm(ls, lt, A("cg"), False, True)
-        copy(lu, ls)
-        q, sn, mn, t2, nd, pn, qn, pc, s1, p1 = (A(n, a0, a1) for n in ("Q", "SN", "MN", "TT", "ND", "PN", "QN", "PC", "SX", "SP"))
-        ne, yes, no = (B(kb, 128 * k, 128 * k + 128) for k in range(3))
-        copy(q, IND(A("PW", 256 - a1, 256 + a1), lu))
-        act(sn, IND(A("csn"), lu), AF.Copy)
-        tt(ne, ps, q, OP.not_equal)
-        tt(mn, ps, q, OP.min)
-        tt(t2, ne, mn, OP.mult)
-        ts(nd, t2, 0.0, None, OP.is_le)
-        for o, w, c in ((yes, "c8", 0), (no, "n8", 128)):
-            mm(o, A("cib"), A("ck", c, c + 128), True, False)
-            mm(o, A(w + "i"), sn, False, False)
-            mm(o, A(w + "b"), nd, False, True)
-        tt(pn, ps, nd, OP.mult)
-        tt(qn, q, nd, OP.mult)
+                mm(B(bank, NA * k, NA * k + NA, 1, na), A("GN", 128 * k, 128 * k + na), A("PR", a0, a1), False, k == 7)
+            o, z = A(("QA", "QB")[i] + s, 0, 512, 1, 0, na), A("QZ", 512 * i, 512 * i + 512, 1, 0, na)
+            if how != "v":
+                act(z, d, AF.Abs)
+                if how == "s":
+                    act(o, z, AF.Relu, bias=1.0, scale=-2.0)
+                else:
+                    ts(o, z, 0.0, None, OP.is_equal)
+            elif tri:
+                tt(o, d, ct, OP.is_equal)
+            else:
+                ts(o, d, 0.0, None, OP.is_equal)
+
+    def pairs(u):
+        a0, a1 = UNITS[u]
+        n, kb, last = a1 - a0, a1 // NA - 1, u == len(UNITS) - 1
+        low = B(kb, 0, 128, 1, n)
+        for h in range(a0 // NA, a1 // NA):
+            p0, todo = NA * h - a0, [(i, na, k) for i, na in blocks(h) for k in range(8)]
+            mm(A("B%d" % kb, 0, 128, 1, p0, p0 + NA), A("cib", 0, NA), A("cpen"), True, False)
+            for i, na, k in todo:
+                mm(A("B%d" % kb, 16 * k, 16 * k + 16, 1, p0, p0 + NA), A(("QA_%d", "QB_%d")[i] % h, NA * k, NA * k + NA, 1, 0, na), A("cw%d" % i, 0, 16, 1, 0, na),
+                   False, (i, na, k) == todo[-1])
+        ls, lu = B(kb, 384, 384 + n // 16), A("LS_%d" % u, 0, n // 16)
+        if last:
+            lt = A("LH", 0, 128, 1, 0, n)
+            ts(lt, low, A("cbb", 2, 3, 1, 0, n), A("cbb", 3, 4, 1, 0, n), OP.max, OP.min)
+            mm(ls, A("cih"), A("cb3h", 0, n // 16), True, False)
+            mm(ls, lt, A("cgn", 0, n // 16, 1, 0, n), False, True)
+            ts(lu, ls, A("cc", 7, 8), None, OP.add)
+        else:
+            la, lt = A("LA", 0, 128, 1, 0, n), A("LT", 0, 128, 1, 0, n)
+            act(la, low, AF.Abs, bias=1279.0)
+            act(lt, la, AF.Relu, bias=A("cbb", u, u + 1, 1, 0, n), scale=-1.0)
+            mm(ls, A("cid"), A("cb2", 0, n // 16), True, False)
+            mm(ls, lt, A("cg", 0, n // 16, 1, 0, n), False, True)
+            copy(lu, ls)
+        w = (256 - n, 512 + n if last else 256 + a1)
+        q, sn, ne, mn, cl, qn, pc, p1 = (A(x, a0, a1) for x in ("Q", "SN", "NE", "MN", "CL", "QN", "PC", "SP"))
+        p = A("PO", a0, a1)
+        yes, no, free, s1 = (B(kb, c, c + n) for c in (0, n, 2 * n, 384))
+        act(sn, IND(A("csn", *w), lu), AF.Copy)
+        act(q, IND(A("PW", *w), lu), AF.Copy)
+        tt(ne, IND(A("PW", *w), lu), p, OP.not_equal)
+        tt(mn, IND(A("PW", *w), lu), p, OP.min)
+        tt(cl, ne, mn, OP.min)
+        mm(B(kb, 0, 3 * n), A("cib"), A("ck", 128 - n, 128 + 2 * n), True, False)
+        mm(yes, A("c8i"), sn, False, False)
+        mm(no, A("n8i"), sn, False, False)
+        mm(yes, A("n8b"), cl, False, False)
+        mm(no, A("c8n"), cl, False, False)
+        mm(free, A("n8i"), cl, False, True)
         tt(s1, yes, A("S", a0, a1), OP.min)
-        tt(p1, no, pn, OP.min)
-        tt(pc, yes, A("PW", 256 + a0, 256 + a1), OP.min)
+        tt(p1, no, p, OP.min)
+        tt(qn, free, q, OP.min)
+        tt(pc, yes, p, OP.min)
         tt(A("P", 256 + a0, 256 + a1), s1, p1, OP.max)
-        tt(IND(A("P", 256 - a1, 256 + a1), lu), qn, pc, OP.max)
+        tt(IND(A("P", *w), lu), qn, pc, OP.max)
 
     for t in range(4):
         for h in range(NS):
@@ -680,10 +739,12 @@ def main(g, core, T, topo, r, N):
                     look(h, p + 1, t)
                 else:
                     names(h, t)
-                    if h % 2:
-                        lead[0] = 1
-                        pairs(h // 2)
-    ts(A("YO"), A("P", 256, 512), -1.0, None, OP.add)
+                    compare(h)
+                    for u, (b0, b1) in enumerate(UNITS):
+                        if b1 == NA * h + NA:
+                            lead[0] = 1
+                            pairs(u)
+    ts(A("YO"), A("P", 256, 512), 0.0, -1.0, OP.max, OP.add)
 
     for o in schedule(ops):
         o[3]()

from concourse.bass import DstId, RemoteDMATransfer
from concourse.mybir import AluOpType as OP, ActivationFunctionType as AF

BLK = 4112
NS, NC, NA = 4, 4, 64
LOOK = (("s", 9, 13), ("v", 0, 5), ("s", 13, 16), ("v", 5, 9))
R0 = max(x[2] for x in LOOK if x[0] != "s")
VSUB = 8
MID = ("vs", "sv", "vs", "sv")
PARTS = ((0, 16), (16, 32))
UNITS = ((0, 128), (128, 256))
SAME = ("v", "v", "sv", "vv")
BIG = 16777216.0
LAT, CY, GA, TF, SMALL, ROUNDS, SKEW, BONUS = 0.25, 0.001, 1.56, 0.65, 0.22, 2, 1.1, 2.0
CHOSEN = []
F32, BF, I32, U16, F16 = "float32", "bfloat16", "int32", "uint16", "float16"

SCRATCH = {"TW": ("sbuf", [128, 8 * BLK], BF), "D": ("dram", [8, 128, 32], I32)}
WIDTH, PLACE, TWO, _used = {"TW": 8 * BLK, "D": 1}, {}, {"TW", "FO", "FI"}, {}
for _n, _w, _d in (("NL", 256, I32), ("HT", 4, I32), ("HS", 16, I32), ("FO", 4096, BF), ("FI", 4096, BF), ("P", 640, F32), ("TP", 256, I32), ("SD", 256, I32), ("YO", 256, F32)):
    SCRATCH[_n], WIDTH[_n] = ("sbuf", [128, _w], _d), _w
for _k in range(8):
    SCRATCH["B%d" % _k], WIDTH["B%d" % _k] = ("psum", [128, 512], F32), 512
SPEC = ((BF, 1, "ET 128 Q3 64 QA 512 QB 512"), (F16, 1, "QH 64"), (U16, 1, "JU 8 LU 8 LS 8"), (I32, 1, "KI 16 J 8 BA 8 BB 8 BK 8 L 8"), (F32, 1, "SQ 64"),
        (F32, 0, "E2 256 SC 256 LA 128 LT 128 Q 256 QN 256 SP 256 PW 640 PO 256 PC 256 S 256 HF 16 cone 128 cid 128 cb1 128 cblk 128 "
                 "cg1 8 cg 8 cmi 128 cmk 128 cm0 128 cj 1 cq 1 cs 4 cp 3 cbb 4 ceb 1 clb 4 cb2 16 cbf 16 clc 256 cw0f 16 cc 8 ntx 4 XM 128 DX 512 "
                 "th 4 THK 16 ctk 4 cio 192 cpm 64 cr 1 hs 32 xb 4 csq 128 ctm 128 chh 128 chl 128 cb3 8 cng 8"),
        (I32, 0, "HST 1024 HN 256 cpi 1 cpj 1 cpq 1 wx 128 wh 128 wl 128 hi 8"),
        (BF, 0, "FA 4096 FB 4096 HI 4096 LO 4096 IJ 4096 ER 4096 XV 4096 AX 4096 EB 256 NE 256 MN 256 CL 256 SN 256 c8i 128 n8i 128 n8b 128 c8n 128 ck 384 "
                "cib 128 c2b 128 cnb 128 cmh 512 cml 512 ckp 512 cpen 128 csn 640 coh 16 ZA 144 ZB 144 ZC 144 cpb 64 SEL 1024 c4n 128 CT 1024 GM 512 GN 1024 QZ 1024"),
        (U16, 0, "NO 256 EO 256 LC 256 OF 256 PU 4"),
        (F16, 0, "C 256 HG 256 PR 256 LH 128 cw0 16 cw1 16 cih 128 cbm 192 WX 512 WH 512 WL 512 DN 512 DK 128 XS 512 c4k 64 cz 64 csel 128 cblh 128 cgn 8 cb3h 8 c1 2"))
ARENA = {F32: "af", BF: "ab", I32: "ai", U16: "au", F16: "ah"}
for _d, _each, _s in SPEC:
    _it = _s.split()
    for _n, _w in zip(_it[::2], _it[1::2]):
        for _t in (["_%d" % _k for _k in range(NS)] if _each else [""]):
            _a, _step = ARENA[_d], 16 if _d in (F32, I32) else 32
            PLACE[_n + _t], WIDTH[_n + _t] = (_a, _used.get(_a, 0)), int(_w)
            _used[_a] = _used.get(_a, 0) - (-int(_w) // _step) * _step
            if _step == 32:
                TWO.add(_n + _t)
for _d in ARENA:
    SCRATCH[ARENA[_d]] = ("sbuf", [128, _used[ARENA[_d]]], _d)
SEMAPHORES = ["qv", "qs", "qt", "qg", "stg", "dt0", "dt1", "dhw", "dtp", "dsd", "dnl", "dyp", "nm", "hs", "ft0", "ft1", "tb0", "tbx", "rel0", "rel1", "loc"]


def helper_of(rc, T, topo):
    for c in topo.cores_of(rc):
        if topo.die(c) != topo.die(rc) and c not in T.cores and all(topo.may_write(c, d) for d in T.cores if d != rc):
            return c
    return None


def send(g, T, topo, core, dst, out, in_, rsem, engines=None):
    rid, pid = topo.addr(dst, core)
    eng = topo.engines(core, dst) if engines is None else engines
    m = 0
    for e in eng:
        m |= 1 << e
    g.remote_dma(out, in_, T.sem[rsem], T.sem.loc, pid, rid, m)
    return len(eng)


def relay_engines(rc, hc, topo, T):
    off = topo.engines(rc, T.cores[0] if T.cores[0] != rc else T.cores[1])
    e = [x for x in topo.engines(rc, hc) if x not in off]
    return e if len(e) in (1, 2, 4, 8, 16) else topo.engines(rc, hc)


def rank_program(g, core, T, topo):
    N = len(T.cores)
    r = T.rank_of(core)
    if r is not None:
        main(g, core, T, topo, r, N)
        return
    for s in range(N):
        if helper_of(T.cores[s], T, topo) == core:
            blk = T.TW[:, BLK * s + 16:BLK * (s + 1)]
            tot = 0
            for i in range(2):
                half = T.TW[:, BLK * s + 16 + 2048 * i:BLK * s + 2064 + 2048 * i]
                g.wait_ge(T.sem["rel%d" % i], len(relay_engines(T.cores[s], core, topo, T)))
                tot += send(g, T, topo, core, T.cores[(s - 1) % N], half, half, "tb0")
            for o in (2, 4, 6):
                tot += send(g, T, topo, core, T.cores[(s - o) % N], blk, blk, "tbx")
            g.wait_ge(T.sem.loc, tot)


def is_bank(n):
    return n[0] == "B" and n[1:].isdigit()


def overlap(x, y):
    if x[1] >= y[2] or y[1] >= x[2] or x[3] >= y[4] or y[3] >= x[4]:
        return False
    return not (x[5] == y[5] and x[5] > 1 and (x[3] - y[3]) % x[5])


def covers(x, y):
    return x[5] == 1 and x[1] <= y[1] and x[2] >= y[2] and x[3] <= y[3] and x[4] >= y[4]


def depends(ops):
    preds, acc, runs, lastg = [set() for _ in ops], {}, {}, None
    for i, (q, rd, wr) in enumerate(o[:3] for o in ops):
        if q == "g":
            if lastg is not None:
                preds[i].add(lastg)
            lastg = i
        for keys, w in ((rd, False), (wr, True)):
            for x in keys:
                lst = acc.setdefault(x[0], [])
                if is_bank(x[0]):
                    run = runs.setdefault(x[0], [q, [], []])
                    if run[0] != q:
                        run[:] = [q, [e[2] for e in run[2]][-1:] if run[0] == "t" else [e[2] for e in run[2]], []]
                    preds[i].update(run[1])
                    preds[i].update([e[2] for e in run[2]][-1:] if q == "t" else [e[2] for e in run[2] if (w or e[1]) and overlap(x, e[0])])
                    run[2].append((x, w, i))
                    continue
                preds[i].update(e[2] for e in lst if (w or e[1]) and overlap(x, e[0]))
                acc[x[0]] = [e for e in lst if not (w and covers(x, e[0]))] + [(x, w, i)]
        preds[i].discard(i)
    return preds


def schedule(ops):
    n = len(ops)
    preds, succs = depends(ops), [[] for _ in ops]
    if CHOSEN and len(CHOSEN[0]) == n:
        place = {j: k for k, j in enumerate(CHOSEN[0])}
        if all(place[j] < place[i] for i in range(n) for j in preds[i]):
            return [ops[i] for i in CHOSEN[0]]
    for i in range(n):
        for j in preds[i]:
            succs[j].append(i)
    queue, cost = [o[0] for o in ops], [o[4] for o in ops]

    def lat(i, k):
        if queue[k] == "t" == queue[i]:
            return LAT if ops[i][2][0][6:] != ops[k][2][0][6:] else 0.0
        return 0.0 if "x" in (queue[i], queue[k]) else LAT

    def pack(turns, before, earliest):
        start, fin, busy = [0.0] * n, [0.0] * n, {}
        for i in turns:
            q, t = queue[i], max([earliest[i]] + [fin[k] + lat(i, k) for k in before[i]])
            if q != "x":
                s = busy.setdefault(q, [])
                lo, hi = 0, len(s)
                while lo < hi:
                    mid = (lo + hi) // 2
                    if s[mid][1] <= t:
                        lo = mid + 1
                    else:
                        hi = mid
                while lo < len(s) and s[lo][0] < t + cost[i]:
                    t = max(t, s[lo][1])
                    lo += 1
                s.insert(lo, (t, t + cost[i]))
            start[i], fin[i] = t, t + cost[i]
        return start, fin

    prio = [0.0] * n
    for i in range(n - 1, -1, -1):
        prio[i] = cost[i] + max([prio[j] + lat(i, j) for j in succs[i]] + [0.0])
    first, none = [o[5] for o in ops], [0.0] * n
    urge = [p + SKEW * o[6] + BONUS * (o[4] < SMALL) for p, o in zip(prio, ops)]
    left = [len(p) for p in preds]
    start, fin, free = [0.0] * n, [0.0] * n, {}
    ready = {i: first[i] for i in range(n) if not left[i]}
    while ready:
        t0, _, i = min((max(ready[i], free.get(queue[i], 0.0)), -urge[i], i) for i in ready)
        del ready[i]
        start[i], fin[i] = t0, t0 + cost[i]
        if queue[i] != "x":
            free[queue[i]] = fin[i]
        for j in succs[i]:
            left[j] -= 1
            if not left[j]:
                ready[j] = max([first[j]] + [fin[k] + lat(j, k) for k in preds[j]])
    best = (max(fin), start)
    for _ in range(ROUNDS):
        start, fin = pack(sorted(range(n), key=lambda i: (-fin[i], -start[i], -i)), succs, none)
        start, fin = pack(sorted(range(n), key=lambda i: (-fin[i], -start[i], i)), preds, first)
        best = min(best, (max(fin), start))
    CHOSEN[:] = [sorted(range(n), key=lambda i: (best[1][i], i))]
    return [ops[i] for i in CHOSEN[0]]


def main(g, core, T, topo, r, N):
    eng = {"v": g.vector, "s": g.scalar, "t": g.tensor, "g": g, "y": g.sync}
    qsem = {"v": "qv", "s": "qs", "t": "qt", "g": "qg"}
    cnt = {"v": 0, "s": 0, "t": 0, "g": 0}
    known = {q: {} for q in eng}
    snaps, acc, ops, lead = {}, {}, [], [0]

    def need(q, sem, val):
        k = known[q]
        if k.get(sem, 0) >= val:
            return
        eng[q].wait_ge(T.sem[sem], val)
        for s, v in snaps.get((sem, val), {}).items():
            if k.get(s, 0) < v:
                k[s] = v
        k[sem] = val

    def order(q, reads, writes):
        todo = {}
        for keys, w in ((reads, False), (writes, True)):
            for x in keys:
                keep = []
                for e in acc.get(x[0], []):
                    y, ew, eq, sem, val = e
                    if is_bank(x[0]):
                        hit = eq != q or ((ew or w) and overlap(x, y) if q != "t" else x[6:] != y[6:])
                        drop = eq != q
                    else:
                        hit = (ew or w) and overlap(x, y)
                        drop = w and covers(x, y)
                    if hit and todo.get(sem, 0) < val:
                        todo[sem] = val
                    if not drop:
                        keep.append(e)
                acc[x[0]] = keep
        for sem in sorted(todo, key=lambda s: (s == qsem.get(q), s)):
            need(q, sem, todo[sem])

    def note(q, reads, writes, sem, val):
        for keys, w in ((reads, False), (writes, True)):
            for x in keys:
                lst = acc.setdefault(x[0], [])
                lst[:] = [e for e in lst if not (e[0] == x and e[1] == w and e[2] == q and e[3] == sem)]
                lst.append((x, w, q, sem, val))
        snaps[(sem, val)] = dict(known.get(q, {}))

    def rec(q, rd, wr, call, cost):
        def emit():
            order(q, rd, wr)
            i = call()
            if i is not None:
                cnt[q] += 1
                i.then_inc(T.sem[qsem[q]], 1)
                note(q, rd, wr, qsem[q], cnt[q])
        ops.append([q, rd, wr, emit, cost, 0.0, lead[0]])

    def ext(writes, sem, val, when, after=False):
        if after:
            ops.append(["x", [(sem, 0, 1, 0, 1, 1)], writes, lambda: note("ext", [], writes, sem, val), when, 0.0, 0])
        else:
            ops.append(["x", [], writes, lambda: note("ext", [], writes, sem, val), 0.01, when, 0])

    def A(n, c0=0, c1=None, st=1, p0=0, p1=128):
        c1 = WIDTH[n] if c1 is None else c1
        b, o = PLACE.get(n, (n, 0))
        return (T[b][p0:p1, o + c0:o + c1] if st == 1 else T[b][p0:p1, o + c0:o + c1:st], [(n, p0, p1, c0, c1, st)], -(-(c1 - c0) // st))

    def B(k, c0=0, c1=512, st=1, p1=128):
        return A("B%d" % k, c0, c1, st, 0, p1)

    def IND(w, o):
        return (w[0].indirect(o[0]), w[1] + o[1], 16 * o[2], True)

    def vcost(out, ins, per=None):
        if any(len(o) > 3 for o in [out] + ins):
            return 0.05 + CY * (3.8 if len(out) > 3 else GA) * out[2]
        if per is None:
            per = 0.5 if all(o[1][0][0] in TWO for o in [out] + ins) else 1
        return CY * max(64.0, per * out[2])

    def copy(out, in_):
        rec("v", in_[1], out[1], lambda: g.vector.tensor_copy(out[0], in_[0]), vcost(out, [in_]))

    def tt(out, a, b, o):
        wr, rd = out[1], a[1] + b[1]
        if len(out) > 3:
            wr, rd = out[1][:1], rd + out[1]
        two = not (is_bank(a[1][0][0]) or is_bank(b[1][0][0]))
        rec("v", rd, wr, lambda: g.vector.tensor_tensor(out[0], a[0], b[0], o), vcost(out, [a, b], 2 if two else 1))

    def ts(out, a, s1, s2, o1, o2=None):
        rd = a[1] + [k for s in (s1, s2) if isinstance(s, tuple) for k in s[1]]
        v1 = s1[0] if isinstance(s1, tuple) else s1
        v2 = s2[0] if isinstance(s2, tuple) else s2
        if o2 is None:
            rec("v", rd, out[1], lambda: g.vector.tensor_scalar(out[0], a[0], v1, v2, o1), vcost(out, [a]))
        else:
            rec("v", rd, out[1], lambda: g.vector.tensor_scalar(out[0], a[0], v1, v2, o1, o2), vcost(out, [a]))

    def scan(out, d0, d1, init, o1, o2):
        rec("v", d0[1] + d1[1], out[1], lambda: g.vector.tensor_tensor_scan(out[0], d0[0], d1[0], init, o1, o2), vcost(out, [d0, d1]))

    def act(out, in_, f, **kw):
        c = 0.065 + CY * GA * out[2] if len(in_) > 3 else CY * max(64.0, out[2])
        rd = in_[1] + [k for s in kw.values() if isinstance(s, tuple) for k in s[1]]
        kw = {k: s[0] if isinstance(s, tuple) else s for k, s in kw.items()}
        rec("s", rd, out[1], lambda: g.scalar.activation(out[0], in_[0], f, **kw), c)

    def mm(out, l, rh, start=True, stop=True):
        c = TF * CY * max(min(64, l[2]), out[2]) * (1 if l[1][0][0] in TWO else 4)
        rec("t", l[1] + rh[1], [out[1][0] + l[1][0][1:3]], lambda: g.tensor.matmul(out[0], l[0], rh[0], start, stop), c)

    def ms(out, c):
        rec("v", [], out[1], lambda: g.vector.memset(out[0], c), vcost(out, []))

    def iota(out, pat, base, cm, exact=False):
        if exact:
            rec("g", [], out[1], lambda: g.iota(out[0], pat, base, cm), 0.15 + 0.002 * out[2])
        else:
            rec("g", [], out[1], lambda: g.iota(out[0], pat, base, cm, allow_small_or_imprecise_dtypes=True), 0.15 + 0.002 * out[2])

    def asel(out, in_, pat, cmp, fill, base, cm):
        rec("g", in_[1], out[1], lambda: g.affine_select(out[0], in_[0], pat, cmp, fill, base, cm), 0.2 + 0.002 * out[2])

    def remote(rd, f, sem=None):
        rec("g", rd, [], lambda: f(), 1.0)
        if sem:
            ops[-1][2] = [(sem, 0, 1, 0, 1, 1)]

    hc = helper_of(core, T, topo)
    qs = [(r + 1 + t) % N for t in range(4)]
    others = [(r + o) % N for o in range(1, N)]
    dkey = [("D", 0, 128, 0, 1, 1)]
    own = A("TW", BLK * r + 16, BLK * (r + 1))
    halves = [A("TW", BLK * r + 16 + 2048 * i, BLK * r + 2064 + 2048 * i) for i in range(2)]
    tot_loc = [0]

    for k in range(8):
        for i, (y0, y1) in enumerate(PARTS):
            (g.sync if (k + i) % 2 == 0 else g.scalar).dma_start(T.D[:, 16 * k:16 * k + 16, y0:y1], T.tp[16 * k:16 * k + 16, 8 * y0:8 * y1]).then_inc(T.sem.stg, 16)
    g.sync.dma_start(halves[0][0], T.tz[:, 0:2048]).then_inc(T.sem.dt0, 16)
    g.scalar.dma_start(halves[1][0], T.tz[:, 2048:4096]).then_inc(T.sem.dt1, 16)
    g.scalar.dma_start(T.HT[:, 0:3], T.hw[:]).then_inc(T.sem.dhw, 16)
    g.scalar.dma_start(T.HT[:, 3:4], T.th[:]).then_inc(T.sem.dhw, 16)
    need("y", "stg", 128 * len(PARTS))
    g.sync.dma_start(T.NL[:, 32 * r:32 * r + 32], T.D[r]).then_inc(T.sem.dnl, 16)
    g.sync.dma_start(T.TP[:], T.tp[:]).then_inc(T.sem.dtp, 16)
    g.sync.dma_start(T.SD[:], T.sd[:]).then_inc(T.sem.dsd, 16)
    for k, sem, val, when in ((dkey, "stg", 128 * len(PARTS), 4.0), (A("HT")[1], "dhw", 32, 4.0), (halves[0][1], "dt0", 16, 5.0), (halves[1][1], "dt1", 16, 6.5),
                              (A("TP")[1], "dtp", 16, 8.0), (A("SD")[1], "dsd", 16, 8.0), (A("NL", 32 * r, 32 * r + 32)[1], "dnl", 16, 7.0)):
        ext(k, sem, val, when)

    for q in [r] + others:
        ms(A("TW", BLK * q, BLK * q + 16), -256.0)
    ms(A("cone"), 1.0)
    iota(A("cpi"), [[0, 1]], 0, 1, True)
    iota(A("cmi"), [[0, 8], [1, 16]], 0, 0)
    iota(A("cbf"), [[16, 16]], 0, 0)
    asel(A("cid"), A("cone"), [[-1, 128]], OP.is_equal, 0.0, 0, 1)
    asel(A("cg1"), A("cone", 0, 8), [[-16, 8]], OP.is_ge, 0.0, 0, 1)
    asel(A("cg"), A("cg1"), [[16, 8]], OP.is_ge, 0.0, 15, -1)

    def fused(pairs, rsem):
        tr = []
        for i, (d, src, dst) in enumerate(pairs):
            rid, pid = topo.addr(T.cores[d], core)
            e = topo.engines(core, T.cores[d])
            tr.append(RemoteDMATransfer(dst_ids=[DstId(rid=rid, pnc=pid)], dma_engine_mask=1 << e[i % len(e)], remote_sem=T.sem[rsem], srcs=[src], dsts=[dst]))
        g.remote_dma_fused(tr, local_sem=T.sem.loc)
        tot_loc[0] += len(tr)

    def table_out(d, x, rsem, engines=None):
        tot_loc[0] += send(g, T, topo, core, d, x[0], x[0], rsem, engines)

    remote(dkey, lambda: fused([(d, T.D[d], T.NL[:, 32 * r:32 * r + 32]) for d in others], "nm"), "nm")
    for d in others:
        ext(A("NL", 32 * d, 32 * d + 32)[1], "nm", N - 1, 3.0, True)
    for i in range(2):
        remote(halves[i][1], lambda i=i: table_out(hc, halves[i], "rel%d" % i, relay_engines(core, hc, topo, T)))
    remote(A("HT")[1], lambda: fused([((r - 1 - t) % N, T.HT[:], T.HS[:, 4 * t:4 * t + 4]) for t in range(4)], "hs"), "hs")
    ext(A("HS")[1], "hs", 4, 3.0, True)
    for y0, y1 in PARTS:
        iota(A("clc", 8 * y0, 8 * y1), [[1, 8], [16, y1 - y0]], 128 * y0, 0)
    asel(A("cpm"), A("cone", 0, NA), [[-1, 16], [-16, NC]], OP.is_equal, 0.0, 0, 1)
    asel(A("cb1"), A("cone"), [[-16, 8], [0, 16]], OP.is_ge, 0.0, 0, 1)
    asel(A("cblk"), A("cb1"), [[16, 8], [0, 16]], OP.is_ge, 0.0, 15, -1)
    ts(A("NO"), A("NL"), 16.0, None, OP.add)
    win = A("TW", BLK * r, BLK * (r + 1))
    for i, (y0, y1) in enumerate(PARTS):
        def slot(n, d, y0=y0, y1=y1):
            return A(n, 128 * y0 + 16 * (y1 - y0) * d, 128 * y0 + 16 * (y1 - y0) * (d + 1))
        for k, d in enumerate(others + [r]):
            o, a = slot("FI" if d == r else "FO", d), IND(win, A("NO", 32 * d + y0, 32 * d + y1))
            if k % 2:
                copy(o, a)
            else:
                act(o, a, AF.Copy)
        remote([k for d in others for k in slot("FO", d)[1]], lambda slot=slot, i=i: fused([(d, slot("FO", d)[0], slot("FI", r)[0]) for d in others], "ft%d" % i), "ft%d" % i)
        for d in others:
            ext(slot("FI", d)[1], "ft%d" % i, N - 1, 3.0 + 0.16 * (y1 - y0), True)
        if i == 0:
            iota(A("cio"), [[1024, 3], [1, NA]], -1024, 0)
    for o in (3, 5, 7):
        remote(own[1], lambda o=o: table_out(T.cores[(r - o) % N], own, "tbx"))
    iota(A("cw0f"), [[0, 16]], -1024, -1)
    iota(A("ctk"), [[16, NC]], 15 - 2048, 0)
    iota(A("cb3"), [[-240, 8]], 0, 0)
    for q in others:
        ext(A("TW", BLK * q + 16, BLK * (q + 1))[1], *(("tb0", 16, 21.0) if q == qs[0] else ("tbx", 48, 55.0)))

    ts(A("cpj"), A("cpi"), 15, None, OP.bitwise_and)
    ts(A("cpq"), A("cpj"), 1, None, OP.arith_shift_right)
    for a, b in (("cj", "cpj"), ("cq", "cpq")):
        copy(A(a), A(b))
    copy(A("cp", 0, 1), A("cpi"))
    ts(A("cp", 1, 2), A("cpi"), -64.0, None, OP.add)
    ts(A("ceb"), A("cq"), float(BLK), 15.0, OP.mult, OP.add)
    for i, (y0, y1) in enumerate(PARTS):
        ts(A("cs", i, i + 1), A("cq"), 16.0 * (y1 - y0 - 1), None, OP.mult)
        ts(A("clb", i, i + 1), A("cj"), 8.0, A("cs", i, i + 1), OP.mult, OP.add)
        ts(A("LC", 8 * y0, 8 * y1), A("clc", 8 * y0, 8 * y1), A("clb", i, i + 1), None, OP.add)
    ts(A("cb2"), A("cbf"), A("cj"), None, OP.add)
    for n, fill, first in (("cmh", 256.0, 0.0), ("cml", 0.0, 255.0), ("ckp", 1.0, 0.0)):
        ms(A(n), fill)
        ms(A(n, 0, 512, 16), first)
    ms(A("cm0"), -BIG)
    ms(A("cm0", 0, 128, 16), BIG)
    for h in range(NS):
        ms(A("IJ", 16 * NA * h, 16 * NA * h + NA * R0), 0.0)
    copy(A("cih"), A("cid"))
    copy(A("cblh"), A("cblk"))
    for n, src, w in (("cib", "cid", 1.0), ("c4n", "cid", -4096.0), ("c8i", "cid", 8192.0), ("n8i", "cid", -8192.0),
                      ("n8b", "cblk", -8192.0), ("chh", "cblk", 16.0), ("chl", "cblk", 0.5), ("cpb", "cpm", 1.0), ("cng", "cg", -1.0)):
        act(A(n), A(src), AF.Copy, scale=w)
    for n, w, how in (("ZA", 4096.0, "vs"), ("ZB", 8192.0, "b"), ("ZC", -4096.0, "b")):
        if any(x[0] in how for x in LOOK):
            ms(A(n), 0.0)
            ts(A(n, 15, 143, 16), A("cg"), w, None, OP.mult)
    ts(A("cr"), A("cj"), 16.0 * NC, None, OP.mult)
    ts(A("cbm"), A("cio"), A("cr"), None, OP.add)
    for m in range(16):
        act(A("SEL", NA * R0 + m, 16 * NA, 16), A("cpb", NC * R0, NA), AF.Copy, scale=-1.0)
    ts(A("cmk"), A("cmi"), A("cj"), None, OP.is_equal)
    ts(A("hi", 3, 4), A("cpj"), 3, None, OP.bitwise_and)
    ts(A("hi", 4, 5), A("cpj"), 2, None, OP.arith_shift_right)
    ts(A("cs", 2, 3), A("hi", 3, 4), 16.0, None, OP.mult)
    tt(A("cs", 3, 4), A("cs", 2, 3), A("hi", 4, 5), OP.add)
    ts(A("PU", 0, NC), A("cbf", 0, NC), 0.25, A("cs", 3, 4), OP.mult, OP.add)
    ms(A("c4k"), 4096.0)
    ts(A("cp", 2, 3), A("cj"), float(R0), 1.0, OP.is_lt, OP.add)
    act(A("c2b"), A("cid"), AF.Copy, scale=A("cp", 2, 3))
    ms(A("c1"), 1.0)
    ts(A("cc", 0, 1), A("cj"), -1.0, 1.0, OP.mult, OP.add)
    ts(A("cc", 1, 2), A("cj"), 2.0, -4096.0, OP.is_lt, OP.mult)
    ts(A("ctm"), A("cmi"), A("cc", 0, 1), A("cc", 1, 2), OP.not_equal, OP.mult)
    tt(A("csel"), A("ctm"), A("cblk"), OP.mult)
    ts(A("cc", 2, 3), A("cj"), 2.0, 1.0 / 64, OP.is_equal, OP.mult)
    ts(A("cc", 3, 4), A("cj"), 2.0, -1.0 / 64, OP.is_lt, OP.mult)
    tt(A("cc", 4, 5), A("cc", 2, 3), A("cc", 3, 4), OP.add)
    ts(A("csq"), A("cblk"), A("cc", 4, 5), None, OP.mult)
    ts(A("cc", 5, 6), A("cj"), 2.0, 4196352.0, OP.is_ge, OP.mult)
    ts(A("cc", 6, 7), A("cc", 5, 6), 4196352.0, None, OP.add)
    copy(A("HF"), A("HS"))
    for t in range(4):
        w1, w2, k, th = (A("HF", 4 * t + i, 4 * t + i + 1) for i in range(4))
        c0, c1 = 128 * t, 128 * t + 128

        def col(i, t=t):
            return A("hs", 8 * t + i, 8 * t + i + 1)
        tt(col(4), w1, w2, OP.add)
        ts(A("WX", c0, c1), A("chl"), col(4), None, OP.mult)
        ts(A("WX", c0, c1, 16), A("cg"), w1, 0.5, OP.mult, OP.mult)
        ts(A("WX", c0 + 1, c1, 16), A("cg"), w2, 0.5, OP.mult, OP.mult)
        ts(col(5), col(4), 64.0, None, OP.mult)
        ts(A("DK"), A("cih"), k, None, OP.mult)
        b = B(4 + t, 0, 128)
        mm(b, A("cblh"), A("DK"))
        ts(A("wx"), b, w2, col(5), OP.mult, OP.add)
        ts(A("wh"), A("wx"), 5, 127, OP.arith_shift_right, OP.bitwise_and)
        ts(A("wl"), A("wx"), 31, None, OP.bitwise_and)
        tt(A("WH", c0, c1), A("wh"), A("chh"), OP.mult)
        tt(A("WL", c0, c1), A("wl"), A("chl"), OP.mult)
        sx, sa, sl = (B(4 + t, 128 + i, 129 + i) for i in range(3))
        mm(sx, A("WX", c0, c1), A("c1", 0, 1))
        mm(sl, A("WL", c0, c1), A("c1", 0, 1))
        mm(sa, A("WH", c0, c1), A("c1", 0, 1), True, False)
        mm(sa, A("WL", c0, c1), A("c1", 0, 1), False, True)
        ts(col(0), sx, -0.5, 1024.5 + 1.0 / 8192, OP.mult, OP.add)
        ts(col(1), sx, -2048.0, A("cc", 6, 7), OP.mult, OP.add)
        ts(A("hi", 0, 1), sl, -2048.0, 2048.0, OP.mult, OP.add)
        ts(A("hi", 1, 2), A("hi", 0, 1), 4095, None, OP.bitwise_and)
        ts(col(3), A("hi", 1, 2), -2048.0 - 31.0 / 64, None, OP.add)
        ts(A("hi", 2, 3), sa, -2303.0 / 4096 / 8, 6100.0 / 8, OP.mult, OP.add)
        ts(col(6), A("hi", 2, 3), 8.0, None, OP.mult)
        ts(col(2), sl, 2303.0 / 4096, col(6), OP.mult, OP.add)
        ts(A("DN", c0, c1), A("cih"), col(6), None, OP.mult)
        ts(A("th", t, t + 1), th, 4096.0, A("cr"), OP.mult, OP.add)
        ts(A("THK", 4 * t, 4 * t + NC), A("ctk"), A("th", t, t + 1), None, OP.add)
        x = float(2 * qs[t] + t // N)
        ts(A("ntx", t, t + 1), A("cj"), x, None, OP.not_equal)
        ts(A("xb", t, t + 1), A("cj"), x, 2049.0, OP.is_equal, OP.mult)
        act(A("DX", c0, c1), A("cid"), AF.Copy, scale=A("ntx", t, t + 1))
        ts(A("XM"), A("cmi"), x, None, OP.is_equal)
        tt(A("XS", c0, c1), A("XM"), A("cblk"), OP.mult)
    ts(A("P", 256, 512), A("TP"), 1.0, None, OP.add)
    for n in ("P", "PW"):
        ms(A(n, 0, 256), 0.0)
        ms(A(n, 512, 640), 0.0)
    ts(A("S"), A("SD"), 1.0, None, OP.add)
    for h in range(NS):
        ts(A("HST", 256 * h + 128, 256 * h + 192), A("cio", NA, 2 * NA), -2.0, -2.0 - 2 * NA * h, OP.mult, OP.add)
    copy(A("coh"), A("cmk", 0, 16))
    ts(A("cpen"), A("cmk"), -524288.0, 524288.0, OP.mult, OP.add)
    ms(A("ck", 0, 128), 0.0)
    ms(A("ck", 128, 384), 8192.0)
    ts(A("ctm"), A("cid"), -262144.0, None, OP.mult)
    tt(A("c8n"), A("ctm"), A("n8b"), OP.subtract)
    ms(A("csn"), 0.0)
    ms(A("csn", 256, 512), 1.0)
    for k in range(8):
        act(A("GM", NA * k, NA * k + NA), A("cone", 0, NA), AF.Copy, scale=A("cg", k, k + 1))
        act(A("GN", 128 * k, 128 * k + 128), A("cone"), AF.Copy, scale=A("cng", k, k + 1))
    for i in range(2):
        ts(A("CT", 512 * i, 512 * i + NA), A("cio", NA, 2 * NA), A("cp", i, i + 1), 0.5, OP.is_le, OP.mult)
        for k in (1, 2, 4):
            act(A("CT", 512 * i + NA * k, 512 * i + 2 * NA * k), A("CT", 512 * i, 512 * i + NA * k), AF.Copy)
    copy(A("cw0"), A("cw0f"))
    ts(A("cw1"), A("cw0f"), -128.0, None, OP.add)
    for u, (b0, b1) in enumerate(UNITS[:-1]):
        ts(A("cbb", u, u + 1), A("cp", 0, 1), -1.0, 255.0 + b1 - b0, OP.mult, OP.add)
    n = float(UNITS[-1][1] - UNITS[-1][0])
    ts(A("cbb", 2, 3), A("cp", 0, 1), -1.0, -1280.0, OP.mult, OP.add)
    ts(A("cbb", 3, 4), A("cp", 0, 1), -1.0, n - 1024.0, OP.mult, OP.add)
    ts(A("cc", 7, 8), A("cj"), 16 * (n - 1024.0) - 120.0, None, OP.add)
    copy(A("cb3h"), A("cb3"))
    ts(A("cgn"), A("cg"), -1.0, None, OP.mult)

    def shape(h):
        return "_%d" % h, NA * h, NA * h + NA, 16 * NA * h

    def middle(h, t):
        s, a0, a1, x0 = shape(h)
        if t:
            ts(A("EO", a0, a1), A("P", 256 + a0, 256 + a1), 0.0, A("ceb"), OP.max, OP.add)
        cut = [a0 + 2 * (NA * k // (2 * len(MID[h]))) for k in range(len(MID[h]) + 1)]
        for k, e in enumerate(MID[h]):
            o, x = cut[k:k + 2], (16 * cut[k], 16 * cut[k + 1])
            src = IND(A("TW"), A("EO", *o)) if t else IND(A("FI", 0, 128 * min(y1 for y0, y1 in PARTS if 8 * y1 >= a1)), A("LC", *o))
            if e == "v":
                copy(A("FA", *x), src)
            else:
                act(A("FA", *x), src, AF.Copy)
            act(A("FB", *x), A("FA", *x), AF.Abs)
            for c in range(x[0], x[1], 512):
                n = min(512, x[1] - c)
                scan(A("HI", c, c + n), A("cmh", 0, n), A("FA", c, c + n), 0.0, OP.min, OP.max)
                scan(A("LO", c, c + n), A("cml", 0, n), A("FB", c, c + n), 255.0, OP.max, OP.min)
        se = B(h, 128, 128 + NA)
        mm(se, A("cib"), A("HI", x0 + 15, x0 + 16 * NA, 16), True, False)
        mm(se, A("cib"), A("LO", x0 + 15, x0 + 16 * NA, 16), False, True)
        ts(A("C", a0, a1), se, 2047.5, None, OP.add)
        ts(A("EB", a0, a1), A("C", a0, a1), 0.5, -1024.0, OP.mult, OP.add)

    def spread(h, step):
        s, a0, a1, x0 = shape(h)
        et = B(4 + h, 128, 256, 1, NA)
        if step == 0:
            act(A("IJ", x0, x0 + 16 * NA, 16), IND(A("EB", a0, a1), A("PU", 0, NC)), AF.Copy)
            mm(et, A("EB", a0, a1), A("cib"))
            return
        act(A("ET" + s, 0, 128, 1, 0, NA), et, AF.Copy)
        for c in range(x0, x0 + NA * R0, 512):
            n = min(512, x0 + NA * R0 - c)
            scan(A("ER", c, c + n), A("ckp", 0, n), A("IJ", c, c + n), 0.0, OP.mult, OP.add)

    def restore(h):
        s, a0, a1, x0 = shape(h)
        mm(B(4 + h, 0, NA), A("ET" + s, 0, 128, 1, 0, NA), A("c2b", 0, NA, 1, 0, NA))
        act(A("E2", a0, a1), B(4 + h, 0, NA), AF.Identity, bias=2047.5)

    def hash_(h, p, t):
        s, a0, a1, x0 = shape(h)
        c0, c1 = 128 * t, 128 * t + 128
        x, hh = B(h, NA, 2 * NA), B(4 + h, 0, NA)
        c, wx, wh, wl, dn = A("C", a0, a1), A("WX", c0, c1), A("WH", c0, c1), A("WL", c0, c1), A("DN", c0, c1)
        mm(x, wx, c)
        ts(A("QH" + s), x, 1.0 / 4096, A("hs", 8 * t, 8 * t + 1), OP.mult, OP.add)
        mm(hh, wh, c)
        if p == 0:
            spread(h, 0)
        act(A("Q3" + s), hh, AF.Identity, bias=A("hs", 8 * t + 2, 8 * t + 3), scale=1.0 / 4096)
        if p == 0:
            spread(h, 1)
        mm(x, wx, c, True, False)
        mm(x, A("csel"), A("QH" + s), False, True)
        act(A("SQ" + s), x, AF.Square, bias=A("hs", 8 * t + 1, 8 * t + 2))
        mm(hh, dn, A("c4k"), True, False)
        mm(hh, wh, c, False, False)
        mm(hh, A("c4n"), A("Q3" + s), False, False)
        mm(hh, wl, c, False, False)
        mm(hh, A("csq"), A("SQ" + s), False, True)
        ts(A("HN", a0, a1), hh, A("hs", 8 * t + 3, 8 * t + 4), None, OP.add)
        k = 4 * a0 + NA * ((p + 3) % 4)
        d = A("HST", k, k + NA)
        ts(d, IND(A("HN", a0, a1), A("PU", 0, NC)), 4095, None, OP.bitwise_and)
        copy(A("OF", a0, a1), d)

    def look(h, p, t):
        s, a0, a1, x0 = shape(h)
        key, w = B(h, 0, NA), A("TW", BLK * qs[t] + 16, BLK * qs[t] + BLK)
        for i, (how, r0, r1) in enumerate(LOOK):
            x = (x0 + NA * r0, x0 + NA * r1)
            xv, ax = A("XV", *x), A("AX", *x)
            if how == "s":
                b = B(4 + h, 0, x[1] - x[0]) if i else B(h, 512 - x[1] + x[0], 512)
                act(xv, IND(w, A("OF", a0 + NC * r0, a0 + NC * r1)), AF.Copy)
                mm(b, A("ET" + s, 0, 128, 1, 0, NA), A("SEL", NA * r0, NA * r1, 1, 0, NA), True, False)
                mm(b, A("cib"), xv, False, True)
                act(ax, b, AF.Abs)
            else:
                for k in range(r0, r1, VSUB):
                    e = min(r1, k + VSUB)
                    y = (x0 + NA * k, x0 + NA * e)
                    tt(A("XV", *y), IND(w, A("OF", a0 + NC * k, a0 + NC * e)), A("ER", *y), OP.subtract)
                if how == "v":
                    act(ax, xv, AF.Abs)
                else:
                    ts(ax, xv, 0.0, None, OP.max)
            if i == 0:
                mm(key, A("cih"), A("cbm", NA * p, NA * p + NA), True, False)
            for k in range(r0, r1):
                if how == "b":
                    mm(key, A("ZC", 15 - k, 143 - k), A("XV", x0 + NA * k, x0 + NA * k + NA), False, False)
            for k in range(r0, r1):
                mm(key, A("ZB" if how == "b" else "ZA", 15 - k, 143 - k), A("AX", x0 + NA * k, x0 + NA * k + NA), False, i == len(LOOK) - 1 and k == r1 - 1)

    def winner(h, p, t):
        s, a0, a1, x0 = shape(h)
        scan(A("SC", a0, a1), A("cm0", 0, NA), B(h, 0, NA), BIG, OP.max, OP.min)
        if p < 2:
            k = A("KI" + s, 8 * p, 8 * p + NC)
            copy(k, A("SC", a0 + 15, a1, 16))
            ts(A("J" + s, 0, NC), k, 1023, None, OP.bitwise_and)
            copy(A("JU" + s, 0, NC), A("J" + s, 0, NC))
            tt(A("C", a0, a1), IND(A("XV", x0, x0 + 16 * NA), A("JU" + s, 0, NC)), A("E2", a0, a1), OP.add)
        if p == 1:
            tt(A("BA" + s, 0, NC), A("KI" + s, 0, NC), A("KI" + s, 8, 8 + NC), OP.min)
            tt(A("BB" + s, 0, NC), A("BA" + s, 0, NC), A("THK", 4 * t, 4 * t + NC), OP.min)

    def names(h, t):
        s, a0, a1, x0 = shape(h)
        bk, ps = A("BK" + s, 0, NC), B(h, 192, 192 + NA)
        tt(bk, A("SC", a0 + 15, a1, 16), A("BB" + s, 0, NC), OP.min)
        ts(A("L" + s, 0, NC), bk, 4, 255, OP.arith_shift_right, OP.bitwise_and)
        ts(A("L" + s, NC, 2 * NC), bk, 15, None, OP.bitwise_and)
        copy(A("LU" + s), A("L" + s))
        ts(A("HG", a0, a1), IND(A("HST", 4 * a0, 4 * a1), A("LU" + s, 0, NC)), -2048.0, None, OP.add)
        tt(A("PR", a0, a1), IND(A("coh"), A("LU" + s, NC, 2 * NC)), A("HG", a0, a1), OP.mult)
        mm(ps, A("DX", 128 * t, 128 * t + 128), A("P", 256 + a0, 256 + a1), True, False)
        mm(ps, A("XS", 128 * t, 128 * t + 128), A("PR", a0, a1), False, True)
        act(A("PW", 256 + a0, 256 + a1), ps, AF.Relu, bias=A("xb", t, t + 1))
        act(A("PO", a0, a1), ps, AF.Relu, bias=A("xb", t, t + 1))

    def blocks(h):
        return [(i, min(128, NA * h + NA - 128 * i)) for i in range(h // 2 + 1)]

    def compare(h):
        s, a0, a1, x0 = shape(h)
        for i, na in blocks(h):
            bank, how, tri = (4 + h, 2 + h)[i], SAME[h][i], i == h // 2
            d, ct = B(bank, 0, 512, 1, na), A("CT", 512 * (h % 2), 512 * (h % 2) + 512, 1, 0, na)
            if tri and how != "v":
                mm(d, A("cib", 0, na, 1, 0, na), ct, True, False)
            mm(d, A("PR", 128 * i, 128 * i + na), A("GM"), not tri or how == "v", False)
            for k in range(8):
                mm(B(bank, NA * k, NA * k + NA, 1, na), A("GN", 128 * k, 128 * k + na), A("PR", a0, a1), False, k == 7)
            o, z = A(("QA", "QB")[i] + s, 0, 512, 1, 0, na), A("QZ", 512 * i, 512 * i + 512, 1, 0, na)
            if how != "v":
                act(z, d, AF.Abs)
                if how == "s":
                    act(o, z, AF.Relu, bias=1.0, scale=-2.0)
                else:
                    ts(o, z, 0.0, None, OP.is_equal)
            elif tri:
                tt(o, d, ct, OP.is_equal)
            else:
                ts(o, d, 0.0, None, OP.is_equal)

    def pairs(u):
        a0, a1 = UNITS[u]
        n, kb, last = a1 - a0, a1 // NA - 1, u == len(UNITS) - 1
        low = B(kb, 0, 128, 1, n)
        for h in range(a0 // NA, a1 // NA):
            p0, todo = NA * h - a0, [(i, na, k) for i, na in blocks(h) for k in range(8)]
            mm(A("B%d" % kb, 0, 128, 1, p0, p0 + NA), A("cib", 0, NA), A("cpen"), True, False)
            for i, na, k in todo:
                mm(A("B%d" % kb, 16 * k, 16 * k + 16, 1, p0, p0 + NA), A(("QA_%d", "QB_%d")[i] % h, NA * k, NA * k + NA, 1, 0, na), A("cw%d" % i, 0, 16, 1, 0, na),
                   False, (i, na, k) == todo[-1])
        ls, lu = B(kb, 384, 384 + n // 16), A("LS_%d" % u, 0, n // 16)
        if last:
            lt = A("LH", 0, 128, 1, 0, n)
            ts(lt, low, A("cbb", 2, 3, 1, 0, n), A("cbb", 3, 4, 1, 0, n), OP.max, OP.min)
            mm(ls, A("cih"), A("cb3h", 0, n // 16), True, False)
            mm(ls, lt, A("cgn", 0, n // 16, 1, 0, n), False, True)
            ts(lu, ls, A("cc", 7, 8), None, OP.add)
        else:
            la, lt = A("LA", 0, 128, 1, 0, n), A("LT", 0, 128, 1, 0, n)
            act(la, low, AF.Abs, bias=1279.0)
            act(lt, la, AF.Relu, bias=A("cbb", u, u + 1, 1, 0, n), scale=-1.0)
            mm(ls, A("cid"), A("cb2", 0, n // 16), True, False)
            mm(ls, lt, A("cg", 0, n // 16, 1, 0, n), False, True)
            copy(lu, ls)
        w = (256 - n, 512 + n if last else 256 + a1)
        q, sn, ne, mn, cl, qn, pc, p1 = (A(x, a0, a1) for x in ("Q", "SN", "NE", "MN", "CL", "QN", "PC", "SP"))
        p = A("PO", a0, a1)
        yes, no, free, s1 = (B(kb, c, c + n) for c in (0, n, 2 * n, 384))
        act(sn, IND(A("csn", *w), lu), AF.Copy)
        act(q, IND(A("PW", *w), lu), AF.Copy)
        tt(ne, IND(A("PW", *w), lu), p, OP.not_equal)
        tt(mn, IND(A("PW", *w), lu), p, OP.min)
        tt(cl, ne, mn, OP.min)
        mm(B(kb, 0, 3 * n), A("cib"), A("ck", 128 - n, 128 + 2 * n), True, False)
        mm(yes, A("c8i"), sn, False, False)
        mm(no, A("n8i"), sn, False, False)
        mm(yes, A("n8b"), cl, False, False)
        mm(no, A("c8n"), cl, False, False)
        mm(free, A("n8i"), cl, False, True)
        tt(s1, yes, A("S", a0, a1), OP.min)
        tt(p1, no, p, OP.min)
        tt(qn, free, q, OP.min)
        tt(pc, yes, p, OP.min)
        tt(A("P", 256 + a0, 256 + a1), s1, p1, OP.max)
        tt(IND(A("P", *w), lu), qn, pc, OP.max)

    for t in range(4):
        for h in range(NS):
            lead[0] = NS - 1 - h
            middle(h, t)
            hash_(h, 0, t)
            look(h, 0, t)
            restore(h)
        for p in range(3):
            for h in range(NS):
                lead[0] = NS - 1 - h
                winner(h, p, t)
                if p < 2:
                    hash_(h, p + 1, t)
                    look(h, p + 1, t)
                else:
                    names(h, t)
                    compare(h)
                    for u, (b0, b1) in enumerate(UNITS):
                        if b1 == NA * h + NA:
                            lead[0] = 1
                            pairs(u)
    ts(A("YO"), A("P", 256, 512), 0.0, -1.0, OP.max, OP.add)

    for o in schedule(ops):
        o[3]()
    order("y", A("YO")[1], [])
    g.sync.dma_start(T.yp[:], T.YO[:]).then_inc(T.sem.dyp, 16)
    need("y", "dyp", 16)
    g.wait_ge(T.sem.loc, tot_loc[0])
    for q in ("v", "s", "t", "g"):
        need("y", qsem[q], cnt[q])
